import numpy as np, ml_dtypes
CORES = [3,11,19,27,35,43]
N = 6
import mx_ref
BF = ml_dtypes.bfloat16
def entries(a):
    return np.ascontiguousarray(a.T).reshape(-1)
def table(e):
    return np.ascontiguousarray(np.reshape(e, (-1, 16)).T).astype(np.int32)
def f(rng, *shape):
    return mx_ref.flush((rng.standard_normal(shape, dtype=np.float32) * np.exp2(rng.integers(-2, 3, shape[:-1] + (1,)))).astype(BF))
def wide(rng, *shape, cols=0):
    v = rng.standard_normal(shape, dtype=np.float32) * np.exp2(rng.integers(-12, 13, shape)).astype(np.float32)
    if cols: v *= np.repeat(np.exp2(rng.integers(-cols, cols + 1, shape[:-2] + (1, shape[-1] // 4))) * (rng.random(shape[:-2] + (1, shape[-1] // 4)) > 0.0625), 4, axis=-1).astype(np.float32)
    return mx_ref.flush(v.astype(BF))
R, P, MOST = 5, 48, 5
def lists(rng, plan, tie=False):
    v = rng.integers(0, 1001, (N, R, P))
    hold = np.arange(P).reshape(N, 8)
    for t in range(R):
        for a in range(t % 2, N - 1, 2):
            A, B, go = v[a, t], v[a + 1, t], set(int(k) for k in plan(t, a))
            for k in range(8):
                p, q = int(hold[a, k]), int(hold[a + 1, k])
                if tie:
                    A[[p, q]] = rng.integers(300, 701, 2)
                    B[[p, q]] = A[[p, q]] + rng.integers(-200, 201)
                    if k in go: A[q] += 1
                else:
                    while A[q] + B[p] == A[p] + B[q]:
                        A[[p, q]] = rng.integers(0, 1001, 2)
                        B[[p, q]] = rng.integers(0, 1001, 2)
                    if (A[q] + B[p] > A[p] + B[q]) != (k in go):
                        A[[p, q]] = A[[q, p]]
                        B[[p, q]] = B[[q, p]]
                if k in go: hold[a, k], hold[a + 1, k] = q, p
    return {"dm": np.stack([table(e.reshape(-1)) for e in v])}
def setup_inputs(rng):
    return {"x": f(rng, N, 128, 512 * R), "w": f(rng, N, 128, 1024), **lists(rng, lambda t, a: rng.permutation(8)[:rng.integers(0, MOST + 1)])}
def setup_inputs_back(rng):
    go = rng.permutation(8)[:MOST]
    return {**setup_inputs(rng), **lists(rng, lambda t, a: [] if t % 2 else go)}
def setup_inputs_carry(rng):
    d = setup_inputs(rng)
    go = rng.permutation(8)[:MOST]
    c = rng.permutation(np.repeat([-5, 5], 4))
    e = np.where(np.arange(N)[:, None] % 2 == 0, c, -c)
    s = np.exp2(e).astype(np.float32)[:, None, :, None]
    d["w"] = mx_ref.flush((d["w"].astype(np.float32).reshape(N, 128, 8, 128) * s).reshape(N, 128, 1024).astype(BF))
    return {**d, **lists(rng, lambda t, a: go)}
def setup_inputs_equal(rng):
    return {**setup_inputs(rng), **lists(rng, lambda t, a: rng.permutation(8)[:MOST], tie=True)}
def setup_inputs_turn(rng):
    go = rng.permutation(8)
    return {**setup_inputs(rng), **lists(rng, lambda t, a: go[:MOST] if t < 2 else go[8 - MOST:])}
def setup_inputs_spread(rng):
    d = setup_inputs(rng); d["x"] = wide(rng, N, 128, 512 * R, cols=6); return d
def rounds(dm):
    v = np.stack([entries(e) for e in dm]).reshape(N, R, P)
    hold = np.arange(P).reshape(N, 8)
    held, most = [], 0
    for t in range(R):
        for a in range(t % 2, N - 1, 2):
            n = 0
            for k in range(8):
                p, q = int(hold[a, k]), int(hold[a + 1, k])
                if v[a, t, q] + v[a + 1, t, p] > v[a, t, p] + v[a + 1, t, q]:
                    hold[a, k], hold[a + 1, k] = q, p
                    n += 1
            most = max(most, n)
        held.append(np.array(hold))
    return held, most
def check_inputs(d):
    for n in ("x", "w"):
        m = np.abs(d[n].astype(np.float32))
        if not np.all((m == 0) | ((m >= 2.0 ** -30) & (m <= 2.0 ** 30))): return [n]
    if d["dm"].min() < 0 or d["dm"].max() > 1000: return ["dm"]
    return ["more than MOST slots change at a pair in a round"] if rounds(d["dm"])[1] > MOST else []
def reference(x, w, dm):
    held = rounds(dm)[0]
    y = np.zeros((N, 128, 256 * R), np.float32)
    for t in range(R):
        for r in range(N):
            X = mx_ref.quantize(np.ascontiguousarray(x[r][:, 512 * t:512 * t + 512]))
            for h in range(2):
                S = np.concatenate([w[p >> 3][:, 128 * (p & 7):128 * (p & 7) + 128] for p in held[t][r, 4 * h:4 * h + 4]], axis=1)
                y[r][:, 256 * t + 128 * h:256 * t + 128 * h + 128] = mx_ref.matmul(mx_ref.quantize(S), X)
    return {"y": y}

@@ -1,0 +1,498 @@
+from concourse.bass import DstId, RemoteDMATransfer
+from concourse.mybir import dt, AluOpType, ActivationFunctionType
+
+NR = 6
+RD = 5
+PC = 32
+LANES = 5
+BLK = LANES * PC
+OWN = 16 * PC
+W1 = OWN + 2 * BLK
+W3 = W1 + 2 * BLK
+LC = 9
+SB = 12 * PC - PC
+XA = 3
+KH = 144
+
+F32 = "float32"
+SCRATCH = {
+    "wt": ("sbuf", [128, 1024], "bfloat16"),
+    "xt": ("sbuf", [128, 512 * RD], "bfloat16"),
+    "lst": ("sbuf", [128, 56], "int32"),
+    "p1c": ("sbuf", [128, OWN], "float8_e4m3fn_x4"), "p1s": ("sbuf", [128, OWN], "uint8"),
+    "p2c": ("sbuf", [128, W3], "float8_e4m3fn_x4"), "p2s": ("sbuf", [128, W3], "uint8"),
+    "snd1c": ("sbuf", [128, SB], "float8_e4m3fn_x4"), "snd1s": ("sbuf", [128, SB], "uint8"),
+    "snd3c": ("sbuf", [128, SB], "float8_e4m3fn_x4"), "snd3s": ("sbuf", [128, SB], "uint8"),
+    "xqc": ("sbuf", [128, 128 * RD], "float8_e4m3fn_x4"), "xqs": ("sbuf", [128, 128 * RD], "uint8"),
+    "yb": ("sbuf", [128, 256 * RD], F32),
+    "ps": ("psum", [128, 4096], F32),
+    "pi": ("sbuf", [128, 8], "int32"),
+    "klist": ("sbuf", [128, 8], "uint16"), "rep": ("sbuf", [128, 12], "uint16"), "m4": ("sbuf", [128, 2], "uint16"),
+    "off1": ("sbuf", [128, 24], "uint16"), "off3": ("sbuf", [128, 24], "uint16"), "ofh": ("sbuf", [128, 16], "uint16"),
+}
+for _t in range(RD):
+    SCRATCH["of%d" % _t] = ("sbuf", [128, 16], "uint16")
+    SCRATCH["st%dc" % _t] = ("sbuf", [128, 256], "float8_e4m3fn_x4")
+    SCRATCH["st%ds" % _t] = ("sbuf", [128, 256], "uint8")
+_WORK = {
+    "pf": 8, "z32": 32, "k32p": 32, "mod16": 16, "mod32": 64, "g40": 64, "mod8": 96, "g96": 96, "n96": 96, "base1": 64, "base3": 64,
+    "gd": 64, "xx": 96, "kq": 2 * KH, "reca": 64, "recb": 64, "dk0": 4, "d4": 4, "mk": 32, "m256": 4,
+    "da0": 32, "db0": 32, "da1": 32, "db1": 32, "da2": 16, "db2": 32, "db3": 32,
+    "sa0": 32, "sb0": 32, "sa1": 32, "sb1": 32, "sb2": 32, "sb3": 32,
+    "me0": 64, "me1": 64, "me2": 96, "me3": 64, "me4": 32,
+    "v0": 64, "fm1": 64, "fm2": 96, "fm3": 64, "fm4": 32, "v1": 64, "v2": 64, "v3": 64, "v4": 8,
+    "in1": 64, "ma1": 64, "eq1": 96, "pr1": 96, "sl1": 96, "in3": 64, "ma3": 64, "eq3": 96, "pr3": 96, "sl3": 96,
+    "out3": 64, "e0": 8, "f0": 8, "bv": 64, "q1": 64, "q2": 64, "q3": 64, "e2": 8, "f2": 8, "r1": 64, "ret": 64, "far": 8,
+    "bf": 64, "nr32": 64, "g1": 64, "g2": 64, "g3": 64, "w4": 64, "a1": 64, "a2": 64, "a3": 64, "e4": 8, "f4": 8,
+}
+for _n in _WORK:
+    SCRATCH[_n] = ("sbuf", [128, _WORK[_n]], F32)
+
+SEMAPHORES = ["v", "a", "mm", "gi", "sdm", "sw", "sxa", "sxb", "sy", "al", "aw", "ar1", "ar3", "loc"]
+
+ADD, SUB, MUL, MIN = AluOpType.add, AluOpType.subtract, AluOpType.mult, AluOpType.min
+LT, GT, EQ = AluOpType.is_lt, AluOpType.is_gt, AluOpType.is_equal
+AND, SHR = AluOpType.bitwise_and, AluOpType.logical_shift_right
+COPY, IDENT = ActivationFunctionType.Copy, ActivationFunctionType.Identity
+
+T_WAKE, T_CYC, T_PE = 0.1, 0.001, 0.3
+T_EXT = {"gi": 1.2, "sw": 3.4, "sxa": 5.0, "al": 6.0, "aw": 8.5, "sxb": 10.5, "ar1": 13.5, "ar3": 17.0}
+
+
+def R(name, a, b, step=1):
+    return (name, a, b, step)
+
+
+def rank_program(g, core, T, topo):
+    r = T.rank_of(core)
+    if r is None:
+        return
+    cores = T.cores
+    pair = r // 2
+    base, e = 2 * pair, r % 2
+    mate = base + 1 - e
+    mid = pair == 1
+    vec, sca = g.vector, g.scalar
+    S = T.sem
+
+    near = None if mid else (0 if pair == 0 else 1)
+    far = None if mid else 1 - near
+    nb = (0, 40) if mid else (32 * near, 32 * near + 8)
+    low = 0 if mid else 1
+    mine = low if e == 0 else 1 - low
+
+    def N(name):
+        return R(name, nb[0], nb[1])
+
+    def blk(name, b):
+        return R(name, 32 * b, 32 * b + 8)
+
+    def ap(o):
+        name, a, b, step = o
+        return T[name][:, a:b] if step == 1 else T[name][:, a:b:step]
+
+    def sender(s, q):
+        for m in (2 * s, 2 * s + 1):
+            if topo.same_plane(topo.chip(cores[m]), topo.chip(cores[q])):
+                return m
+        return 2 * s
+
+    def peers(s):
+        return [q for q in (2 * s, 2 * s + 1) if sender(pair, q) == r]
+
+    n_off = len(topo.engines(core, cores[mate]))
+
+    def addr(q):
+        rid, pid, _ = topo.addr(cores[q])
+        return rid, pid
+
+    ops = []
+
+    def note(q, call, args, reads, writes, cost, ext=(), tail=0.0, lag=0.0, kw=None):
+        ops.append((q, call, args, kw or {}, reads, writes, tuple(ext), max(64, cost) * T_CYC, tail, lag))
+        return len(ops) - 1
+
+    def val(x):
+        return ap(x) if isinstance(x, tuple) else x
+
+    def width(o):
+        return len(range(o[1], o[2], o[3]))
+
+    def ts(out, in0, s1, op0, s2=None, op1=None, ext=()):
+        args = (ap(out), ap(in0), val(s1), None, op0) if op1 is None else (ap(out), ap(in0), val(s1), val(s2), op0, op1)
+        return note("v", vec.tensor_scalar, args, [x for x in (in0, s1, s2) if isinstance(x, tuple)], [out], width(out), ext)
+
+    def af(out, in0, scale, bias):
+        return note("a", sca.activation, (ap(out), ap(in0), IDENT), [x for x in (in0, scale, bias) if isinstance(x, tuple)], [out],
+                    width(out), kw={"bias": val(bias), "scale": val(scale)})
+
+    def tt(out, a, b, op, ext=()):
+        return note("v", vec.tensor_tensor, (ap(out), ap(a), ap(b), op), [a, b], [out], 2 * width(out), ext)
+
+    def ti(out, win, off, b, op):
+        return note("v", vec.tensor_tensor, (ap(out), ap(win).indirect(ap(off)), ap(b), op), [win, off, b], [out], 50 + 1.5 * width(out))
+
+    def tr(out, a):
+        return note("v", vec.transpose, (ap(out), ap(a)), [a], [out], width(out))
+
+    def scan(out, d0, d1):
+        return note("v", vec.tensor_tensor_scan, (ap(out), ap(d0), ap(d1), 0.0, MUL, ADD), [d0, d1], [out], width(out))
+
+    def cp(out, a):
+        return note("v", vec.tensor_copy, (ap(out), ap(a)), [a], [out], width(out))
+
+    def fill(name, v, a=0, b=None):
+        o = R(name, a, _WORK[name] if b is None else b)
+        return note("v", vec.memset, (ap(o), v), [], [o], width(o))
+
+    def quant(c, s, src, ext):
+        return note("v", vec.quantize_mx, (ap(c), ap(s), ap(src)), [], [c, s], 12 + 0.22 * width(src), ext)
+
+    picks = {}
+
+    def pick(key, dst, src, wid, off, n, ext, tail=0.0, at=0):
+        o = R(off, 0, n)
+        c, d, w = 50 + 1.5 * 16 * n, R(dst + "c", at, at + 16 * n), R(src + "c", 0, wid)
+        i = note("v", vec.tensor_copy, (ap(d).bitcast(dt.uint32), ap(w).bitcast(dt.uint32).indirect(ap(o))), [w, o], [d], c, ext, tail)
+        d, w = R(dst + "s", at, at + 16 * n), R(src + "s", 0, wid)
+        j = note("a", sca.activation, (ap(d), ap(w).indirect(ap(o)), COPY), [w, o], [d], c, ext, tail)
+        picks[key] = (i, j)
+
+    fill("z32", 0.0)
+    fill("gd", 0.0)
+    fill("xx", 0.0)
+    for h in range(2):
+        fill("kq", 0.0, KH * h + 128, KH * h + KH)
+    for n in ("mk", "da1", "db1", "db3", "v2", "out3"):
+        fill(n, 0.0)
+    if not mid:
+        fill("me2", 0.0)
+        fill("ma3", 0.0)
+    fill("base1", float(OWN - PC), 0, 32)
+    fill("base1", float(OWN + BLK - PC), 32, 64)
+    fill("base3", float(W1 - PC), 0, 32)
+    fill("base3", float(W1 + (BLK if mid else 0) - PC), 32, 64)
+    gi = [("gi", 5)]
+    P = lambda c: R("pi", c, c + 1)
+    F = lambda c: R("pf", c, c + 1)
+    ts(P(1), P(0), 15, AND, ext=gi)
+    ts(P(2), P(0), 7, AND, ext=gi)
+    ts(P(3), P(0), 3, AND, ext=gi)
+    ts(P(4), P(0), 2, SHR, 3, AND, ext=gi)
+    ts(R("g40", 0, 64), R("mod32", 0, 64), 1.0, MIN, ext=gi)
+    ts(R("g96", 0, 96), R("mod8", 0, 96), 1.0, MIN, ext=gi)
+    cp(F(0), P(1))
+    cp(F(2), P(2))
+    cp(F(3), P(3))
+    ts(F(4), P(4), 18.0, MUL)
+    ts(F(1), F(0), 16.0, ADD)
+    tt(F(5), F(4), F(3), ADD)
+    ts(R("k32p", 0, 32), R("z32", 0, 32), F(2), ADD, float(PC), MUL)
+    ts(R("m4", 0, 2), R("z32", 0, 2), F(3), ADD)
+    his = 8 * PC * (1 - e)
+    ts(R("ofh", 0, 16), R("mod16", 0, 16), F(0), ADD, float(his), ADD, ext=gi)
+    ts(R("rep", 0, 3), R("z32", 0, 3), F(2), ADD)
+    ts(R("rep", 3, 9), R("z32", 0, 6), F(2), ADD, 32.0, ADD)
+    for h in range(2):
+        for o in range(2):
+            for t1 in (1, 2):
+                c = 4 * h + 2 * o + t1 - 1
+                ts(R("klist", c, c + 1), F(5), float(64 * o + LC * (t1 % 2) + 3 * t1), ADD)
+
+    my = (8 * PC * e, 8 * PC * (e + 1))
+    i_w = quant(R("p1c", *my), R("p1s", *my), R("wt", 0, 1024), [("sw", 16)])
+    quant(R("p2c", *my), R("p2s", *my), R("wt", 0, 1024), [("sw", 16)])
+    i_xa = quant(R("xqc", 0, 128 * XA), R("xqs", 0, 128 * XA), R("xt", 0, 512 * XA), [("sxa", 16)])
+    i_xb = quant(R("xqc", 128 * XA, 128 * RD), R("xqs", 128 * XA, 128 * RD), R("xt", 512 * XA, 512 * RD), [("sxb", 16)])
+
+    tt(R("gd", 0, 5 * LC), R("lst", 0, 5 * LC), R("lst", LC, 6 * LC), SUB, [("sdm", 128), ("al", (NR - 1) * n_off)])
+    tr(R("xx", 0, 64), R("gd", 0, 64))
+    for q in range(4):
+        k = KH * (q // 2) + 64 * (q % 2)
+        tr(R("kq", k, k + 64), R("xx", 8 * q, 8 * q + 64))
+    E = lambda x, a, b: R("rec" + x, a, b)
+    O = lambda x, a, b: R("rec" + x, 32 + a, 32 + b)
+    for h, x in enumerate("ab"):
+        k, l = R("kq", KH * h, KH * h + KH), R("klist", 4 * h, 4 * h + 4)
+        note("v", vec.tensor_copy, (ap(R("rec" + x, 0, 64)), ap(k).indirect(ap(l))), [k, l], [R("rec" + x, 0, 64)], 50 + 1.5 * 64)
+
+    def widen(me, b, key):
+        return ts(R(me, 32 * b, 32 * b + 32), R("z32", 0, 32), key, LT)
+
+    def widen_a(me, b, m):
+        return af(R(me, 32 * b, 32 * b + 32), R("z32", 0, 32), 1.0, m)
+
+    def M(t, c, n=1):
+        return R("mk", 8 * t + c, 8 * t + c + n)
+
+    def change(x, t, a):
+        d, s = "d%s%d" % (x, t), "s%s%d" % (x, t)
+        ti(R(s, a, 32), M(t, 0, 8), R("m4", 0, (32 - a) // 16), R(d, a, 32), MUL)
+        if t % 2 == 0:
+            tt(E(x, a, 32), E(x, a, 32), R(s, a, 32), ADD)
+            tt(O(x, a, 32), O(x, a, 32), R(s, a, 32), SUB)
+        else:
+            tt(O(x, a, 31), O(x, a, 31), R(s, a, 31), ADD)
+            tt(E(x, a + 1, 32), E(x, a + 1, 32), R(s, a, 31), SUB)
+
+    tt(R("dk0", 0, 3), R("kq", 64, 103, 19), R("kq", 0, 39, 19), SUB)
+    ts(M(0, 0, 3), R("dk0", 0, 3), 0.0, GT)
+    for x in "ab":
+        tt(R("d%s0" % x, 0, 32), O(x, 0, 32), E(x, 0, 32), SUB)
+        change(x, 0, 0)
+    af(R("m256", 0, 1), M(0, pair), 8.0 * PC, 0.0)
+    af(R("me0", 32 * low, 32 * low + 32), R("k32p", 0, 32), 1.0, R("m256", 0, 1))
+    af(R("m256", 1, 2), R("m256", 0, 1), -1.0, 8.0 * PC)
+    af(R("me0", 32 - 32 * low, 64 - 32 * low), R("k32p", 0, 32), 1.0, R("m256", 1, 2))
+    i_v0 = tr(R("v0", 0, 64), R("me0", 0, 64))
+    tt(R("da1", 0, 31), E("a", 1, 32), O("a", 0, 31), SUB)
+    for b in range(2):
+        widen("me1", b, R("da1", 5 * b, 5 * b + 1))
+    tr(R("fm1", 0, 64), R("me1", 0, 64))
+    ts(M(1, 0, 2), R("da1", 0, 6, 5), 0.0, GT)
+    change("a", 1, 16)
+    tt(R("db1", 0, 31), E("b", 1, 32), O("b", 0, 31), SUB)
+    change("b", 1, 0)
+
+    def lanes(i, fm, blocks):
+        inc, ma, eq, pr, sl, off = ["%s%d" % (n, i) for n in ("in", "ma", "eq", "pr", "sl", "off")]
+        nn = 48 * len(blocks)
+        rc = (0, 6) if len(blocks) == 2 else ((0, 3) if blocks[0] == 0 else (6, 9))
+        rep = R("rep", *rc)
+        scan(R(inc, 0, 40), R("g40", 0, 40), R(fm, 0, 40))
+        ti(R(eq, 0, nn), R(inc, 0, 40), rep, R("n96", 0, nn), EQ)
+        ti(R(pr, 0, nn), R(ma, 0, 40), rep, R(eq, 0, nn), MUL)
+        scan(R(sl, 0, nn), R("g96", 0, nn), R(pr, 0, nn))
+        cols = 12 * len(blocks)
+        ts(R(off, 0, cols, 2), R(sl, 7, nn, 8), F(0), ADD)
+        ts(R(off, 1, cols, 2), R(sl, 7, nn, 8), F(1), ADD)
+
+    near_blocks = [0, 1] if mid else [near]
+    tt(R("ma1", 0, 40), R("fm1", 0, 40), R("v0", 0, 40), MUL)
+    lanes(1, "fm1", near_blocks)
+    aw = [("aw", 2 * n_off)]
+    pick("snd1", "snd1", "p1", OWN, "off1", 22 if mid else 10, aw, 9.0)
+    pick("his", "p2", "p1", OWN, "ofh", 16, aw, at=his)
+    tt(R("da2", 0, 16), O("a", 16, 32), E("a", 16, 32), SUB)
+    ts(M(2, 0, 3), R("da2", 0, 11, 5), 0.0, GT)
+    tt(R("db2", 0, 32), O("b", 0, 32), E("b", 0, 32), SUB)
+    change("b", 2, 0)
+    for b, c in ([(0, 0), (1, 2), (2, 1)] if mid else [(near, 1), (2, pair)]):
+        widen_a("me2", b, M(2, c))
+    tr(R("fm2", 0, 96), R("me2", 0, 96))
+    tt(R("db3", 0, 31), E("b", 1, 32), O("b", 0, 31), SUB)
+    for b in range(2):
+        widen("me3", b, R("db3", 5 * b, 5 * b + 1))
+    tr(R("fm3", 0, 64), R("me3", 0, 64))
+    tt(R("e0", 0, 8), blk("v0", 1), blk("v0", 0), SUB)
+    tt(R("f0", 0, 8), R("fm2", 64, 72), R("e0", 0, 8), MUL)
+    for b in near_blocks:
+        tt(blk("out3", b), blk("v0", b), R("f0", 0, 8), SUB if b else ADD)
+    if mid:
+        tt(R("ma3", 0, 40), R("fm3", 0, 40), R("out3", 0, 40), MUL)
+    else:
+        tt(blk("ma3", far), blk("fm3", far), blk("v0", near), MUL)
+        tt(blk("ma3", near), blk("fm3", near), blk("out3", near), MUL)
+    lanes(3, "fm3", [0, 1])
+    pick("snd3", "snd3", "p1", OWN, "off3", 22, aw, 7.5)
+    ts(M(3, 0, 2), R("db3", 0, 6, 5), 0.0, GT)
+    change("b", 3, 16)
+    tt(N("bv"), N("base1"), N("v0"), SUB)
+    af(N("q1"), N("in1"), float(PC), 0.0)
+    tt(N("q2"), N("q1"), N("bv"), ADD)
+    tt(N("q3"), N("fm1"), N("q2"), MUL)
+    tt(N("v1"), N("v0"), N("q3"), ADD)
+    V1 = [blk("v1" if mid or b == near else "v0", b) for b in range(2)]
+    tt(R("e2", 0, 8), V1[1], V1[0], SUB)
+    tt(R("f2", 0, 8), R("fm2", 64, 72), R("e2", 0, 8), MUL)
+    tt(blk("v2", 0), V1[0], R("f2", 0, 8), ADD)
+    tt(blk("v2", 1), V1[1], R("f2", 0, 8), SUB)
+    tt(N("r1"), N("fm1"), N("fm2"), MUL)
+    tt(N("ret"), N("fm1"), N("r1"), SUB)
+    if mid:
+        bf = N("base3")
+    else:
+        tt(R("far", 0, 8), blk("fm1", far), blk("fm2", near), MUL)
+        af(N("bf"), R("far", 0, 8), float(BLK), float(W1 - PC))
+        bf = N("bf")
+    af(N("nr32"), N("ret"), float(-PC), float(PC))
+    tt(N("g1"), N("v0"), bf, SUB)
+    tt(N("g2"), N("ret"), N("g1"), MUL)
+    tt(N("g3"), bf, N("v2"), SUB)
+    tt(N("w4"), N("g2"), N("g3"), ADD)
+    tt(N("a1"), N("nr32"), N("in3"), MUL)
+    tt(N("a2"), N("a1"), N("w4"), ADD)
+    tt(N("a3"), N("fm3"), N("a2"), MUL)
+    tt(N("v3"), N("v2"), N("a3"), ADD)
+    kc = 16 + 5 * pair
+    tt(R("d4", 0, 1), O("b", kc, kc + 1), E("b", kc, kc + 1), SUB)
+    widen("me4", 0, R("d4", 0, 1))
+    tr(R("fm4", 0, 32), R("me4", 0, 32))
+    V3 = [blk("v3" if mid or b == near else "v2", b) for b in range(2)]
+    tt(R("e4", 0, 8), V3[1], V3[0], SUB)
+    tt(R("f4", 0, 8), R("fm4", 0, 8), R("e4", 0, 8), MUL)
+    tt(R("v4", 0, 8), V3[mine], R("f4", 0, 8), ADD if mine == 0 else SUB)
+
+    def out_of(t, h):
+        bank, c = 512 * ((2 * t + h) % 8), 256 * t + 128 * h
+        return T.yb[:, c:c + 128], T.ps[:, bank:bank + 128]
+
+    where = [blk("v0", mine), V1[mine], blk("v2", mine), V3[mine], R("v4", 0, 8)]
+    n_in1 = sum(2 * (n_off // 2 if s == 1 else n_off) for s in ([0, 2] if mid else [1]))
+    n_in3 = 2 * 2 * (n_off // 2)
+    ext = [aw, [("ar1", n_in1)], [("ar1", n_in1)], [("ar3", n_in3)], [("ar3", n_in3)]]
+    evac, later = {}, []
+    for t in range(RD):
+        later.append(ts(R("of%d" % t, 0, 16, 2), where[t], F(0), ADD))
+        later.append(ts(R("of%d" % t, 1, 16, 2), where[t], F(1), ADD))
+        pick(t, "st%d" % t, "p1" if t == 0 else "p2", (OWN, W1, W1, W3, W3)[t], "of%d" % t, 16, ext[t], 2.5 if t == 4 else 0.0)
+        for h in range(2):
+            q = "v" if t >= 3 and h == 0 else "a"
+            args = out_of(t, h) if q == "v" else out_of(t, h) + (COPY,)
+            evac[t, h] = note(q, vec.tensor_copy if q == "v" else sca.activation, args,
+                              [R("st%dc" % t, 0, 1), R("st%ds" % t, 0, 1), R("xqc", 0, 128 * t + 128)],
+                              [R("yb", 256 * t + 128 * h, 256 * t + 128 * h + 128)], 128, [("mm", 2 * t + h + 1)], 2.0 if t == 4 else 1.0, T_PE)
+
+    n_ops = len(ops)
+    queue = [o[0] for o in ops]
+    raw = [set() for _ in ops]
+    seq = [set() for _ in ops]
+    hist = {}
+    for i, o in enumerate(ops):
+        for kind, regs in (("r", o[4]), ("w", o[5])):
+            for name, a, b, step in regs:
+                cols = set(range(a, b, step))
+                for j, k2, c2 in hist.get(name, []):
+                    if j != i and (kind == "w" or k2 == "w") and not cols.isdisjoint(c2):
+                        (raw if k2 == "w" or queue[j] != queue[i] else seq)[i].add(j)
+        for kind, regs in (("r", o[4]), ("w", o[5])):
+            for name, a, b, step in regs:
+                hist.setdefault(name, []).append((i, kind, set(range(a, b, step))))
+    for a, b in (("snd1", "snd3"), ("snd3", 0), ("snd3", "his"), (0, 1), (1, 2), (2, 3), (3, 4)):
+        for n in range(2):
+            seq[picks[b][n]].add(picks[a][n])
+    for i in [i_xb] + later:
+        seq[i].add(picks["snd3"][0])
+    prio = [0.0] * n_ops
+    for i in range(n_ops - 1, -1, -1):
+        prio[i] += ops[i][7] + ops[i][8]
+        for j in raw[i]:
+            prio[j] = max(prio[j], prio[i] + T_WAKE)
+        for j in seq[i]:
+            prio[j] = max(prio[j], prio[i])
+    done, tok, now, count, order = {}, {}, {"v": 0.0, "a": 0.6}, {"v": 0, "a": 0}, []
+    while len(order) < n_ops:
+        best = None
+        for i in range(n_ops):
+            if i in tok or not all(j in tok for j in raw[i]) or not all(j in tok for j in seq[i]):
+                continue
+            at = max([now[queue[i]]] + [done[j] + T_WAKE + ops[i][9] for j in raw[i]] + [T_EXT.get(s, 0.0) for s, _ in ops[i][6]])
+            if best is None or (at, -prio[i]) < best[:2]:
+                best = (at, -prio[i], i)
+        i = best[2]
+        q = queue[i]
+        now[q] = done[i] = best[0] + ops[i][7]
+        count[q] += 1
+        tok[i] = count[q]
+        order.append(i)
+
+    for b in range(4):
+        for h, q in ((0, g.sync), (1, sca)):
+            p0 = 32 * b + 16 * h
+            q.dma_start(T.lst[p0:p0 + 16, LC * r:LC * r + LC], T.dm[:, 6 * h:6 * h + LC]).then_inc(S.sdm, 16)
+    g.sync.dma_start(T.wt[:], T.w[:]).then_inc(S.sw, 16)
+    g.sync.dma_start(T.xt[:, 0:512 * XA], T.x[:, 0:512 * XA]).then_inc(S.sxa, 16)
+    g.sync.wait_ge(S.v, tok[i_v0])
+    g.sync.dma_start(T.xt[:, 512 * XA:], T.x[:, 512 * XA:]).then_inc(S.sxb, 16)
+
+    waited = {}
+
+    def wait(q, sem, n):
+        if waited.get((q, sem), 0) < n:
+            (vec if q == "v" else sca).wait_ge(S[sem], n)
+            waited[q, sem] = n
+
+    for i in order:
+        q, call, args, kw, reads, writes, ex, cost, tail, lag = ops[i]
+        for sem, n in ex:
+            wait(q, sem, n)
+        for s in ("v", "a"):
+            wait(q, s, max([0] + [tok[j] for j in raw[i] if queue[j] == s]))
+        call(*args, **kw).then_inc(S[q], 1)
+
+    big = {"allow_small_or_imprecise_dtypes": True}
+    g.iota(T.pi[:, 0:1], [[0, 1]], 0, 1).then_inc(S.gi, 1)
+    g.iota(T.mod32[:], [[0, 2], [1, 32]], 0, 0, **big).then_inc(S.gi, 1)
+    g.iota(T.mod8[:], [[0, 12], [1, 8]], 0, 0, **big).then_inc(S.gi, 1)
+    g.iota(T.n96[:], [[0, 2], [1, 6], [0, 8]], 1, 0, **big).then_inc(S.gi, 1)
+    g.iota(T.mod16[:], [[16, 16]], 0, 0, **big).then_inc(S.gi, 1)
+    left = [0]
+    others = sorted([q for q in range(NR) if q != r], key=lambda q: (q // 2 != 1, (q - r) % NR))
+    mycol = T.lst[:, LC * r:LC * r + LC]
+    g.wait_ge(S.sdm, 128)
+    g.remote_dma_fused([RemoteDMATransfer(
+        dst_ids=[DstId(rid=addr(q)[0], pnc=addr(q)[1]) for q in others], dma_engine_mask=topo.mask(core, cores[others[0]]),
+        remote_sem=S.al, srcs=[mycol], dsts=[mycol] * len(others))], local_sem=S.loc)
+    left[0] += n_off
+    g.wait_ge(S.v, tok[i_w])
+    mys = slice(*my)
+    rid, pid = addr(mate)
+    mk = topo.mask(core, cores[mate])
+    g.remote_dma(T.p1c[:, mys].bitcast(dt.uint8), T.p1c[:, mys].bitcast(dt.uint8), S.aw, S.loc, pid, rid, mk)
+    g.remote_dma(T.p1s[:, mys], T.p1s[:, mys], S.aw, S.loc, pid, rid, mk)
+    left[0] += 2 * n_off
+
+    def send(i, jobs):
+        key = "snd%d" % i
+        g.wait_ge(S.v, tok[picks[key][0]])
+        eng = topo.engines(core, cores[jobs[0][1]])
+        per = len(eng) // len(jobs)
+        for kind in ("c", "s"):
+            if kind == "s":
+                g.wait_ge(S.a, tok[picks[key][1]])
+            trs = []
+            for n, (a, q, p) in enumerate(jobs):
+                src, dst = T[key + kind][:, a:a + BLK], T["p2" + kind][:, p:p + BLK]
+                if kind == "c":
+                    src, dst = src.bitcast(dt.uint8), dst.bitcast(dt.uint8)
+                trs.append(RemoteDMATransfer(dst_ids=[DstId(rid=addr(q)[0], pnc=addr(q)[1])], srcs=[src], dsts=[dst],
+                                             dma_engine_mask=sum(1 << x for x in eng[per * n:per * n + per]), remote_sem=S["ar%d" % i]))
+            g.remote_dma_fused(trs, local_sem=S.loc)
+            left[0] += per * len(jobs)
+
+    GA = 6 * PC
+    jobs = []
+    for n, b in enumerate(near_blocks):
+        for q in peers(pair - 1 if b == pair - 1 else pair + 1):
+            jobs.append((GA * n, q, OWN + BLK * b))
+    send(1, jobs)
+    jobs = []
+    for b in range(2):
+        if mid:
+            dst, col = 2 * b, W1
+        elif b == near:
+            dst, col = 1, W1 + (BLK if pair == 2 else 0)
+        else:
+            dst, col = 2 - pair, W1 + BLK
+        for q in peers(dst):
+            jobs.append((GA * b, q, col))
+    send(3, jobs)
+
+    for t in range(RD):
+        g.tensor.wait_ge(S.v, max(tok[picks[t][0]], tok[i_xa if t < XA else i_xb]))
+        g.tensor.wait_ge(S.a, tok[picks[t][1]])
+        for h in range(2):
+            if t == 4:
+                g.tensor.wait_ge(S.a, tok[evac[0, h]])
+            st, c = slice(128 * h, 128 * h + 128), slice(128 * t, 128 * t + 128)
+            g.tensor.matmul_mx(out_of(t, h)[1], T["st%dc" % t][:, st], T["st%ds" % t][:, st], T.xqc[:, c], T.xqs[:, c], True, True).then_inc(S.mm, 1)
+
+    for t in range(RD):
+        for h in range(2):
+            i = evac[t, h]
+            g.sync.wait_ge(S[queue[i]], tok[i])
+        g.sync.dma_start(T.y[:, 256 * t:256 * t + 256], T.yb[:, 256 * t:256 * t + 256]).then_inc(S.sy, 16)
+    g.sync.wait_ge(S.v, count["v"])
+    g.sync.wait_ge(S.a, count["a"])
+    g.sync.wait_ge(S.sy, 16 * RD)
+    g.wait_ge(S.loc, left[0])

@@ -6,105 +6,136 @@ RD = 5
 PC = 32
 LANES = 5
 BLK = LANES * PC
-OWN = 16 * PC
-W1 = OWN + 2 * BLK
-W3 = W1 + 2 * BLK
+HALF = 8 * PC
+OWN = 2 * HALF
+POOL = 2 * OWN + BLK
+AWAY = 4096.0
 LC = 9
-SB = 12 * PC - PC
 XA = 3
-KH = 144
+PAD = 8
+KC = 256
 
 F32 = "float32"
+CODES = "float8_e4m3fn_x4"
 SCRATCH = {
     "wt": ("sbuf", [128, 1024], "bfloat16"),
     "xt": ("sbuf", [128, 512 * RD], "bfloat16"),
     "lst": ("sbuf", [128, 56], "int32"),
-    "p1c": ("sbuf", [128, OWN], "float8_e4m3fn_x4"), "p1s": ("sbuf", [128, OWN], "uint8"),
-    "p2c": ("sbuf", [128, W3], "float8_e4m3fn_x4"), "p2s": ("sbuf", [128, W3], "uint8"),
-    "snd1c": ("sbuf", [128, SB], "float8_e4m3fn_x4"), "snd1s": ("sbuf", [128, SB], "uint8"),
-    "snd3c": ("sbuf", [128, SB], "float8_e4m3fn_x4"), "snd3s": ("sbuf", [128, SB], "uint8"),
-    "xqc": ("sbuf", [128, 128 * RD], "float8_e4m3fn_x4"), "xqs": ("sbuf", [128, 128 * RD], "uint8"),
     "yb": ("sbuf", [128, 256 * RD], F32),
     "ps": ("psum", [128, 4096], F32),
     "pi": ("sbuf", [128, 8], "int32"),
-    "klist": ("sbuf", [128, 8], "uint16"), "rep": ("sbuf", [128, 12], "uint16"), "m4": ("sbuf", [128, 2], "uint16"),
-    "off1": ("sbuf", [128, 24], "uint16"), "off3": ("sbuf", [128, 24], "uint16"), "ofh": ("sbuf", [128, 16], "uint16"),
+    "klist": ("sbuf", [128, 6], "uint16"), "l8": ("sbuf", [128, 4], "uint16"), "l4": ("sbuf", [128, 4], "uint16"),
+    "lkh": ("sbuf", [128, 2], "uint16"),
+    "off1": ("sbuf", [128, 10], "uint16"), "off3": ("sbuf", [128, 10], "uint16"), "ofh": ("sbuf", [128, 16], "uint16"),
 }
+for _n, _w in (("p1", OWN), ("p2", POOL), ("snd1", BLK), ("snd3", BLK), ("xq", 128 * RD), ("ha", HALF), ("hb", HALF), ("hc", BLK)):
+    SCRATCH[_n + "c"] = ("sbuf", [128, _w], CODES)
+    SCRATCH[_n + "s"] = ("sbuf", [128, _w], "uint8")
 for _t in range(RD):
     SCRATCH["of%d" % _t] = ("sbuf", [128, 16], "uint16")
-    SCRATCH["st%dc" % _t] = ("sbuf", [128, 256], "float8_e4m3fn_x4")
+    SCRATCH["st%dc" % _t] = ("sbuf", [128, 256], CODES)
     SCRATCH["st%ds" % _t] = ("sbuf", [128, 256], "uint8")
 _WORK = {
-    "pf": 8, "z32": 32, "k32p": 32, "mod16": 16, "mod32": 64, "g40": 64, "mod8": 96, "g96": 96, "n96": 96, "base1": 64, "base3": 64,
-    "gd": 64, "xx": 96, "kq": 2 * KH, "reca": 64, "recb": 64, "dk0": 4, "d4": 4, "mk": 32, "m256": 4,
-    "da0": 32, "db0": 32, "da1": 32, "db1": 32, "da2": 16, "db2": 32, "db3": 32,
-    "sa0": 32, "sb0": 32, "sa1": 32, "sb1": 32, "sb2": 32, "sb3": 32,
-    "me0": 64, "me1": 64, "me2": 96, "me3": 64, "me4": 32,
-    "v0": 64, "fm1": 64, "fm2": 96, "fm3": 64, "fm4": 32, "v1": 64, "v2": 64, "v3": 64, "v4": 8,
-    "in1": 64, "ma1": 64, "eq1": 96, "pr1": 96, "sl1": 96, "in3": 64, "ma3": 64, "eq3": 96, "pr3": 96, "sl3": 96,
-    "out3": 64, "e0": 8, "f0": 8, "bv": 64, "q1": 64, "q2": 64, "q3": 64, "e2": 8, "f2": 8, "r1": 64, "ret": 64, "far": 8,
-    "bf": 64, "nr32": 64, "g1": 64, "g2": 64, "g3": 64, "w4": 64, "a1": 64, "a2": 64, "a3": 64, "e4": 8, "f4": 8,
+    "pf": 16, "kf": 8, "z64": 64, "one8": 8, "c64": 128, "cut": 128, "n48": 48, "io64": 64, "mod16": 16,
+    "gd": 64, "xx": 96, "kq": KC + 80, "mk": 32, "lf": 2, "t4": 2,
+    "rec": 96, "rec0": 96, "rec1": 96, "rec2": 96, "rec3": 96,
+    "d0": 64, "d1": 64, "d2": 64, "d3": 64, "d4": 8, "s0": 48, "s1": 48, "s2": 48, "s3": 48,
+    "me1": 128, "me3": 128, "fm1": 128, "fm3": 128, "ln1": 128, "ln3": 128,
 }
+for _t in (1, 3):
+    _WORK.update({"wv%d" % _t: 32, "v%d" % _t: 32, "dv%d" % _t: 8, "dr%d" % _t: 48, "in%d" % _t: 16, "ge%d" % _t: 48, "sl%d" % _t: 48})
+for _t in range(RD):
+    _WORK.update({"wc%d" % _t: 64, "tc%d" % _t: 64})
 for _n in _WORK:
     SCRATCH[_n] = ("sbuf", [128, _WORK[_n]], F32)
 
-SEMAPHORES = ["v", "a", "mm", "gi", "sdm", "sw", "sxa", "sxb", "sy", "al", "aw", "ar1", "ar3", "loc"]
+_ARR = ["aw", "am", "b1n", "b1o", "b3n", "b3o", "h0", "h1"]
+SEMAPHORES = ["v", "a", "mm", "gi", "sdm", "sw", "sxa", "sxb", "sy", "al", "loc"] + [n + k for n in _ARR for k in "cs"]
 
 ADD, SUB, MUL, MIN = AluOpType.add, AluOpType.subtract, AluOpType.mult, AluOpType.min
-LT, GT, EQ = AluOpType.is_lt, AluOpType.is_gt, AluOpType.is_equal
+LT, GT, GE, NE = AluOpType.is_lt, AluOpType.is_gt, AluOpType.is_ge, AluOpType.not_equal
 AND, SHR = AluOpType.bitwise_and, AluOpType.logical_shift_right
 COPY, IDENT = ActivationFunctionType.Copy, ActivationFunctionType.Identity
 
 T_WAKE, T_CYC, T_PE = 0.1, 0.001, 0.3
-T_EXT = {"gi": 1.2, "sw": 3.4, "sxa": 5.0, "al": 6.0, "aw": 8.5, "sxb": 10.5, "ar1": 13.5, "ar3": 17.0}
+T_EXT = {"gi": 1.2, "sw": 3.4, "sxa": 5.0, "al": 6.0, "aw": 8.0, "sxb": 9.0, "am": 11.0, "b1": 10.5, "far": 12.5, "b3": 13.0}
 
 
 def R(name, a, b, step=1):
     return (name, a, b, step)
 
 
+def on_plane(T, topo, r, s):
+    return [q for q in (2 * s, 2 * s + 1) if topo.same_plane(topo.chip(T.cores[r]), topo.chip(T.cores[q]))][0]
+
+
+def helpers(T, topo, r):
+    c = T.cores[r]
+    hs = [h for h in topo.cores_of(c) if T.rank_of(h) is None and topo.may_write(h, T.cores[r ^ 1])]
+    return sorted(hs, key=lambda h: topo.die(h) != topo.die(c))
+
+
+def relays(T, topo, r):
+    hs = helpers(T, topo, r)
+    if r // 2 == 1:
+        to = lambda qs: [(q, "p2", OWN + HALF * (r % 2)) for q in qs]
+        return [(hs[0], "hb", HALF, "h0", to([1, NR - 2]), "am"), (hs[1], "hb", HALF, "h0", to([0, NR - 1]), "am")]
+    return [(hs[0], "ha", HALF, "h0", [(r ^ 1, "p1", HALF * (r % 2))], "aw"),
+            (hs[0], "hc", BLK, "h1", [(on_plane(T, topo, r, 2 - r // 2), "p2", 2 * OWN)], "b1o")]
+
+
+def side(T, name, kind, a, n):
+    v = T[name + kind][:, a:a + n]
+    return v.bitcast(dt.uint8) if kind == "c" else v
+
+
+def transfer(T, topo, src, dsts, sem, engines):
+    return RemoteDMATransfer(dst_ids=[DstId(rid=topo.addr(c)[0], pnc=topo.addr(c)[1]) for c, _ in dsts], srcs=[src],
+                             dsts=[v for _, v in dsts], dma_engine_mask=sum(1 << x for x in engines), remote_sem=sem)
+
+
+def chip_engines(T, topo, r):
+    off = topo.engines(T.cores[r], T.cores[r ^ 1])
+    return [x for x in topo.engines(T.cores[r], helpers(T, topo, r)[0]) if x not in off]
+
+
+def hand_on(g, core, T, topo):
+    left = 0
+    for r in range(NR):
+        for h, buf, n, sem, dsts, there in relays(T, topo, r):
+            if h != core:
+                continue
+            eng = topo.engines(core, T.cores[dsts[0][0]])
+            for kind in "cs":
+                g.wait_ge(T.sem[sem + kind], len(chip_engines(T, topo, r)))
+                g.remote_dma_fused([transfer(T, topo, side(T, buf, kind, 0, n), [(T.cores[q], side(T, b, kind, c, n)) for q, b, c in dsts],
+                                             T.sem[there + kind], eng)], local_sem=T.sem.loc)
+                left += len(eng)
+    if left:
+        g.wait_ge(T.sem.loc, left)
+
+
 def rank_program(g, core, T, topo):
     r = T.rank_of(core)
     if r is None:
+        hand_on(g, core, T, topo)
         return
     cores = T.cores
     pair = r // 2
     base, e = 2 * pair, r % 2
-    mate = base + 1 - e
+    mate = r ^ 1
     mid = pair == 1
+    edge = r in (0, NR - 1)
+    near = e if mid else pair // 2
     vec, sca = g.vector, g.scalar
     S = T.sem
-
-    near = None if mid else (0 if pair == 0 else 1)
-    far = None if mid else 1 - near
-    nb = (0, 40) if mid else (32 * near, 32 * near + 8)
-    low = 0 if mid else 1
-    mine = low if e == 0 else 1 - low
-
-    def N(name):
-        return R(name, nb[0], nb[1])
-
-    def blk(name, b):
-        return R(name, 32 * b, 32 * b + 8)
+    off_eng = topo.engines(core, cores[mate])
+    on_eng = chip_engines(T, topo, r)
+    n_off = len(off_eng)
 
     def ap(o):
         name, a, b, step = o
         return T[name][:, a:b] if step == 1 else T[name][:, a:b:step]
-
-    def sender(s, q):
-        for m in (2 * s, 2 * s + 1):
-            if topo.same_plane(topo.chip(cores[m]), topo.chip(cores[q])):
-                return m
-        return 2 * s
-
-    def peers(s):
-        return [q for q in (2 * s, 2 * s + 1) if sender(pair, q) == r]
-
-    n_off = len(topo.engines(core, cores[mate]))
-
-    def addr(q):
-        rid, pid, _ = topo.addr(cores[q])
-        return rid, pid
 
     ops = []
 
@@ -122,15 +153,18 @@ def rank_program(g, core, T, topo):
         args = (ap(out), ap(in0), val(s1), None, op0) if op1 is None else (ap(out), ap(in0), val(s1), val(s2), op0, op1)
         return note("v", vec.tensor_scalar, args, [x for x in (in0, s1, s2) if isinstance(x, tuple)], [out], width(out), ext)
 
-    def af(out, in0, scale, bias):
-        return note("a", sca.activation, (ap(out), ap(in0), IDENT), [x for x in (in0, scale, bias) if isinstance(x, tuple)], [out],
-                    width(out), kw={"bias": val(bias), "scale": val(scale)})
+    def af(out, in0, bias):
+        return note("a", sca.activation, (ap(out), ap(in0), IDENT), [x for x in (in0, bias) if isinstance(x, tuple)], [out],
+                    width(out), kw={"bias": val(bias)})
 
     def tt(out, a, b, op, ext=()):
         return note("v", vec.tensor_tensor, (ap(out), ap(a), ap(b), op), [a, b], [out], 2 * width(out), ext)
 
     def ti(out, win, off, b, op):
         return note("v", vec.tensor_tensor, (ap(out), ap(win).indirect(ap(off)), ap(b), op), [win, off, b], [out], 50 + 1.5 * width(out))
+
+    def ci(out, win, off):
+        return note("v", vec.tensor_copy, (ap(out), ap(win).indirect(ap(off))), [win, off], [out], 50 + 1.5 * width(out))
 
     def tr(out, a):
         return note("v", vec.transpose, (ap(out), ap(a)), [a], [out], width(out))
@@ -141,216 +175,193 @@ def rank_program(g, core, T, topo):
     def cp(out, a):
         return note("v", vec.tensor_copy, (ap(out), ap(a)), [a], [out], width(out))
 
-    def fill(name, v, a=0, b=None):
-        o = R(name, a, _WORK[name] if b is None else b)
+    def fill(name, v, a=0, b=None, step=1):
+        o = R(name, a, _WORK[name] if b is None else b, step)
         return note("v", vec.memset, (ap(o), v), [], [o], width(o))
 
-    def quant(c, s, src, ext):
-        return note("v", vec.quantize_mx, (ap(c), ap(s), ap(src)), [], [c, s], 12 + 0.22 * width(src), ext)
+    def quant(c, s, src, ext, tail=0.0):
+        return note("v", vec.quantize_mx, (ap(c), ap(s), ap(src)), [], [c, s], 12 + 0.22 * width(src), ext, tail)
 
     picks = {}
 
     def pick(key, dst, src, wid, off, n, ext, tail=0.0, at=0):
         o = R(off, 0, n)
         c, d, w = 50 + 1.5 * 16 * n, R(dst + "c", at, at + 16 * n), R(src + "c", 0, wid)
-        i = note("v", vec.tensor_copy, (ap(d).bitcast(dt.uint32), ap(w).bitcast(dt.uint32).indirect(ap(o))), [w, o], [d], c, ext, tail)
+        i = note("v", vec.tensor_copy, (ap(d).bitcast(dt.uint32), ap(w).bitcast(dt.uint32).indirect(ap(o))), [w, o], [d], c,
+                 [(s + "c", k) for s, k in ext], tail)
         d, w = R(dst + "s", at, at + 16 * n), R(src + "s", 0, wid)
-        j = note("a", sca.activation, (ap(d), ap(w).indirect(ap(o)), COPY), [w, o], [d], c, ext, tail)
+        j = note("a", sca.activation, (ap(d), ap(w).indirect(ap(o)), COPY), [w, o], [d], c, [(s + "s", k) for s, k in ext], tail)
         picks[key] = (i, j)
 
-    fill("z32", 0.0)
-    fill("gd", 0.0)
-    fill("xx", 0.0)
-    for h in range(2):
-        fill("kq", 0.0, KH * h + 128, KH * h + KH)
-    for n in ("mk", "da1", "db1", "db3", "v2", "out3"):
+    c2 = [0, 1, 2] if mid else [near, near + 1]
+    b3 = [0, 1] if mid else [near]
+    keys = [(1, 1), (3, 1)] + [(2 * c, 2) for c in c2] + [(2 * b + 1, 3) for b in b3] + [(base, 4)]
+    first = {1: 0, 2: 2, 3: 2 + len(c2), 4: len(keys) - 1, 5: len(keys)}
+    nk = len(keys) + 1
+
+    def col(t, pos, n=1):
+        c = PAD + 8 * (nk - 1) + pos
+        return R("rec%d" % t, c, c + n)
+
+    for n in ["z64", "gd", "xx", "mk", "rec0", "rec1", "rec2", "rec3", "d0", "d1", "d2", "d3"] + ([] if mid else ["in1", "in3"]):
         fill(n, 0.0)
-    if not mid:
-        fill("me2", 0.0)
-        fill("ma3", 0.0)
-    fill("base1", float(OWN - PC), 0, 32)
-    fill("base1", float(OWN + BLK - PC), 32, 64)
-    fill("base3", float(W1 - PC), 0, 32)
-    fill("base3", float(W1 + (BLK if mid else 0) - PC), 32, 64)
-    gi = [("gi", 5)]
+    fill("kq", 0.0, KC)
+    gi = [("gi", 3 if mid else 5)]
     P = lambda c: R("pi", c, c + 1)
     F = lambda c: R("pf", c, c + 1)
-    ts(P(1), P(0), 15, AND, ext=gi)
-    ts(P(2), P(0), 7, AND, ext=gi)
-    ts(P(3), P(0), 3, AND, ext=gi)
-    ts(P(4), P(0), 2, SHR, 3, AND, ext=gi)
-    ts(R("g40", 0, 64), R("mod32", 0, 64), 1.0, MIN, ext=gi)
-    ts(R("g96", 0, 96), R("mod8", 0, 96), 1.0, MIN, ext=gi)
-    cp(F(0), P(1))
-    cp(F(2), P(2))
-    cp(F(3), P(3))
-    ts(F(4), P(4), 18.0, MUL)
-    ts(F(1), F(0), 16.0, ADD)
-    tt(F(5), F(4), F(3), ADD)
-    ts(R("k32p", 0, 32), R("z32", 0, 32), F(2), ADD, float(PC), MUL)
-    ts(R("m4", 0, 2), R("z32", 0, 2), F(3), ADD)
-    his = 8 * PC * (1 - e)
-    ts(R("ofh", 0, 16), R("mod16", 0, 16), F(0), ADD, float(his), ADD, ext=gi)
-    ts(R("rep", 0, 3), R("z32", 0, 3), F(2), ADD)
-    ts(R("rep", 3, 9), R("z32", 0, 6), F(2), ADD, 32.0, ADD)
-    for h in range(2):
-        for o in range(2):
-            for t1 in (1, 2):
-                c = 4 * h + 2 * o + t1 - 1
-                ts(R("klist", c, c + 1), F(5), float(64 * o + LC * (t1 % 2) + 3 * t1), ADD)
+    for c, (sh, m) in enumerate([(0, 15), (0, 7), (0, 3), (0, 31), (3, 1), (0, 1), (1, 7)]):
+        ts(P(c + 1), P(0), sh, SHR, m, AND, ext=gi)
+    cp(R("pf", 0, 3), R("pi", 1, 4))
+    ts(F(3), F(0), 16.0, ADD)
+    ts(F(4), P(4), 8.0, LT)
+    ts(F(5), F(4), float(PC), MUL)
+    tt(F(6), F(5), F(1), MUL)
+    cp(F(7), P(7))
+    ts(F(8), P(5), -4.0, MUL, F(7), ADD)
+    ts(F(9), P(6), 64.0, MUL, F(8), ADD)
+    ts(R("l8", 0, 4), R("z64", 0, 4), F(1), ADD)
+    ts(R("l4", 0, 4), R("z64", 0, 4), F(2), ADD)
+    ts(R("lkh", 0, 1), P(6), 32.0, MUL, F(7), ADD)
+    at_key = [128 * (t // 3) + LC * a + 3 * t - 6 * (t // 3) for a, t in keys] + [KC, KC]
+    nl = (nk + 1) // 2
+    for c in range(nl):
+        ts(R("kf", c, c + 1), P(5), float(at_key[2 * c + 1] - at_key[2 * c]), MUL, float(at_key[2 * c]), ADD)
+    ts(R("klist", 0, nl), R("kf", 0, nl), F(9), ADD)
+    for q in range(NR):
+        home = HALF * (q % 2) + (0 if q // 2 == pair else OWN if q // 2 == 1 else AWAY)
+        c = KC + 64 * (q % 2) + q // 2
+        ts(R("kq", c, c + 1), F(4), float(home), MUL, F(6), ADD)
+    nc = 128 if mid else 64
+    ts(R("cut", 0, nc), R("c64", 0, nc), F(1), NE, ext=gi)
+    fill("cut", -1.0, 32, nc, 64)
+    his = HALF * (1 - e)
+    if not mid:
+        fill("one8", 1.0)
+        ts(R("ofh", 0, 16), R("mod16", 0, 16), F(0), ADD, float(his), ADD, ext=gi)
 
-    my = (8 * PC * e, 8 * PC * (e + 1))
-    i_w = quant(R("p1c", *my), R("p1s", *my), R("wt", 0, 1024), [("sw", 16)])
-    quant(R("p2c", *my), R("p2s", *my), R("wt", 0, 1024), [("sw", 16)])
+    my = (HALF * e, HALF * (e + 1))
+    src_w = "p2" if mid else "p1"
+    i_w = quant(R(src_w + "c", *my), R(src_w + "s", *my), R("wt", 0, 1024), [("sw", 16)], 20.0)
+    if not mid:
+        quant(R("p2c", *my), R("p2s", *my), R("wt", 0, 1024), [("sw", 16)])
     i_xa = quant(R("xqc", 0, 128 * XA), R("xqs", 0, 128 * XA), R("xt", 0, 512 * XA), [("sxa", 16)])
     i_xb = quant(R("xqc", 128 * XA, 128 * RD), R("xqs", 128 * XA, 128 * RD), R("xt", 512 * XA, 512 * RD), [("sxb", 16)])
 
     tt(R("gd", 0, 5 * LC), R("lst", 0, 5 * LC), R("lst", LC, 6 * LC), SUB, [("sdm", 128), ("al", (NR - 1) * n_off)])
     tr(R("xx", 0, 64), R("gd", 0, 64))
     for q in range(4):
-        k = KH * (q // 2) + 64 * (q % 2)
-        tr(R("kq", k, k + 64), R("xx", 8 * q, 8 * q + 64))
-    E = lambda x, a, b: R("rec" + x, a, b)
-    O = lambda x, a, b: R("rec" + x, 32 + a, 32 + b)
-    for h, x in enumerate("ab"):
-        k, l = R("kq", KH * h, KH * h + KH), R("klist", 4 * h, 4 * h + 4)
-        note("v", vec.tensor_copy, (ap(R("rec" + x, 0, 64)), ap(k).indirect(ap(l))), [k, l], [R("rec" + x, 0, 64)], 50 + 1.5 * 64)
+        tr(R("kq", 64 * q, 64 * q + 64), R("xx", 8 * q, 8 * q + 64))
+    ci(R("rec", PAD, PAD + 16 * nl), R("kq", 0, KC + 80), R("klist", 0, nl))
 
-    def widen(me, b, key):
-        return ts(R(me, 32 * b, 32 * b + 32), R("z32", 0, 32), key, LT)
+    def sides(name, t, k):
+        a, b = PAD + 8 * k - t % 2, PAD + 8 * nk - t % 2
+        return R(name, a, b, 2), R(name, a + 1, b, 2)
 
-    def widen_a(me, b, m):
-        return af(R(me, 32 * b, 32 * b + 32), R("z32", 0, 32), 1.0, m)
+    def before(t):
+        return "rec%d" % (t - 1) if t else "rec"
 
-    def M(t, c, n=1):
-        return R("mk", 8 * t + c, 8 * t + c + n)
+    def diff(t):
+        k = first.get(t, 0)
+        lo, up = sides(before(t), t, k)
+        tt(R("d%d" % t, 0, 4 * (nk - k)), up, lo, SUB)
 
-    def change(x, t, a):
-        d, s = "d%s%d" % (x, t), "s%s%d" % (x, t)
-        ti(R(s, a, 32), M(t, 0, 8), R("m4", 0, (32 - a) // 16), R(d, a, 32), MUL)
-        if t % 2 == 0:
-            tt(E(x, a, 32), E(x, a, 32), R(s, a, 32), ADD)
-            tt(O(x, a, 32), O(x, a, 32), R(s, a, 32), SUB)
-        else:
-            tt(O(x, a, 31), O(x, a, 31), R(s, a, 31), ADD)
-            tt(E(x, a + 1, 32), E(x, a + 1, 32), R(s, a, 31), SUB)
+    def change(t):
+        k = first[t + 1]
+        a, n = 4 * (k - first.get(t, 0)), 4 * (nk - k)
+        w = (n + 15) // 16
+        s = "s%d" % t
+        ti(R(s, 0, 16 * w), R("mk", 8 * t, 8 * t + 8), R("l4", 0, w), R("d%d" % t, a, a + 16 * w), MUL)
+        for new, old, op in zip(sides("rec%d" % t, t, k), sides(before(t), t, k), (ADD, SUB)):
+            tt(new, old, R(s, 0, n), op)
 
-    tt(R("dk0", 0, 3), R("kq", 64, 103, 19), R("kq", 0, 39, 19), SUB)
-    ts(M(0, 0, 3), R("dk0", 0, 3), 0.0, GT)
-    for x in "ab":
-        tt(R("d%s0" % x, 0, 32), O(x, 0, 32), E(x, 0, 32), SUB)
-        change(x, 0, 0)
-    af(R("m256", 0, 1), M(0, pair), 8.0 * PC, 0.0)
-    af(R("me0", 32 * low, 32 * low + 32), R("k32p", 0, 32), 1.0, R("m256", 0, 1))
-    af(R("m256", 1, 2), R("m256", 0, 1), -1.0, 8.0 * PC)
-    af(R("me0", 32 - 32 * low, 64 - 32 * low), R("k32p", 0, 32), 1.0, R("m256", 1, 2))
-    i_v0 = tr(R("v0", 0, 64), R("me0", 0, 64))
-    tt(R("da1", 0, 31), E("a", 1, 32), O("a", 0, 31), SUB)
-    for b in range(2):
-        widen("me1", b, R("da1", 5 * b, 5 * b + 1))
-    tr(R("fm1", 0, 64), R("me1", 0, 64))
-    ts(M(1, 0, 2), R("da1", 0, 6, 5), 0.0, GT)
-    change("a", 1, 16)
-    tt(R("db1", 0, 31), E("b", 1, 32), O("b", 0, 31), SUB)
-    change("b", 1, 0)
+    def widen(me, at, n, key):
+        ts(R(me, at, at + n), R("z64", 0, n), key, LT, F(5), MUL)
 
-    def lanes(i, fm, blocks):
-        inc, ma, eq, pr, sl, off = ["%s%d" % (n, i) for n in ("in", "ma", "eq", "pr", "sl", "off")]
-        nn = 48 * len(blocks)
-        rc = (0, 6) if len(blocks) == 2 else ((0, 3) if blocks[0] == 0 else (6, 9))
-        rep = R("rep", *rc)
-        scan(R(inc, 0, 40), R("g40", 0, 40), R(fm, 0, 40))
-        ti(R(eq, 0, nn), R(inc, 0, 40), rep, R("n96", 0, nn), EQ)
-        ti(R(pr, 0, nn), R(ma, 0, 40), rep, R(eq, 0, nn), MUL)
-        scan(R(sl, 0, nn), R("g96", 0, nn), R(pr, 0, nn))
-        cols = 12 * len(blocks)
-        ts(R(off, 0, cols, 2), R(sl, 7, nn, 8), F(0), ADD)
-        ts(R(off, 1, cols, 2), R(sl, 7, nn, 8), F(1), ADD)
+    def lanes_out(t, key, pos, ext, tail):
+        n = str(t)
+        af(R("wv" + n, 0, 32), R("z64", 0, 32), col(t - 1, pos))
+        tr(R("v" + n, 0, 32), R("wv" + n, 0, 32))
+        tt(R("dv" + n, 0, 8), R("v" + n, 0, 8), R("v" + n, 1, 9), SUB)
+        ci(R("dr" + n, 0, 48), R("dv" + n, 0, 8), R("l8", 0, 3))
+        widen("me" + n, 0, 32, key)
+        tr(R("fm" + n, 0, 32), R("me" + n, 0, 32))
+        scan(R("in" + n, 1, 9), R("one8", 0, 8), R("fm" + n, 0, 8))
+        ti(R("ge" + n, 0, 48), R("in" + n, 0, 16), R("l8", 0, 3), R("n48", 0, 48), GE)
+        scan(R("sl" + n, 0, 40), R("ge" + n, 0, 40), R("dr" + n, 0, 40))
+        for h in range(2):
+            ts(R("off" + n, h, 10, 2), R("sl" + n, 7, 40, 8), F(3 * h), ADD, float(OWN - 1), MIN)
+        pick("snd" + n, "snd" + n, "p1", OWN, "off" + n, 10, ext, tail)
 
-    near_blocks = [0, 1] if mid else [near]
-    tt(R("ma1", 0, 40), R("fm1", 0, 40), R("v0", 0, 40), MUL)
-    lanes(1, "fm1", near_blocks)
-    aw = [("aw", 2 * n_off)]
-    pick("snd1", "snd1", "p1", OWN, "off1", 22 if mid else 10, aw, 9.0)
-    pick("his", "p2", "p1", OWN, "ofh", 16, aw, at=his)
-    tt(R("da2", 0, 16), O("a", 16, 32), E("a", 16, 32), SUB)
-    ts(M(2, 0, 3), R("da2", 0, 11, 5), 0.0, GT)
-    tt(R("db2", 0, 32), O("b", 0, 32), E("b", 0, 32), SUB)
-    change("b", 2, 0)
-    for b, c in ([(0, 0), (1, 2), (2, 1)] if mid else [(near, 1), (2, pair)]):
-        widen_a("me2", b, M(2, c))
-    tr(R("fm2", 0, 96), R("me2", 0, 96))
-    tt(R("db3", 0, 31), E("b", 1, 32), O("b", 0, 31), SUB)
-    for b in range(2):
-        widen("me3", b, R("db3", 5 * b, 5 * b + 1))
-    tr(R("fm3", 0, 64), R("me3", 0, 64))
-    tt(R("e0", 0, 8), blk("v0", 1), blk("v0", 0), SUB)
-    tt(R("f0", 0, 8), R("fm2", 64, 72), R("e0", 0, 8), MUL)
-    for b in near_blocks:
-        tt(blk("out3", b), blk("v0", b), R("f0", 0, 8), SUB if b else ADD)
+    def lanes_in(t, at, ks):
+        n = str(t)
+        for i, key in enumerate(ks):
+            widen("me" + n, at + 64 * i, 64, key)
+        w = 64 * len(ks)
+        tr(R("fm" + n, at, at + w), R("me" + n, at, at + w))
+        scan(R("ln" + n, 0, w - 24), R("cut", 0, w - 24), R("fm" + n, at, at + w - 24))
+        return [R("ln" + n, 64 * i + 39, 64 * i + 40) for i in range(len(ks))]
+
+    aw = [("aw", n_off)]
+    D = lambda t, c: R("d%d" % t, c, c + 1)
+    tt(R("mk", 0, 3), R("kq", 64, 103, 19), R("kq", 0, 39, 19), GT)
+    diff(0)
+    change(0)
+    diff(1)
+    ts(R("mk", 9, 11), R("d1", 1, 7, 5), 0.0, GT)
+    change(1)
+
+    def arrivals(t, lane):
+        for b in range(2):
+            ts(col(t, 2 + b), lane[b], float(OWN + BLK * (t - 1 + (b != near))), ADD, col(t, 2 + b), MIN)
+
     if mid:
-        tt(R("ma3", 0, 40), R("fm3", 0, 40), R("out3", 0, 40), MUL)
+        arrivals(1, lanes_in(1, 0, [D(1, 1), D(1, 6)]))
     else:
-        tt(blk("ma3", far), blk("fm3", far), blk("v0", near), MUL)
-        tt(blk("ma3", near), blk("fm3", near), blk("out3", near), MUL)
-    lanes(3, "fm3", [0, 1])
-    pick("snd3", "snd3", "p1", OWN, "off3", 22, aw, 7.5)
-    ts(M(3, 0, 2), R("db3", 0, 6, 5), 0.0, GT)
-    change("b", 3, 16)
-    tt(N("bv"), N("base1"), N("v0"), SUB)
-    af(N("q1"), N("in1"), float(PC), 0.0)
-    tt(N("q2"), N("q1"), N("bv"), ADD)
-    tt(N("q3"), N("fm1"), N("q2"), MUL)
-    tt(N("v1"), N("v0"), N("q3"), ADD)
-    V1 = [blk("v1" if mid or b == near else "v0", b) for b in range(2)]
-    tt(R("e2", 0, 8), V1[1], V1[0], SUB)
-    tt(R("f2", 0, 8), R("fm2", 64, 72), R("e2", 0, 8), MUL)
-    tt(blk("v2", 0), V1[0], R("f2", 0, 8), ADD)
-    tt(blk("v2", 1), V1[1], R("f2", 0, 8), SUB)
-    tt(N("r1"), N("fm1"), N("fm2"), MUL)
-    tt(N("ret"), N("fm1"), N("r1"), SUB)
+        pos = 1 + 3 * near
+        lanes_out(1, D(1, 5 * near + 1), pos, aw, 9.0)
+        af(R("lf", 0, 1), lanes_in(1, 32, [D(1, 6 - 5 * near)])[0], float(2 * OWN))
+    diff(2)
+    ts(R("mk", 16 + c2[0], 17 + c2[-1]), R("d2", c2[0], c2[0] + 5 * len(c2) - 4, 5), 0.0, GT)
+    change(2)
+    diff(3)
+    ts(R("mk", 25 + b3[0], 26 + b3[-1]), R("d3", 1 + b3[0], b3[0] + 5 * len(b3) - 3, 5), 0.0, GT)
+    change(3)
     if mid:
-        bf = N("base3")
+        arrivals(3, lanes_in(3, 0, [D(3, 1), D(3, 6)]))
     else:
-        tt(R("far", 0, 8), blk("fm1", far), blk("fm2", near), MUL)
-        af(N("bf"), R("far", 0, 8), float(BLK), float(W1 - PC))
-        bf = N("bf")
-    af(N("nr32"), N("ret"), float(-PC), float(PC))
-    tt(N("g1"), N("v0"), bf, SUB)
-    tt(N("g2"), N("ret"), N("g1"), MUL)
-    tt(N("g3"), bf, N("v2"), SUB)
-    tt(N("w4"), N("g2"), N("g3"), ADD)
-    tt(N("a1"), N("nr32"), N("in3"), MUL)
-    tt(N("a2"), N("a1"), N("w4"), ADD)
-    tt(N("a3"), N("fm3"), N("a2"), MUL)
-    tt(N("v3"), N("v2"), N("a3"), ADD)
-    kc = 16 + 5 * pair
-    tt(R("d4", 0, 1), O("b", kc, kc + 1), E("b", kc, kc + 1), SUB)
-    widen("me4", 0, R("d4", 0, 1))
-    tr(R("fm4", 0, 32), R("me4", 0, 32))
-    V3 = [blk("v3" if mid or b == near else "v2", b) for b in range(2)]
-    tt(R("e4", 0, 8), V3[1], V3[0], SUB)
-    tt(R("f4", 0, 8), R("fm4", 0, 8), R("e4", 0, 8), MUL)
-    tt(R("v4", 0, 8), V3[mine], R("f4", 0, 8), ADD if mine == 0 else SUB)
+        lanes_out(3, D(3, 1 + near), pos, aw, 7.5)
+        ts(col(3, base, 2), col(3, base, 2), R("lf", 0, 1), MIN)
+        pick("his", "p2", "p1", OWN, "ofh", 16, aw, at=his)
+    diff(4)
+    ts(R("t4", 0, 1), D(4, pair), 0.0, GT, D(4, 4 + pair), MUL)
 
     def out_of(t, h):
         bank, c = 512 * ((2 * t + h) % 8), 256 * t + 128 * h
         return T.yb[:, c:c + 128], T.ps[:, bank:bank + 128]
 
-    where = [blk("v0", mine), V1[mine], blk("v2", mine), V3[mine], R("v4", 0, 8)]
-    n_in1 = sum(2 * (n_off // 2 if s == 1 else n_off) for s in ([0, 2] if mid else [1]))
-    n_in3 = 2 * 2 * (n_off // 2)
-    ext = [aw, [("ar1", n_in1)], [("ar1", n_in1)], [("ar3", n_in3)], [("ar3", n_in3)]]
+    if mid:
+        names = ["b1n", "b1o", "b3n", "b3o"]
+        src = [("p2", OWN + BLK * t, aw + [(s, n_off) for s in names[:t]]) for t in range(RD)]
+    else:
+        am = aw + [("am", 2 * n_off)]
+        src = [("p1", OWN, aw)] + [("p2", 2 * OWN, am)] * 2 + [("p2", POOL, am + [("b1o", n_off)])] * 2
+    tile = [t - 1 if edge and t % 2 else t for t in range(RD)]
     evac, later = {}, []
     for t in range(RD):
-        later.append(ts(R("of%d" % t, 0, 16, 2), where[t], F(0), ADD))
-        later.append(ts(R("of%d" % t, 1, 16, 2), where[t], F(1), ADD))
-        pick(t, "st%d" % t, "p1" if t == 0 else "p2", (OWN, W1, W1, W3, W3)[t], "of%d" % t, 16, ext[t], 2.5 if t == 4 else 0.0)
+        if tile[t] == t:
+            wc, tc = R("wc%d" % t, 0, 64), R("tc%d" % t, 0, 64)
+            if t < 4:
+                af(wc, R("io64", 0, 64), col(t, r))
+            else:
+                later.append(ts(wc, R("io64", 0, 64), R("t4", 0, 1), SUB if e else ADD, col(3, r), ADD))
+            later.append(tr(tc, wc))
+            later.append(ci(R("of%d" % t, 0, 16), tc, R("lkh", 0, 1)))
+            pick(t, "st%d" % t, src[t][0], src[t][1], "of%d" % t, 16, src[t][2], 2.5 if t == 4 else 0.0)
         for h in range(2):
             q = "v" if t >= 3 and h == 0 else "a"
             args = out_of(t, h) if q == "v" else out_of(t, h) + (COPY,)
             evac[t, h] = note(q, vec.tensor_copy if q == "v" else sca.activation, args,
-                              [R("st%dc" % t, 0, 1), R("st%ds" % t, 0, 1), R("xqc", 0, 128 * t + 128)],
+                              [R("st%dc" % tile[t], 0, 1), R("st%ds" % tile[t], 0, 1), R("xqc", 0, 128 * t + 128)],
                               [R("yb", 256 * t + 128 * h, 256 * t + 128 * h + 128)], 128, [("mm", 2 * t + h + 1)], 2.0 if t == 4 else 1.0, T_PE)
 
     n_ops = len(ops)
@@ -362,17 +373,20 @@ def rank_program(g, core, T, topo):
         for kind, regs in (("r", o[4]), ("w", o[5])):
             for name, a, b, step in regs:
                 cols = set(range(a, b, step))
-                for j, k2, c2 in hist.get(name, []):
-                    if j != i and (kind == "w" or k2 == "w") and not cols.isdisjoint(c2):
+                for j, k2, cs in hist.get(name, []):
+                    if j != i and (kind == "w" or k2 == "w") and not cols.isdisjoint(cs):
                         (raw if k2 == "w" or queue[j] != queue[i] else seq)[i].add(j)
         for kind, regs in (("r", o[4]), ("w", o[5])):
             for name, a, b, step in regs:
                 hist.setdefault(name, []).append((i, kind, set(range(a, b, step))))
-    for a, b in (("snd1", "snd3"), ("snd3", 0), ("snd3", "his"), (0, 1), (1, 2), (2, 3), (3, 4)):
+    chain = sorted(set(tile))
+    if not mid:
+        chain = ["snd1", "snd3", 0, "his"] + chain[1:]
+        for i in [i_xb] + later:
+            seq[i].add(picks["snd3"][0])
+    for a, b in zip(chain, chain[1:]):
         for n in range(2):
             seq[picks[b][n]].add(picks[a][n])
-    for i in [i_xb] + later:
-        seq[i].add(picks["snd3"][0])
     prio = [0.0] * n_ops
     for i in range(n_ops - 1, -1, -1):
         prio[i] += ops[i][7] + ops[i][8]
@@ -380,13 +394,19 @@ def rank_program(g, core, T, topo):
             prio[j] = max(prio[j], prio[i] + T_WAKE)
         for j in seq[i]:
             prio[j] = max(prio[j], prio[i])
+
+    def ext_time(s):
+        if s[:2] == "b1":
+            return T_EXT["b1" if mid else "far"]
+        return T_EXT.get(s, T_EXT.get(s[:2], 0.0))
+
     done, tok, now, count, order = {}, {}, {"v": 0.0, "a": 0.6}, {"v": 0, "a": 0}, []
     while len(order) < n_ops:
         best = None
         for i in range(n_ops):
             if i in tok or not all(j in tok for j in raw[i]) or not all(j in tok for j in seq[i]):
                 continue
-            at = max([now[queue[i]]] + [done[j] + T_WAKE + ops[i][9] for j in raw[i]] + [T_EXT.get(s, 0.0) for s, _ in ops[i][6]])
+            at = max([now[queue[i]]] + [done[j] + T_WAKE + ops[i][9] for j in raw[i]] + [ext_time(s) for s, _ in ops[i][6]])
             if best is None or (at, -prio[i]) < best[:2]:
                 best = (at, -prio[i], i)
         i = best[2]
@@ -402,7 +422,7 @@ def rank_program(g, core, T, topo):
             q.dma_start(T.lst[p0:p0 + 16, LC * r:LC * r + LC], T.dm[:, 6 * h:6 * h + LC]).then_inc(S.sdm, 16)
     g.sync.dma_start(T.wt[:], T.w[:]).then_inc(S.sw, 16)
     g.sync.dma_start(T.xt[:, 0:512 * XA], T.x[:, 0:512 * XA]).then_inc(S.sxa, 16)
-    g.sync.wait_ge(S.v, tok[i_v0])
+    g.sync.wait_ge(S.al, (NR - 1) * n_off)
     g.sync.dma_start(T.xt[:, 512 * XA:], T.x[:, 512 * XA:]).then_inc(S.sxb, 16)
 
     waited = {}
@@ -412,6 +432,7 @@ def rank_program(g, core, T, topo):
             (vec if q == "v" else sca).wait_ge(S[sem], n)
             waited[q, sem] = n
 
+    wait("a", "gi", gi[0][1])
     for i in order:
         q, call, args, kw, reads, writes, ex, cost, tail, lag = ops[i]
         for sem, n in ex:
@@ -422,70 +443,54 @@ def rank_program(g, core, T, topo):
 
     big = {"allow_small_or_imprecise_dtypes": True}
     g.iota(T.pi[:, 0:1], [[0, 1]], 0, 1).then_inc(S.gi, 1)
-    g.iota(T.mod32[:], [[0, 2], [1, 32]], 0, 0, **big).then_inc(S.gi, 1)
-    g.iota(T.mod8[:], [[0, 12], [1, 8]], 0, 0, **big).then_inc(S.gi, 1)
-    g.iota(T.n96[:], [[0, 2], [1, 6], [0, 8]], 1, 0, **big).then_inc(S.gi, 1)
-    g.iota(T.mod16[:], [[16, 16]], 0, 0, **big).then_inc(S.gi, 1)
+    g.iota(T.c64[:, 0:nc], [[0, nc // 64], [1, 64]], 0, 0, **big).then_inc(S.gi, 1)
+    g.iota(T.io64[:], [[16, 2], [0, 2], [1, 16]], 0, 0, **big).then_inc(S.gi, 1)
+    if not mid:
+        g.iota(T.n48[:], [[PC, 6], [0, 8]], PC, 0, **big).then_inc(S.gi, 1)
+        g.iota(T.mod16[:], [[16, 16]], 0, 0, **big).then_inc(S.gi, 1)
     left = [0]
-    others = sorted([q for q in range(NR) if q != r], key=lambda q: (q // 2 != 1, (q - r) % NR))
+
+    def send(trs):
+        g.remote_dma_fused(trs, local_sem=S.loc)
+        left[0] += n_off * len(trs)
+
+    others = sorted([q for q in range(NR) if q != r], key=lambda q: (q // 2 == 1, (q - r) % NR))
     mycol = T.lst[:, LC * r:LC * r + LC]
     g.wait_ge(S.sdm, 128)
-    g.remote_dma_fused([RemoteDMATransfer(
-        dst_ids=[DstId(rid=addr(q)[0], pnc=addr(q)[1]) for q in others], dma_engine_mask=topo.mask(core, cores[others[0]]),
-        remote_sem=S.al, srcs=[mycol], dsts=[mycol] * len(others))], local_sem=S.loc)
-    left[0] += n_off
+    send([transfer(T, topo, mycol, [(cores[q], mycol) for q in others], S.al, off_eng)])
+    rel = relays(T, topo, r)
     g.wait_ge(S.v, tok[i_w])
-    mys = slice(*my)
-    rid, pid = addr(mate)
-    mk = topo.mask(core, cores[mate])
-    g.remote_dma(T.p1c[:, mys].bitcast(dt.uint8), T.p1c[:, mys].bitcast(dt.uint8), S.aw, S.loc, pid, rid, mk)
-    g.remote_dma(T.p1s[:, mys], T.p1s[:, mys], S.aw, S.loc, pid, rid, mk)
-    left[0] += 2 * n_off
-
-    def send(i, jobs):
-        key = "snd%d" % i
-        g.wait_ge(S.v, tok[picks[key][0]])
-        eng = topo.engines(core, cores[jobs[0][1]])
-        per = len(eng) // len(jobs)
-        for kind in ("c", "s"):
-            if kind == "s":
-                g.wait_ge(S.a, tok[picks[key][1]])
-            trs = []
-            for n, (a, q, p) in enumerate(jobs):
-                src, dst = T[key + kind][:, a:a + BLK], T["p2" + kind][:, p:p + BLK]
-                if kind == "c":
-                    src, dst = src.bitcast(dt.uint8), dst.bitcast(dt.uint8)
-                trs.append(RemoteDMATransfer(dst_ids=[DstId(rid=addr(q)[0], pnc=addr(q)[1])], srcs=[src], dsts=[dst],
-                                             dma_engine_mask=sum(1 << x for x in eng[per * n:per * n + per]), remote_sem=S["ar%d" % i]))
-            g.remote_dma_fused(trs, local_sem=S.loc)
-            left[0] += per * len(jobs)
-
-    GA = 6 * PC
-    jobs = []
-    for n, b in enumerate(near_blocks):
-        for q in peers(pair - 1 if b == pair - 1 else pair + 1):
-            jobs.append((GA * n, q, OWN + BLK * b))
-    send(1, jobs)
-    jobs = []
-    for b in range(2):
+    for kind in "cs":
+        src_v = side(T, src_w, kind, my[0], HALF)
+        to_h = [(h, side(T, buf, kind, 0, HALF)) for h, buf, n, sem, _, _ in rel if sem == "h0"]
+        trs = [transfer(T, topo, src_v, to_h, S["h0" + kind], on_eng)]
         if mid:
-            dst, col = 2 * b, W1
-        elif b == near:
-            dst, col = 1, W1 + (BLK if pair == 2 else 0)
-        else:
-            dst, col = 2 - pair, W1 + BLK
-        for q in peers(dst):
-            jobs.append((GA * b, q, col))
-    send(3, jobs)
+            trs.append(transfer(T, topo, src_v, [(cores[mate], src_v)], S["aw" + kind], off_eng))
+        send(trs)
+    if not mid:
+        q = on_plane(T, topo, r, 1)
+        other = int(near != q % 2)
+        for t in (1, 3):
+            key = "snd%d" % t
+            for kind, sem, i in zip("cs", (S.v, S.a), picks[key]):
+                g.wait_ge(sem, tok[i])
+                src_v = side(T, key, kind, 0, BLK)
+                trs = [transfer(T, topo, src_v, [(cores[q], side(T, "p2", kind, OWN + BLK * (t - 1 + other), BLK))],
+                                S["b%d%s%s" % (t, "no"[other], kind)], off_eng)]
+                if t == 1:
+                    h, buf, n, sem, _, _ = rel[1]
+                    trs.append(transfer(T, topo, src_v, [(h, side(T, buf, kind, 0, BLK))], S[sem + kind], on_eng))
+                send(trs)
 
     for t in range(RD):
-        g.tensor.wait_ge(S.v, max(tok[picks[t][0]], tok[i_xa if t < XA else i_xb]))
-        g.tensor.wait_ge(S.a, tok[picks[t][1]])
+        g.tensor.wait_ge(S.v, max(tok[picks[tile[t]][0]], tok[i_xa if t < XA else i_xb]))
+        g.tensor.wait_ge(S.a, tok[picks[tile[t]][1]])
         for h in range(2):
             if t == 4:
                 g.tensor.wait_ge(S.a, tok[evac[0, h]])
             st, c = slice(128 * h, 128 * h + 128), slice(128 * t, 128 * t + 128)
-            g.tensor.matmul_mx(out_of(t, h)[1], T["st%dc" % t][:, st], T["st%ds" % t][:, st], T.xqc[:, c], T.xqs[:, c], True, True).then_inc(S.mm, 1)
+            g.tensor.matmul_mx(out_of(t, h)[1], T["st%dc" % tile[t]][:, st], T["st%ds" % tile[t]][:, st], T.xqc[:, c], T.xqs[:, c],
+                               True, True).then_inc(S.mm, 1)
 
     for t in range(RD):
         for h in range(2):

@@ -26,7 +26,7 @@ SCRATCH = {
     "pi": ("sbuf", [128, 8], "int32"),
     "klist": ("sbuf", [128, 6], "uint16"), "l8": ("sbuf", [128, 4], "uint16"), "l4": ("sbuf", [128, 4], "uint16"),
     "lkh": ("sbuf", [128, 2], "uint16"),
-    "off1": ("sbuf", [128, 10], "uint16"), "off3": ("sbuf", [128, 10], "uint16"), "ofh": ("sbuf", [128, 16], "uint16"),
+    "off1": ("sbuf", [128, 10], "uint16"), "off3": ("sbuf", [128, 10], "uint16"),
 }
 for _n, _w in (("p1", OWN), ("p2", POOL), ("snd1", BLK), ("snd3", BLK), ("xq", 128 * RD), ("ha", HALF), ("hb", HALF), ("hc", BLK)):
     SCRATCH[_n + "c"] = ("sbuf", [128, _w], CODES)
@@ -36,29 +36,30 @@ for _t in range(RD):
     SCRATCH["st%dc" % _t] = ("sbuf", [128, 256], CODES)
     SCRATCH["st%ds" % _t] = ("sbuf", [128, 256], "uint8")
 _WORK = {
-    "pf": 16, "kf": 8, "z64": 64, "one8": 8, "c64": 128, "cut": 128, "n48": 48, "io64": 64, "mod16": 16,
-    "gd": 64, "xx": 96, "kq": KC + 80, "mk": 32, "lf": 2, "t4": 2,
+    "pf": 16, "kf": 8, "z64": 64, "one8": 8, "c64": 128, "cut": 128, "n48": 48, "io64": 64,
+    "gd": 64, "xx": 96, "kq": KC + 80, "mk": 32, "lf": 2, "t4": 2, "nb1": 2, "nb2": 2,
     "rec": 96, "rec0": 96, "rec1": 96, "rec2": 96, "rec3": 96,
     "d0": 64, "d1": 64, "d2": 64, "d3": 64, "d4": 8, "s0": 48, "s1": 48, "s2": 48, "s3": 48,
     "me1": 128, "me3": 128, "fm1": 128, "fm3": 128, "ln1": 128, "ln3": 128,
 }
 for _t in (1, 3):
-    _WORK.update({"wv%d" % _t: 32, "v%d" % _t: 32, "dv%d" % _t: 8, "dr%d" % _t: 48, "in%d" % _t: 16, "ge%d" % _t: 48, "sl%d" % _t: 48})
+    _WORK.update({"wn%d" % _t: 32, "dv%d" % _t: 8, "dr%d" % _t: 48, "in%d" % _t: 16, "ge%d" % _t: 48, "sl%d" % _t: 48})
 for _t in range(RD):
     _WORK.update({"wc%d" % _t: 64, "tc%d" % _t: 64})
 for _n in _WORK:
     SCRATCH[_n] = ("sbuf", [128, _WORK[_n]], F32)
 
 _ARR = ["aw", "am", "b1n", "b1o", "b3n", "b3o", "h0", "h1"]
-SEMAPHORES = ["v", "a", "mm", "gi", "sdm", "sw", "sxa", "sxb", "sy", "al", "loc"] + [n + k for n in _ARR for k in "cs"]
+SEMAPHORES = ["v", "a", "mm", "gi", "sdm", "sw", "sxa", "sxb", "sy", "al", "loc", "shc", "shs"] + [n + k for n in _ARR for k in "cs"]
 
 ADD, SUB, MUL, MIN = AluOpType.add, AluOpType.subtract, AluOpType.mult, AluOpType.min
 LT, GT, GE, NE = AluOpType.is_lt, AluOpType.is_gt, AluOpType.is_ge, AluOpType.not_equal
 AND, SHR = AluOpType.bitwise_and, AluOpType.logical_shift_right
 COPY, IDENT = ActivationFunctionType.Copy, ActivationFunctionType.Identity
 
-T_WAKE, T_CYC, T_PE = 0.1, 0.001, 0.3
-T_EXT = {"gi": 1.2, "sw": 3.4, "sxa": 5.0, "al": 6.0, "aw": 8.0, "sxb": 9.0, "am": 11.0, "b1": 10.5, "far": 12.5, "b3": 13.0}
+T_WAKE, T_CYC, T_PE, T_URGENT, T_SLACK = 0.1, 0.001, 0.3, 1.0, 0.02
+T_BLOCK, T_LAST, T_SCALES = 1.0, 3.0, 0.3
+T_EXT = {"gi": 1.0, "sw": 2.3, "sxa": 4.0, "al": 6.0, "aw": 8.2, "sxb": 8.5, "am": 11.0, "sh": 10.5, "b1": 10.5, "far": 12.0, "b3": 12.5}
 
 
 def R(name, a, b, step=1):
@@ -79,7 +80,9 @@ def relays(T, topo, r):
     hs = helpers(T, topo, r)
     if r // 2 == 1:
         to = lambda qs: [(q, "p2", OWN + HALF * (r % 2)) for q in qs]
-        return [(hs[0], "hb", HALF, "h0", to([1, NR - 2]), "am"), (hs[1], "hb", HALF, "h0", to([0, NR - 1]), "am")]
+        ends = [1, NR - 2, 0, NR - 1]
+        across = [q for q in ends if on_plane(T, topo, r, q // 2) != q]
+        return [(h, "hb", HALF, "h0", to([q]), "am") for h, q in zip(hs[-2:], across)]
     return [(hs[0], "ha", HALF, "h0", [(r ^ 1, "p1", HALF * (r % 2))], "aw"),
             (hs[0], "hc", BLK, "h1", [(on_plane(T, topo, r, 2 - r // 2), "p2", 2 * OWN)], "b1o")]
 
@@ -106,7 +109,7 @@ def hand_on(g, core, T, topo):
             if h != core:
                 continue
             eng = topo.engines(core, T.cores[dsts[0][0]])
-            for kind in "cs":
+            for kind in "s" if buf == "ha" else "cs":
                 g.wait_ge(T.sem[sem + kind], len(chip_engines(T, topo, r)))
                 g.remote_dma_fused([transfer(T, topo, side(T, buf, kind, 0, n), [(T.cores[q], side(T, b, kind, c, n)) for q, b, c in dsts],
                                              T.sem[there + kind], eng)], local_sem=T.sem.loc)
@@ -206,7 +209,7 @@ def rank_program(g, core, T, topo):
     for n in ["z64", "gd", "xx", "mk", "rec0", "rec1", "rec2", "rec3", "d0", "d1", "d2", "d3"] + ([] if mid else ["in1", "in3"]):
         fill(n, 0.0)
     fill("kq", 0.0, KC)
-    gi = [("gi", 3 if mid else 5)]
+    gi = [("gi", 3 if mid else 4)]
     P = lambda c: R("pi", c, c + 1)
     F = lambda c: R("pf", c, c + 1)
     for c, (sh, m) in enumerate([(0, 15), (0, 7), (0, 3), (0, 31), (3, 1), (0, 1), (1, 7)]):
@@ -237,15 +240,15 @@ def rank_program(g, core, T, topo):
     his = HALF * (1 - e)
     if not mid:
         fill("one8", 1.0)
-        ts(R("ofh", 0, 16), R("mod16", 0, 16), F(0), ADD, float(his), ADD, ext=gi)
 
     my = (HALF * e, HALF * (e + 1))
     src_w = "p2" if mid else "p1"
     i_w = quant(R(src_w + "c", *my), R(src_w + "s", *my), R("wt", 0, 1024), [("sw", 16)], 20.0)
     if not mid:
         quant(R("p2c", *my), R("p2s", *my), R("wt", 0, 1024), [("sw", 16)])
-    i_xa = quant(R("xqc", 0, 128 * XA), R("xqs", 0, 128 * XA), R("xt", 0, 512 * XA), [("sxa", 16)])
-    i_xb = quant(R("xqc", 128 * XA, 128 * RD), R("xqs", 128 * XA, 128 * RD), R("xt", 512 * XA, 512 * RD), [("sxb", 16)])
+    i_x = [quant(R("xqc", 0, 128 * XA), R("xqs", 0, 128 * XA), R("xt", 0, 512 * XA), [("sxa", 16)])] * XA
+    for t in range(XA, RD):
+        i_x.append(quant(R("xqc", 128 * t, 128 * t + 128), R("xqs", 128 * t, 128 * t + 128), R("xt", 512 * t, 512 * t + 512), [("sxb", 16)], 3.0))
 
     tt(R("gd", 0, 5 * LC), R("lst", 0, 5 * LC), R("lst", LC, 6 * LC), SUB, [("sdm", 128), ("al", (NR - 1) * n_off)])
     tr(R("xx", 0, 64), R("gd", 0, 64))
@@ -274,17 +277,33 @@ def rank_program(g, core, T, topo):
         for new, old, op in zip(sides("rec%d" % t, t, k), sides(before(t), t, k), (ADD, SUB)):
             tt(new, old, R(s, 0, n), op)
 
+    def old(t, k, pos):
+        c = PAD + 8 * k + pos
+        return R(before(t - 1), c, c + 1)
+
+    def step(t, k, pos):
+        c = 4 * (k - first[t]) + (pos + (t - 1) % 2) // 2
+        return R("s%d" % (t - 1), c, c + 1)
+
+    def masks(t, lows):
+        k, n, nb = first[t], len(lows), "nb%d" % t
+        a = PAD + 8 * k + lows[0]
+        tt(R(nb, 0, n), R(before(t - 1), a, a + 10 * n - 9, 10), R(before(t - 1), a + 1, a + 10 * n - 8, 10), SUB)
+        for i, lo in enumerate(lows):
+            c = 8 * t + (lo + t % 2) // 2
+            ts(R("mk", c, c + 1), step(t, k + i, lo), step(t, k + i, lo + 1), ADD, R(nb, i, i + 1), GT)
+
     def widen(me, at, n, key):
         ts(R(me, at, at + n), R("z64", 0, n), key, LT, F(5), MUL)
 
-    def lanes_out(t, key, pos, ext, tail):
-        n = str(t)
-        af(R("wv" + n, 0, 32), R("z64", 0, 32), col(t - 1, pos))
-        tr(R("v" + n, 0, 32), R("wv" + n, 0, 32))
-        tt(R("dv" + n, 0, 8), R("v" + n, 0, 8), R("v" + n, 1, 9), SUB)
+    def lanes_out(t, k, pos, ext, tail):
+        n, lo = str(t), 2 * near + 1
+        ts(R("wn" + n, 0, 32), R("z64", 0, 32), old(t, k, lo), ADD, old(t, k, lo + 1), SUB)
+        ts(R("me" + n, 0, 32), R("wn" + n, 0, 32), step(t, k, lo), SUB, step(t, k, lo + 1), LT)
+        ts(R("me" + n, 32, 64), R("z64", 0, 32), old(t, nk - 1, pos), ADD, step(t, nk - 1, pos), ADD if near else SUB)
+        tr(R("fm" + n, 0, 64), R("me" + n, 0, 64))
+        tt(R("dv" + n, 0, 8), R("fm" + n, 32, 40), R("fm" + n, 33, 41), SUB)
         ci(R("dr" + n, 0, 48), R("dv" + n, 0, 8), R("l8", 0, 3))
-        widen("me" + n, 0, 32, key)
-        tr(R("fm" + n, 0, 32), R("me" + n, 0, 32))
         scan(R("in" + n, 1, 9), R("one8", 0, 8), R("fm" + n, 0, 8))
         ti(R("ge" + n, 0, 48), R("in" + n, 0, 16), R("l8", 0, 3), R("n48", 0, 48), GE)
         scan(R("sl" + n, 0, 40), R("ge" + n, 0, 40), R("dr" + n, 0, 40))
@@ -307,7 +326,7 @@ def rank_program(g, core, T, topo):
     diff(0)
     change(0)
     diff(1)
-    ts(R("mk", 9, 11), R("d1", 1, 7, 5), 0.0, GT)
+    masks(1, [1, 3])
     change(1)
 
     def arrivals(t, lane):
@@ -318,10 +337,13 @@ def rank_program(g, core, T, topo):
         arrivals(1, lanes_in(1, 0, [D(1, 1), D(1, 6)]))
     else:
         pos = 1 + 3 * near
-        lanes_out(1, D(1, 5 * near + 1), pos, aw, 9.0)
-        af(R("lf", 0, 1), lanes_in(1, 32, [D(1, 6 - 5 * near)])[0], float(2 * OWN))
+        lanes_out(1, near, pos, aw, T_BLOCK)
+        af(R("lf", 0, 1), lanes_in(1, 64, [D(1, 6 - 5 * near)])[0], float(2 * OWN))
     diff(2)
-    ts(R("mk", 16 + c2[0], 17 + c2[-1]), R("d2", c2[0], c2[0] + 5 * len(c2) - 4, 5), 0.0, GT)
+    if mid:
+        ts(R("mk", 16 + c2[0], 17 + c2[-1]), R("d2", c2[0], c2[0] + 5 * len(c2) - 4, 5), 0.0, GT)
+    else:
+        masks(2, [2 * c for c in c2])
     change(2)
     diff(3)
     ts(R("mk", 25 + b3[0], 26 + b3[-1]), R("d3", 1 + b3[0], b3[0] + 5 * len(b3) - 3, 5), 0.0, GT)
@@ -329,9 +351,8 @@ def rank_program(g, core, T, topo):
     if mid:
         arrivals(3, lanes_in(3, 0, [D(3, 1), D(3, 6)]))
     else:
-        lanes_out(3, D(3, 1 + near), pos, aw, 7.5)
+        lanes_out(3, first[3], pos, aw, T_LAST)
         ts(col(3, base, 2), col(3, base, 2), R("lf", 0, 1), MIN)
-        pick("his", "p2", "p1", OWN, "ofh", 16, aw, at=his)
     diff(4)
     ts(R("t4", 0, 1), D(4, pair), 0.0, GT, D(4, 4 + pair), MUL)
 
@@ -343,19 +364,19 @@ def rank_program(g, core, T, topo):
         names = ["b1n", "b1o", "b3n", "b3o"]
         src = [("p2", OWN + BLK * t, aw + [(s, n_off) for s in names[:t]]) for t in range(RD)]
     else:
-        am = aw + [("am", 2 * n_off)]
+        am = [("sh", 16), ("am", 2 * n_off)]
         src = [("p1", OWN, aw)] + [("p2", 2 * OWN, am)] * 2 + [("p2", POOL, am + [("b1o", n_off)])] * 2
     tile = [t - 1 if edge and t % 2 else t for t in range(RD)]
-    evac, later = {}, []
+    evac = {}
     for t in range(RD):
         if tile[t] == t:
             wc, tc = R("wc%d" % t, 0, 64), R("tc%d" % t, 0, 64)
             if t < 4:
                 af(wc, R("io64", 0, 64), col(t, r))
             else:
-                later.append(ts(wc, R("io64", 0, 64), R("t4", 0, 1), SUB if e else ADD, col(3, r), ADD))
-            later.append(tr(tc, wc))
-            later.append(ci(R("of%d" % t, 0, 16), tc, R("lkh", 0, 1)))
+                ts(wc, R("io64", 0, 64), R("t4", 0, 1), SUB if e else ADD, col(3, r), ADD)
+            tr(tc, wc)
+            ci(R("of%d" % t, 0, 16), tc, R("lkh", 0, 1))
             pick(t, "st%d" % t, src[t][0], src[t][1], "of%d" % t, 16, src[t][2], 2.5 if t == 4 else 0.0)
         for h in range(2):
             q = "v" if t >= 3 and h == 0 else "a"
@@ -381,9 +402,7 @@ def rank_program(g, core, T, topo):
                 hist.setdefault(name, []).append((i, kind, set(range(a, b, step))))
     chain = sorted(set(tile))
     if not mid:
-        chain = ["snd1", "snd3", 0, "his"] + chain[1:]
-        for i in [i_xb] + later:
-            seq[i].add(picks["snd3"][0])
+        chain = ["snd1", "snd3"] + chain
     for a, b in zip(chain, chain[1:]):
         for n in range(2):
             seq[picks[b][n]].add(picks[a][n])
@@ -396,19 +415,22 @@ def rank_program(g, core, T, topo):
             prio[j] = max(prio[j], prio[i])
 
     def ext_time(s):
-        if s[:2] == "b1":
-            return T_EXT["b1" if mid else "far"]
-        return T_EXT.get(s, T_EXT.get(s[:2], 0.0))
+        if s in T_EXT or s in ("sdm", "mm"):
+            return T_EXT.get(s, 0.0)
+        return T_EXT["far" if s[:2] == "b1" and not mid else s[:2]] + (T_SCALES if s[-1] == "s" else 0.0)
 
     done, tok, now, count, order = {}, {}, {"v": 0.0, "a": 0.6}, {"v": 0, "a": 0}, []
     while len(order) < n_ops:
-        best = None
+        ready = []
         for i in range(n_ops):
             if i in tok or not all(j in tok for j in raw[i]) or not all(j in tok for j in seq[i]):
                 continue
             at = max([now[queue[i]]] + [done[j] + T_WAKE + ops[i][9] for j in raw[i]] + [ext_time(s) for s, _ in ops[i][6]])
-            if best is None or (at, -prio[i]) < best[:2]:
-                best = (at, -prio[i], i)
+            ready.append((at, -prio[i], i))
+        best = min(ready)
+        urgent = [c for c in ready if queue[c[2]] == queue[best[2]] and c[1] < best[1] - T_URGENT and c[0] < best[0] + ops[best[2]][7] - T_SLACK]
+        if urgent:
+            best = min(urgent, key=lambda c: c[1])
         i = best[2]
         q = queue[i]
         now[q] = done[i] = best[0] + ops[i][7]
@@ -424,6 +446,12 @@ def rank_program(g, core, T, topo):
     g.sync.dma_start(T.xt[:, 0:512 * XA], T.x[:, 0:512 * XA]).then_inc(S.sxa, 16)
     g.sync.wait_ge(S.al, (NR - 1) * n_off)
     g.sync.dma_start(T.xt[:, 512 * XA:], T.x[:, 512 * XA:]).then_inc(S.sxb, 16)
+
+    if not mid:
+        g.sync.wait_ge(S.v, tok[picks["snd1"][0]])
+        for kind in "cs":
+            g.sync.wait_ge(S["aw" + kind], n_off)
+            g.sync.dma_start(side(T, "p2", kind, his, HALF), side(T, "p1", kind, his, HALF)).then_inc(S["sh" + kind], 16)
 
     waited = {}
 
@@ -446,8 +474,7 @@ def rank_program(g, core, T, topo):
     g.iota(T.c64[:, 0:nc], [[0, nc // 64], [1, 64]], 0, 0, **big).then_inc(S.gi, 1)
     g.iota(T.io64[:], [[16, 2], [0, 2], [1, 16]], 0, 0, **big).then_inc(S.gi, 1)
     if not mid:
-        g.iota(T.n48[:], [[PC, 6], [0, 8]], PC, 0, **big).then_inc(S.gi, 1)
-        g.iota(T.mod16[:], [[16, 16]], 0, 0, **big).then_inc(S.gi, 1)
+        g.iota(T.n48[:], [[1, 6], [0, 8]], 1, 0, **big).then_inc(S.gi, 1)
     left = [0]
 
     def send(trs):
@@ -463,11 +490,13 @@ def rank_program(g, core, T, topo):
     for kind in "cs":
         src_v = side(T, src_w, kind, my[0], HALF)
         to_h = [(h, side(T, buf, kind, 0, HALF)) for h, buf, n, sem, _, _ in rel if sem == "h0"]
-        trs = [transfer(T, topo, src_v, to_h, S["h0" + kind], on_eng)]
-        if mid:
-            trs.append(transfer(T, topo, src_v, [(cores[mate], src_v)], S["aw" + kind], off_eng))
-        send(trs)
-    if not mid:
+        trs = [transfer(T, topo, src_v, [(cores[mate], src_v)], S["aw" + kind], off_eng), transfer(T, topo, src_v, to_h, S["h0" + kind], on_eng)]
+        send(trs if mid else trs[:1] if kind == "c" else trs[1:])
+    if mid:
+        for q in sorted([on_plane(T, topo, r, s) for s in (0, 2)], key=lambda q: q in (0, NR - 1)):
+            for kind in "cs":
+                send([transfer(T, topo, side(T, "p2", kind, my[0], HALF), [(cores[q], side(T, "p2", kind, OWN + my[0], HALF))], S["am" + kind], off_eng)])
+    else:
         q = on_plane(T, topo, r, 1)
         other = int(near != q % 2)
         for t in (1, 3):
@@ -478,12 +507,12 @@ def rank_program(g, core, T, topo):
                 trs = [transfer(T, topo, src_v, [(cores[q], side(T, "p2", kind, OWN + BLK * (t - 1 + other), BLK))],
                                 S["b%d%s%s" % (t, "no"[other], kind)], off_eng)]
                 if t == 1:
-                    h, buf, n, sem, _, _ = rel[1]
+                    h, buf, n, sem, _, _ = rel[-1]
                     trs.append(transfer(T, topo, src_v, [(h, side(T, buf, kind, 0, BLK))], S[sem + kind], on_eng))
                 send(trs)
 
     for t in range(RD):
-        g.tensor.wait_ge(S.v, max(tok[picks[tile[t]][0]], tok[i_xa if t < XA else i_xb]))
+        g.tensor.wait_ge(S.v, max(tok[picks[tile[t]][0]], tok[i_x[t]]))
         g.tensor.wait_ge(S.a, tok[picks[tile[t]][1]])
         for h in range(2):
             if t == 4:

@@ -28,7 +28,7 @@ SCRATCH = {
     "lkh": ("sbuf", [128, 2], "uint16"),
     "off1": ("sbuf", [128, 10], "uint16"), "off3": ("sbuf", [128, 10], "uint16"),
 }
-for _n, _w in (("p1", OWN), ("p2", POOL), ("snd1", BLK), ("snd3", BLK), ("xq", 128 * RD), ("ha", HALF), ("hb", HALF), ("hc", BLK)):
+for _n, _w in (("p1", OWN), ("p2", POOL), ("snd1", BLK), ("snd3", BLK), ("xq", 128 * RD), ("ha", HALF), ("hb", HALF), ("hc", BLK), ("hd", BLK)):
     SCRATCH[_n + "c"] = ("sbuf", [128, _w], CODES)
     SCRATCH[_n + "s"] = ("sbuf", [128, _w], "uint8")
 for _t in range(RD):
@@ -37,7 +37,7 @@ for _t in range(RD):
     SCRATCH["st%ds" % _t] = ("sbuf", [128, 256], "uint8")
 _WORK = {
     "pf": 16, "kf": 8, "z64": 64, "one8": 8, "c64": 128, "cut": 128, "n48": 48, "io64": 64,
-    "gd": 64, "xx": 96, "kq": KC + 80, "mk": 32, "lf": 2, "t4": 2, "nb1": 2, "nb2": 2,
+    "gd": 64, "xx": 96, "kq": KC + 80, "mk": 32, "lf": 2, "t4": 8, "v64": 64, "nb1": 2, "nb2": 2,
     "rec": 96, "rec0": 96, "rec1": 96, "rec2": 96, "rec3": 96,
     "d0": 64, "d1": 64, "d2": 64, "d3": 64, "d4": 8, "s0": 48, "s1": 48, "s2": 48, "s3": 48,
     "me1": 128, "me3": 128, "fm1": 128, "fm3": 128, "ln1": 128, "ln3": 128,
@@ -49,7 +49,7 @@ for _t in range(RD):
 for _n in _WORK:
     SCRATCH[_n] = ("sbuf", [128, _WORK[_n]], F32)
 
-_ARR = ["aw", "am", "b1n", "b1o", "b3n", "b3o", "h0", "h1"]
+_ARR = ["aw", "am", "b1n", "b1o", "b3n", "b3o", "h0", "h1", "h2"]
 SEMAPHORES = ["v", "a", "mm", "gi", "sdm", "sw", "sxa", "sxb", "sy", "al", "loc", "shc", "shs"] + [n + k for n in _ARR for k in "cs"]
 
 ADD, SUB, MUL, MIN = AluOpType.add, AluOpType.subtract, AluOpType.mult, AluOpType.min
@@ -57,9 +57,11 @@ LT, GT, GE, NE = AluOpType.is_lt, AluOpType.is_gt, AluOpType.is_ge, AluOpType.no
 AND, SHR = AluOpType.bitwise_and, AluOpType.logical_shift_right
 COPY, IDENT = ActivationFunctionType.Copy, ActivationFunctionType.Identity
 
-T_WAKE, T_CYC, T_PE, T_URGENT, T_SLACK = 0.1, 0.001, 0.3, 1.0, 0.02
+T_CYC, T_PE, T_SLACK = 0.001, 0.3, 0.02
+T_ROLE = {"mid": (0.15, 0.2), "edge": (0.14, 0.1), "near": (0.17, 0.5)}
 T_BLOCK, T_LAST, T_SCALES = 1.0, 3.0, 0.3
-T_EXT = {"gi": 1.0, "sw": 2.3, "sxa": 4.0, "al": 6.0, "aw": 8.2, "sxb": 8.5, "am": 11.0, "sh": 10.5, "b1": 10.5, "far": 12.0, "b3": 12.5}
+T_EXT = {"gi": 1.0, "sw": 2.3, "sxa": 4.0, "al": 6.0, "aw": 8.2, "sxb": 8.5, "am": 11.0, "sh": 10.5, "far": 12.0, "b3": 13.5}
+T_MID = {"aw": 9.0, "b1": 11.5, "sxb": 11.8}
 
 
 def R(name, a, b, step=1):
@@ -83,8 +85,11 @@ def relays(T, topo, r):
         ends = [1, NR - 2, 0, NR - 1]
         across = [q for q in ends if on_plane(T, topo, r, q // 2) != q]
         return [(h, "hb", HALF, "h0", to([q]), "am") for h, q in zip(hs[-2:], across)]
-    return [(hs[0], "ha", HALF, "h0", [(r ^ 1, "p1", HALF * (r % 2))], "aw"),
-            (hs[0], "hc", BLK, "h1", [(on_plane(T, topo, r, 2 - r // 2), "p2", 2 * OWN)], "b1o")]
+    q = on_plane(T, topo, r, 1)
+    other = int(r // 4 != q % 2)
+    return [(hs[-1], "ha", HALF, "h0", [(r ^ 1, "p1", HALF * (r % 2))], "aw"),
+            (hs[-1], "hc", BLK, "h1", [(on_plane(T, topo, r, 2 - r // 2), "p2", 2 * OWN)], "b1o"),
+            (hs[-1], "hd", BLK, "h2", [(q, "p2", OWN + BLK * (2 + other))], "b3" + "no"[other])]
 
 
 def side(T, name, kind, a, n):
@@ -109,7 +114,7 @@ def hand_on(g, core, T, topo):
             if h != core:
                 continue
             eng = topo.engines(core, T.cores[dsts[0][0]])
-            for kind in "s" if buf == "ha" else "cs":
+            for kind in "s" if buf in ("ha", "hd") else "cs":
                 g.wait_ge(T.sem[sem + kind], len(chip_engines(T, topo, r)))
                 g.remote_dma_fused([transfer(T, topo, side(T, buf, kind, 0, n), [(T.cores[q], side(T, b, kind, c, n)) for q, b, c in dsts],
                                              T.sem[there + kind], eng)], local_sem=T.sem.loc)
@@ -187,8 +192,8 @@ def rank_program(g, core, T, topo):
 
     picks = {}
 
-    def pick(key, dst, src, wid, off, n, ext, tail=0.0, at=0):
-        o = R(off, 0, n)
+    def pick(key, dst, src, wid, o, ext, tail=0.0, at=0):
+        n = width(o)
         c, d, w = 50 + 1.5 * 16 * n, R(dst + "c", at, at + 16 * n), R(src + "c", 0, wid)
         i = note("v", vec.tensor_copy, (ap(d).bitcast(dt.uint32), ap(w).bitcast(dt.uint32).indirect(ap(o))), [w, o], [d], c,
                  [(s + "c", k) for s, k in ext], tail)
@@ -206,7 +211,7 @@ def rank_program(g, core, T, topo):
         c = PAD + 8 * (nk - 1) + pos
         return R("rec%d" % t, c, c + n)
 
-    for n in ["z64", "gd", "xx", "mk", "rec0", "rec1", "rec2", "rec3", "d0", "d1", "d2", "d3"] + ([] if mid else ["in1", "in3"]):
+    for n in ["z64", "gd", "xx", "mk", "rec0", "rec1", "rec2", "d0", "d1", "d2"] + (["rec3", "d3"] if mid else ["in1", "in3"]):
         fill(n, 0.0)
     fill("kq", 0.0, KC)
     gi = [("gi", 3 if mid else 4)]
@@ -218,6 +223,7 @@ def rank_program(g, core, T, topo):
     ts(F(3), F(0), 16.0, ADD)
     ts(F(4), P(4), 8.0, LT)
     ts(F(5), F(4), float(PC), MUL)
+    ts(R("v64", 0, 64), R("z64", 0, 64), F(5), ADD)
     tt(F(6), F(5), F(1), MUL)
     cp(F(7), P(7))
     ts(F(8), P(5), -4.0, MUL, F(7), ADD)
@@ -277,9 +283,9 @@ def rank_program(g, core, T, topo):
         for new, old, op in zip(sides("rec%d" % t, t, k), sides(before(t), t, k), (ADD, SUB)):
             tt(new, old, R(s, 0, n), op)
 
-    def old(t, k, pos):
+    def old(t, k, pos, name=None):
         c = PAD + 8 * k + pos
-        return R(before(t - 1), c, c + 1)
+        return R(name or before(t - 1), c, c + 1)
 
     def step(t, k, pos):
         c = 4 * (k - first[t]) + (pos + (t - 1) % 2) // 2
@@ -293,12 +299,16 @@ def rank_program(g, core, T, topo):
             c = 8 * t + (lo + t % 2) // 2
             ts(R("mk", c, c + 1), step(t, k + i, lo), step(t, k + i, lo + 1), ADD, R(nb, i, i + 1), GT)
 
-    def widen(me, at, n, key):
-        ts(R(me, at, at + n), R("z64", 0, n), key, LT, F(5), MUL)
+    def widen(me, at, n, m):
+        o, i = R(me, at, at + n), R("v64", 0, n)
+        note("a", sca.activation, (ap(o), ap(i), IDENT), [i, m], [o], n, kw={"scale": ap(m)})
 
     def lanes_out(t, k, pos, ext, tail):
         n, lo = str(t), 2 * near + 1
-        ts(R("wn" + n, 0, 32), R("z64", 0, 32), old(t, k, lo), ADD, old(t, k, lo + 1), SUB)
+        if t == 1:
+            af(R("wn" + n, 0, 32), R("z64", 0, 32), R("nb1", near, near + 1))
+        else:
+            ts(R("wn" + n, 0, 32), R("z64", 0, 32), old(t, k, lo), ADD, old(t, k, lo + 1), SUB)
         ts(R("me" + n, 0, 32), R("wn" + n, 0, 32), step(t, k, lo), SUB, step(t, k, lo + 1), LT)
         ts(R("me" + n, 32, 64), R("z64", 0, 32), old(t, nk - 1, pos), ADD, step(t, nk - 1, pos), ADD if near else SUB)
         tr(R("fm" + n, 0, 64), R("me" + n, 0, 64))
@@ -309,7 +319,7 @@ def rank_program(g, core, T, topo):
         scan(R("sl" + n, 0, 40), R("ge" + n, 0, 40), R("dr" + n, 0, 40))
         for h in range(2):
             ts(R("off" + n, h, 10, 2), R("sl" + n, 7, 40, 8), F(3 * h), ADD, float(OWN - 1), MIN)
-        pick("snd" + n, "snd" + n, "p1", OWN, "off" + n, 10, ext, tail)
+        pick("snd" + n, "snd" + n, "p1", OWN, R("off" + n, 0, 10), ext, tail)
 
     def lanes_in(t, at, ks):
         n = str(t)
@@ -321,7 +331,7 @@ def rank_program(g, core, T, topo):
         return [R("ln" + n, 64 * i + 39, 64 * i + 40) for i in range(len(ks))]
 
     aw = [("aw", n_off)]
-    D = lambda t, c: R("d%d" % t, c, c + 1)
+    M = lambda t, c: R("mk", 8 * t + c, 8 * t + c + 1)
     tt(R("mk", 0, 3), R("kq", 64, 103, 19), R("kq", 0, 39, 19), GT)
     diff(0)
     change(0)
@@ -334,27 +344,35 @@ def rank_program(g, core, T, topo):
             ts(col(t, 2 + b), lane[b], float(OWN + BLK * (t - 1 + (b != near))), ADD, col(t, 2 + b), MIN)
 
     if mid:
-        arrivals(1, lanes_in(1, 0, [D(1, 1), D(1, 6)]))
+        arrivals(1, lanes_in(1, 0, [M(1, 1), M(1, 2)]))
     else:
         pos = 1 + 3 * near
         lanes_out(1, near, pos, aw, T_BLOCK)
-        af(R("lf", 0, 1), lanes_in(1, 64, [D(1, 6 - 5 * near)])[0], float(2 * OWN))
+        af(R("lf", 0, 1), lanes_in(1, 64, [M(1, 2 - near)])[0], float(2 * OWN))
     diff(2)
     if mid:
         ts(R("mk", 16 + c2[0], 17 + c2[-1]), R("d2", c2[0], c2[0] + 5 * len(c2) - 4, 5), 0.0, GT)
     else:
         masks(2, [2 * c for c in c2])
     change(2)
-    diff(3)
-    ts(R("mk", 25 + b3[0], 26 + b3[-1]), R("d3", 1 + b3[0], b3[0] + 5 * len(b3) - 3, 5), 0.0, GT)
-    change(3)
+    U = lambda c: R("t4", c, c + 1)
     if mid:
-        arrivals(3, lanes_in(3, 0, [D(3, 1), D(3, 6)]))
+        diff(3)
+        ts(R("mk", 25, 27), R("d3", 1, 7, 5), 0.0, GT)
+        change(3)
+        arrivals(3, lanes_in(3, 0, [M(3, 1), M(3, 2)]))
+        diff(4)
+        ts(U(0), R("d4", pair, pair + 1), 0.0, GT, R("d4", 4 + pair, 5 + pair), MUL)
+        held, back = col(3, r), e
     else:
         lanes_out(3, first[3], pos, aw, T_LAST)
-        ts(col(3, base, 2), col(3, base, 2), R("lf", 0, 1), MIN)
-    diff(4)
-    ts(R("t4", 0, 1), D(4, pair), 0.0, GT, D(4, 4 + pair), MUL)
+        out, oth, k4 = 2 + near, (NR - 1) * near, first[4]
+        for c, k in ((1, k4), (2, nk - 1)):
+            ts(U(c), old(3, k, out, "rec2"), old(3, k, pos, "rec2"), SUB, R("me3", 0, 1), MUL)
+        ts(U(3), U(2), col(2, pos), ADD, R("lf", 0, 1), MIN)
+        ts(U(4), U(1), old(3, k4, pos, "rec2"), ADD, old(3, k4, oth, "rec2"), LT if near else GT)
+        ts(U(0), U(3), col(2, oth), SUB, U(4), MUL)
+        held, back = (col(2, oth), 0) if edge else (U(3), 1)
 
     def out_of(t, h):
         bank, c = 512 * ((2 * t + h) % 8), 256 * t + 128 * h
@@ -372,17 +390,22 @@ def rank_program(g, core, T, topo):
         if tile[t] == t:
             wc, tc = R("wc%d" % t, 0, 64), R("tc%d" % t, 0, 64)
             if t < 4:
-                af(wc, R("io64", 0, 64), col(t, r))
+                af(wc, R("io64", 0, 64), col(t, r) if t < 3 else held)
             else:
-                ts(wc, R("io64", 0, 64), R("t4", 0, 1), SUB if e else ADD, col(3, r), ADD)
+                ts(wc, R("io64", 0, 64), U(0), SUB if back else ADD, held, ADD)
             tr(tc, wc)
             ci(R("of%d" % t, 0, 16), tc, R("lkh", 0, 1))
-            pick(t, "st%d" % t, src[t][0], src[t][1], "of%d" % t, 16, src[t][2], 2.5 if t == 4 else 0.0)
+            if t < RD - 1:
+                pick((t, 0), "st%d" % t, src[t][0], src[t][1], R("of%d" % t, 0, 16), src[t][2])
+                picks[t, 1] = picks[t, 0]
+            else:
+                for h in range(2):
+                    pick((t, h), "st%d" % t, src[t][0], src[t][1], R("of%d" % t, 8 * h, 8 * h + 8), src[t][2], 2.5 * h, 128 * h)
         for h in range(2):
             q = "v" if t >= 3 and h == 0 else "a"
             args = out_of(t, h) if q == "v" else out_of(t, h) + (COPY,)
             evac[t, h] = note(q, vec.tensor_copy if q == "v" else sca.activation, args,
-                              [R("st%dc" % tile[t], 0, 1), R("st%ds" % tile[t], 0, 1), R("xqc", 0, 128 * t + 128)],
+                              [R("st%d%s" % (tile[t], k), 128 * h, 128 * h + 1) for k in "cs"] + [R("xqc", 0, 128 * t + 128)],
                               [R("yb", 256 * t + 128 * h, 256 * t + 128 * h + 128)], 128, [("mm", 2 * t + h + 1)], 2.0 if t == 4 else 1.0, T_PE)
 
     n_ops = len(ops)
@@ -400,12 +423,13 @@ def rank_program(g, core, T, topo):
         for kind, regs in (("r", o[4]), ("w", o[5])):
             for name, a, b, step in regs:
                 hist.setdefault(name, []).append((i, kind, set(range(a, b, step))))
-    chain = sorted(set(tile))
+    chain = [(t, 0) for t in sorted(set(tile))] + [(RD - 1, 1)]
     if not mid:
         chain = ["snd1", "snd3"] + chain
     for a, b in zip(chain, chain[1:]):
         for n in range(2):
             seq[picks[b][n]].add(picks[a][n])
+    T_WAKE, T_URGENT = T_ROLE["mid" if mid else "edge" if edge else "near"]
     prio = [0.0] * n_ops
     for i in range(n_ops - 1, -1, -1):
         prio[i] += ops[i][7] + ops[i][8]
@@ -415,9 +439,13 @@ def rank_program(g, core, T, topo):
             prio[j] = max(prio[j], prio[i])
 
     def ext_time(s):
+        if mid and s[:3] in T_MID:
+            return T_MID[s[:3]]
+        if mid and s[:2] in T_MID:
+            return T_MID[s[:2]]
         if s in T_EXT or s in ("sdm", "mm"):
             return T_EXT.get(s, 0.0)
-        return T_EXT["far" if s[:2] == "b1" and not mid else s[:2]] + (T_SCALES if s[-1] == "s" else 0.0)
+        return T_EXT["far" if s[:2] == "b1" else s[:2]] + (T_SCALES if s[-1] == "s" else 0.0)
 
     done, tok, now, count, order = {}, {}, {"v": 0.0, "a": 0.6}, {"v": 0, "a": 0}, []
     while len(order) < n_ops:
@@ -448,7 +476,6 @@ def rank_program(g, core, T, topo):
     g.sync.dma_start(T.xt[:, 512 * XA:], T.x[:, 512 * XA:]).then_inc(S.sxb, 16)
 
     if not mid:
-        g.sync.wait_ge(S.v, tok[picks["snd1"][0]])
         for kind in "cs":
             g.sync.wait_ge(S["aw" + kind], n_off)
             g.sync.dma_start(side(T, "p2", kind, his, HALF), side(T, "p1", kind, his, HALF)).then_inc(S["sh" + kind], 16)
@@ -506,27 +533,26 @@ def rank_program(g, core, T, topo):
                 src_v = side(T, key, kind, 0, BLK)
                 trs = [transfer(T, topo, src_v, [(cores[q], side(T, "p2", kind, OWN + BLK * (t - 1 + other), BLK))],
                                 S["b%d%s%s" % (t, "no"[other], kind)], off_eng)]
-                if t == 1:
-                    h, buf, n, sem, _, _ = rel[-1]
-                    trs.append(transfer(T, topo, src_v, [(h, side(T, buf, kind, 0, BLK))], S[sem + kind], on_eng))
-                send(trs)
+                h, buf, n, sem, _, _ = rel[(t + 1) // 2]
+                trs.append(transfer(T, topo, src_v, [(h, side(T, buf, kind, 0, BLK))], S[sem + kind], on_eng))
+                send(trs if t == 1 else trs[:1] if kind == "c" else trs[1:])
 
     for t in range(RD):
-        g.tensor.wait_ge(S.v, max(tok[picks[tile[t]][0]], tok[i_x[t]]))
-        g.tensor.wait_ge(S.a, tok[picks[tile[t]][1]])
         for h in range(2):
-            if t == 4:
-                g.tensor.wait_ge(S.a, tok[evac[0, h]])
+            if h == 0 or t == RD - 1:
+                g.tensor.wait_ge(S.v, max(tok[picks[tile[t], h][0]], tok[i_x[t]]))
+                g.tensor.wait_ge(S.a, max(tok[picks[tile[t], h][1]], tok[evac[0, h]] if t == RD - 1 else 0))
             st, c = slice(128 * h, 128 * h + 128), slice(128 * t, 128 * t + 128)
             g.tensor.matmul_mx(out_of(t, h)[1], T["st%dc" % tile[t]][:, st], T["st%ds" % tile[t]][:, st], T.xqc[:, c], T.xqs[:, c],
                                True, True).then_inc(S.mm, 1)
 
-    for t in range(RD):
-        for h in range(2):
+    for t, hs in [(t, (0, 1)) for t in range(RD - 1)] + [(RD - 1, (0,)), (RD - 1, (1,))]:
+        for h in hs:
             i = evac[t, h]
             g.sync.wait_ge(S[queue[i]], tok[i])
-        g.sync.dma_start(T.y[:, 256 * t:256 * t + 256], T.yb[:, 256 * t:256 * t + 256]).then_inc(S.sy, 16)
+        c = slice(256 * t + 128 * hs[0], 256 * t + 128 * hs[-1] + 128)
+        g.sync.dma_start(T.y[:, c], T.yb[:, c]).then_inc(S.sy, 16)
     g.sync.wait_ge(S.v, count["v"])
     g.sync.wait_ge(S.a, count["a"])
-    g.sync.wait_ge(S.sy, 16 * RD)
+    g.sync.wait_ge(S.sy, 16 * (RD + 1))
     g.wait_ge(S.loc, left[0])

@@ -11,7 +11,7 @@ OWN = 2 * HALF
 POOL = 2 * OWN + BLK
 AWAY = 4096.0
 LC = 9
-XA = 3
+XA_END, XA_MID = 4, 4
 PAD = 8
 KC = 256
 
@@ -36,10 +36,9 @@ for _t in range(RD):
     SCRATCH["st%dc" % _t] = ("sbuf", [128, 256], CODES)
     SCRATCH["st%ds" % _t] = ("sbuf", [128, 256], "uint8")
 _WORK = {
-    "pf": 16, "kf": 8, "z64": 64, "one8": 8, "c64": 128, "cut": 128, "n48": 48, "io64": 64,
-    "gd": 64, "xx": 96, "kq": KC + 80, "mk": 32, "lf": 2, "t4": 8, "v64": 64, "nb1": 2, "nb2": 2,
-    "rec": 96, "rec0": 96, "rec1": 96, "rec2": 96, "rec3": 96,
-    "d0": 64, "d1": 64, "d2": 64, "d3": 64, "d4": 8, "s0": 48, "s1": 48, "s2": 48, "s3": 48,
+    "pf": 16, "kf": 8, "z64": 64, "one32": 32, "wv": 32, "c64": 128, "cut": 128, "n48": 48, "io64": 64,
+    "gd": 64, "xx": 96, "kq": KC + 80, "mk": 32, "lf": 2, "t4": 8, "v64": 64, "nb1": 2, "nb2": 4, "nb3": 2, "cc": 24, "e3": 4,
+    "rec": 72, "rec0": 72, "rec1": 72, "rec2": 72, "d0": 48, "d1": 48, "d2": 48, "s0": 32, "s1": 32, "s2": 32,
     "me1": 128, "me3": 128, "fm1": 128, "fm3": 128, "ln1": 128, "ln3": 128,
 }
 for _t in (1, 3):
@@ -49,19 +48,21 @@ for _t in range(RD):
 for _n in _WORK:
     SCRATCH[_n] = ("sbuf", [128, _WORK[_n]], F32)
 
-_ARR = ["aw", "am", "b1n", "b1o", "b3n", "b3o", "h0", "h1", "h2"]
-SEMAPHORES = ["v", "a", "mm", "gi", "sdm", "sw", "sxa", "sxb", "sy", "al", "loc", "shc", "shs"] + [n + k for n in _ARR for k in "cs"]
+_ARR = ["aw", "am", "b10", "b11", "b30", "b31", "far", "h0", "h1"]
+SEMAPHORES = ["v", "a", "t", "s", "gi", "sdm", "sw", "sxa", "sxb", "al", "loc", "shc", "shs"] + [n + k for n in _ARR for k in "cs"]
 
 ADD, SUB, MUL, MIN = AluOpType.add, AluOpType.subtract, AluOpType.mult, AluOpType.min
 LT, GT, GE, NE = AluOpType.is_lt, AluOpType.is_gt, AluOpType.is_ge, AluOpType.not_equal
 AND, SHR = AluOpType.bitwise_and, AluOpType.logical_shift_right
 COPY, IDENT = ActivationFunctionType.Copy, ActivationFunctionType.Identity
 
-T_CYC, T_PE, T_SLACK = 0.001, 0.3, 0.02
-T_ROLE = {"mid": (0.15, 0.2), "edge": (0.14, 0.1), "near": (0.17, 0.5)}
-T_BLOCK, T_LAST, T_SCALES = 1.0, 3.0, 0.3
-T_EXT = {"gi": 1.0, "sw": 2.3, "sxa": 4.0, "al": 6.0, "aw": 8.2, "sxb": 8.5, "am": 11.0, "sh": 10.5, "far": 12.0, "b3": 13.5}
-T_MID = {"aw": 9.0, "b1": 11.5, "sxb": 11.8}
+T_CYC, T_WAKE, T_SLACK, T_FULL = 0.00104, 0.15, 0.02, 1.0
+T_BLOCK, T_LAST, T_SCALES, T_OUT, T_STORE = 6.0, 5.0, 0.4, 1.3, 1.6
+T_EXT = {"gi": 1.0, "sdm": 1.5, "sw": 2.3, "sxa": 4.0, "al": 5.0, "awc": 6.5, "aws": 8.5, "sxb": 7.0, "am": 10.3, "sh": 9.5, "farc": 11.5, "fars": 11.3}
+EV_FROM, SPLIT3 = {"mid": 2, "edge": 0, "near": 2}, False
+T_EDGE = {"al": 4.7, "am": 11.3, "farc": 12.8, "fars": 12.3}
+T_MID = {"al": 5.2, "aws": 7.0, "sxb": 9.7}
+T_BLOCKS = (10.3, 10.8, 11.8, 11.1, 12.3, 11.7, 13.0, 12.6)
 
 
 def R(name, a, b, step=1):
@@ -84,12 +85,17 @@ def relays(T, topo, r):
         to = lambda qs: [(q, "p2", OWN + HALF * (r % 2)) for q in qs]
         ends = [1, NR - 2, 0, NR - 1]
         across = [q for q in ends if on_plane(T, topo, r, q // 2) != q]
-        return [(h, "hb", HALF, "h0", to([q]), "am") for h, q in zip(hs[-2:], across)]
-    q = on_plane(T, topo, r, 1)
-    other = int(r // 4 != q % 2)
-    return [(hs[-1], "ha", HALF, "h0", [(r ^ 1, "p1", HALF * (r % 2))], "aw"),
-            (hs[-1], "hc", BLK, "h1", [(on_plane(T, topo, r, 2 - r // 2), "p2", 2 * OWN)], "b1o"),
-            (hs[-1], "hd", BLK, "h2", [(q, "p2", OWN + BLK * (2 + other))], "b3" + "no"[other])]
+        outer = [q for q in ends[2:] if q not in across]
+        return [(h, "hb", HALF, "h0", to([q]), "am") for h, q in zip([hs[0], hs[0], hs[-1]], across[:1] + outer + across[1:])]
+    first = (hs[-1], "ha", HALF, "h0", [(r ^ 1, "p1", HALF * (r % 2))], "aw")
+    if r not in (0, NR - 1):
+        return [first, (hs[-1], "hc", BLK, "h1", block_places(1, r // 4)[1:], "b1%d" % (r // 4)),
+                (hs[-1], "hc", BLK, "h1", [(NR - 1 - (r ^ 1), "p2", 2 * OWN)], "far")]
+    return [first, (hs[-1], "hd", BLK, "h1", block_places(3, r // 4)[1:], "b3%d" % (r // 4))]
+
+
+def block_places(t, b):
+    return [(2 + b, "p2", OWN + BLK * (t - 1)), (3 - b, "p2", OWN + BLK * t)]
 
 
 def side(T, name, kind, a, n):
@@ -114,7 +120,7 @@ def hand_on(g, core, T, topo):
             if h != core:
                 continue
             eng = topo.engines(core, T.cores[dsts[0][0]])
-            for kind in "s" if buf in ("ha", "hd") else "cs":
+            for kind in {"ha": "s", "hb": "cs", "hc": "c", "hd": "s"}[buf]:
                 g.wait_ge(T.sem[sem + kind], len(chip_engines(T, topo, r)))
                 g.remote_dma_fused([transfer(T, topo, side(T, buf, kind, 0, n), [(T.cores[q], side(T, b, kind, c, n)) for q, b, c in dsts],
                                              T.sem[there + kind], eng)], local_sem=T.sem.loc)
@@ -161,9 +167,9 @@ def rank_program(g, core, T, topo):
         args = (ap(out), ap(in0), val(s1), None, op0) if op1 is None else (ap(out), ap(in0), val(s1), val(s2), op0, op1)
         return note("v", vec.tensor_scalar, args, [x for x in (in0, s1, s2) if isinstance(x, tuple)], [out], width(out), ext)
 
-    def af(out, in0, bias):
+    def af(out, in0, bias, scale=1.0):
         return note("a", sca.activation, (ap(out), ap(in0), IDENT), [x for x in (in0, bias) if isinstance(x, tuple)], [out],
-                    width(out), kw={"bias": val(bias)})
+                    width(out), kw={"bias": val(bias), "scale": scale})
 
     def tt(out, a, b, op, ext=()):
         return note("v", vec.tensor_tensor, (ap(out), ap(a), ap(b), op), [a, b], [out], 2 * width(out), ext)
@@ -192,26 +198,27 @@ def rank_program(g, core, T, topo):
 
     picks = {}
 
-    def pick(key, dst, src, wid, o, ext, tail=0.0, at=0):
+    def pick(key, dst, src, wid, o, ext, tail=0.0, at=0, by="a"):
         n = width(o)
         c, d, w = 50 + 1.5 * 16 * n, R(dst + "c", at, at + 16 * n), R(src + "c", 0, wid)
         i = note("v", vec.tensor_copy, (ap(d).bitcast(dt.uint32), ap(w).bitcast(dt.uint32).indirect(ap(o))), [w, o], [d], c,
                  [(s + "c", k) for s, k in ext], tail)
         d, w = R(dst + "s", at, at + 16 * n), R(src + "s", 0, wid)
-        j = note("a", sca.activation, (ap(d), ap(w).indirect(ap(o)), COPY), [w, o], [d], c, [(s + "s", k) for s, k in ext], tail)
+        call, args = (sca.activation, (COPY,)) if by == "a" else (vec.tensor_copy, ())
+        j = note(by, call, (ap(d), ap(w).indirect(ap(o))) + args, [w, o], [d], c, [(s + "s", k) for s, k in ext], tail)
         picks[key] = (i, j)
 
     c2 = [0, 1, 2] if mid else [near, near + 1]
     b3 = [0, 1] if mid else [near]
     keys = [(1, 1), (3, 1)] + [(2 * c, 2) for c in c2] + [(2 * b + 1, 3) for b in b3] + [(base, 4)]
     first = {1: 0, 2: 2, 3: 2 + len(c2), 4: len(keys) - 1, 5: len(keys)}
-    nk = len(keys) + 1
+    nk = len(keys) + (not mid)
 
     def col(t, pos, n=1):
         c = PAD + 8 * (nk - 1) + pos
         return R("rec%d" % t, c, c + n)
 
-    for n in ["z64", "gd", "xx", "mk", "rec0", "rec1", "rec2", "d0", "d1", "d2"] + (["rec3", "d3"] if mid else ["in1", "in3"]):
+    for n in ["z64", "gd", "xx", "mk", "rec0", "rec1", "rec2", "d0", "d1", "d2"] + ([] if mid else ["in1", "in3"]):
         fill(n, 0.0)
     fill("kq", 0.0, KC)
     gi = [("gi", 3 if mid else 4)]
@@ -236,25 +243,27 @@ def rank_program(g, core, T, topo):
     for c in range(nl):
         ts(R("kf", c, c + 1), P(5), float(at_key[2 * c + 1] - at_key[2 * c]), MUL, float(at_key[2 * c]), ADD)
     ts(R("klist", 0, nl), R("kf", 0, nl), F(9), ADD)
-    for q in range(NR):
+    for q in range(0 if mid else NR):
         home = HALF * (q % 2) + (0 if q // 2 == pair else OWN if q // 2 == 1 else AWAY)
         c = KC + 64 * (q % 2) + q // 2
         ts(R("kq", c, c + 1), F(4), float(home), MUL, F(6), ADD)
+    for c in range(4 if mid else 0):
+        ts(F(10 + c), F(6), HALF * (c % 2) + AWAY * (c // 2), ADD)
     nc = 128 if mid else 64
     ts(R("cut", 0, nc), R("c64", 0, nc), F(1), NE, ext=gi)
     fill("cut", -1.0, 32, nc, 64)
     his = HALF * (1 - e)
     if not mid:
-        fill("one8", 1.0)
+        fill("one32", 1.0)
 
     my = (HALF * e, HALF * (e + 1))
     src_w = "p2" if mid else "p1"
     i_w = quant(R(src_w + "c", *my), R(src_w + "s", *my), R("wt", 0, 1024), [("sw", 16)], 20.0)
     if not mid:
         quant(R("p2c", *my), R("p2s", *my), R("wt", 0, 1024), [("sw", 16)])
-    i_x = [quant(R("xqc", 0, 128 * XA), R("xqs", 0, 128 * XA), R("xt", 0, 512 * XA), [("sxa", 16)])] * XA
-    for t in range(XA, RD):
-        i_x.append(quant(R("xqc", 128 * t, 128 * t + 128), R("xqs", 128 * t, 128 * t + 128), R("xt", 512 * t, 512 * t + 512), [("sxb", 16)], 3.0))
+    XA = XA_MID if mid else XA_END
+    for t in range(RD):
+        quant(R("xqc", 128 * t, 128 * t + 128), R("xqs", 128 * t, 128 * t + 128), R("xt", 512 * t, 512 * t + 512), [("sxa" if t < XA else "sxb", 16)])
 
     tt(R("gd", 0, 5 * LC), R("lst", 0, 5 * LC), R("lst", LC, 6 * LC), SUB, [("sdm", 128), ("al", (NR - 1) * n_off)])
     tr(R("xx", 0, 64), R("gd", 0, 64))
@@ -305,16 +314,24 @@ def rank_program(g, core, T, topo):
 
     def lanes_out(t, k, pos, ext, tail):
         n, lo = str(t), 2 * near + 1
-        if t == 1:
-            af(R("wn" + n, 0, 32), R("z64", 0, 32), R("nb1", near, near + 1))
-        else:
-            ts(R("wn" + n, 0, 32), R("z64", 0, 32), old(t, k, lo), ADD, old(t, k, lo + 1), SUB)
-        ts(R("me" + n, 0, 32), R("wn" + n, 0, 32), step(t, k, lo), SUB, step(t, k, lo + 1), LT)
-        ts(R("me" + n, 32, 64), R("z64", 0, 32), old(t, nk - 1, pos), ADD, step(t, nk - 1, pos), ADD if near else SUB)
+
+        def was(kk, x):
+            c = at_key[kk] + 64 * (x % 2) + x // 2
+            return R("kq", c, c + 1) if t == 1 else old(t, kk, x)
+
+        ts(R("wn" + n, 0, 32), R("z64", 0, 32), was(k, lo), ADD, was(k, lo + 1), SUB)
+        steps = [R("e3", i, i + 1) for i in range(3)]
+        for s, (kk, x) in zip(steps, [(k, lo), (k, lo + 1), (nk - 1, pos)]):
+            ts(s, was(kk, x | 1), was(kk, x & ~1), SUB, M(t - 1, x // 2), MUL)
+        ts(R("me" + n, 0, 32), R("wn" + n, 0, 32), steps[0], SUB, steps[1], LT)
+        o, c = R("wv", 0, 32), was(nk - 1, pos)
+        note("a", sca.activation, (ap(o), ap(R("one32", 0, 32)), IDENT), [R("one32", 0, 32), c], [o], 32, kw={"scale": ap(c)})
+        af(R("me" + n, 32, 64), o, steps[2], 1.0 if near else -1.0)
         tr(R("fm" + n, 0, 64), R("me" + n, 0, 64))
-        tt(R("dv" + n, 0, 8), R("fm" + n, 32, 40), R("fm" + n, 33, 41), SUB)
-        ci(R("dr" + n, 0, 48), R("dv" + n, 0, 8), R("l8", 0, 3))
-        scan(R("in" + n, 1, 9), R("one8", 0, 8), R("fm" + n, 0, 8))
+        tt(R("dv" + n, 0, 8), R("fm" + n, 33 - near, 41 - near), R("fm" + n, 32 + near, 40 + near), SUB)
+        o, w, l = R("dr" + n, 0, 48), R("dv" + n, 0, 8), R("l8", 0, 3)
+        note("a", sca.activation, (ap(o), ap(w).indirect(ap(l)), COPY), [w, l], [o], 65 + 1.5 * 48)
+        scan(R("in" + n, 1, 9), R("one32", 0, 8), R("fm" + n, 0, 8))
         ti(R("ge" + n, 0, 48), R("in" + n, 0, 16), R("l8", 0, 3), R("n48", 0, 48), GE)
         scan(R("sl" + n, 0, 40), R("ge" + n, 0, 40), R("dr" + n, 0, 40))
         for h in range(2):
@@ -339,74 +356,93 @@ def rank_program(g, core, T, topo):
     masks(1, [1, 3])
     change(1)
 
-    def arrivals(t, lane):
-        for b in range(2):
-            ts(col(t, 2 + b), lane[b], float(OWN + BLK * (t - 1 + (b != near))), ADD, col(t, 2 + b), MIN)
-
-    if mid:
-        arrivals(1, lanes_in(1, 0, [M(1, 1), M(1, 2)]))
-    else:
+    if not mid:
         pos = 1 + 3 * near
-        lanes_out(1, near, pos, aw, T_BLOCK)
+        if not edge:
+            lanes_out(1, near, pos, aw, T_BLOCK)
         af(R("lf", 0, 1), lanes_in(1, 64, [M(1, 2 - near)])[0], float(2 * OWN))
     diff(2)
-    if mid:
-        ts(R("mk", 16 + c2[0], 17 + c2[-1]), R("d2", c2[0], c2[0] + 5 * len(c2) - 4, 5), 0.0, GT)
-    else:
+    if mid or edge:
         masks(2, [2 * c for c in c2])
+    else:
+        ts(R("mk", 16 + near, 18 + near), R("d2", near, near + 6, 5), 0.0, GT)
     change(2)
     U = lambda c: R("t4", c, c + 1)
+    k4 = first[4]
     if mid:
-        diff(3)
-        ts(R("mk", 25, 27), R("d3", 1, 7, 5), 0.0, GT)
-        change(3)
-        arrivals(3, lanes_in(3, 0, [M(3, 1), M(3, 2)]))
-        diff(4)
-        ts(U(0), R("d4", pair, pair + 1), 0.0, GT, R("d4", 4 + pair, 5 + pair), MUL)
-        held, back = col(3, r), e
+        masks(3, [1, 3])
+        for b in range(2):
+            ts(U(1 + b), old(3, k4, 1 + 3 * b, "rec2"), old(3, k4, 2 + b, "rec2"), SUB, M(3, 1 + b), MUL)
+        tt(U(3), old(3, k4, 2, "rec2"), old(3, k4, 3, "rec2"), SUB)
+        ts(U(4), U(2), U(1), SUB, U(3), GT)
+        C = lambda n, b: R("cc", 2 * n + b, 2 * n + b + 1)
+        sg = (1.0, -1.0)
+        lane1, lane3 = lanes_in(1, 0, [M(1, 1), M(1, 2)]), lanes_in(3, 0, [M(3, 1), M(3, 2)])
+        for b in range(2):
+            af(C(0, b), M(0, 1), F(10 + b), sg[b] * HALF)
+            af(C(4, b), C(0, b), float(OWN + BLK * (b != near)), -1.0)
+            ts(C(5, b), lane1[b], C(4, b), ADD, M(1, 1 + b), MUL)
+            af(C(1, b), C(5, b), C(0, b))
+            af(C(6, b), M(0, 1), F(12 + b), sg[b] * HALF)
+            af(C(7, b), M(1, 1 + b), C(6, b), -AWAY)
+            af(C(8, b), M(2, 2 * b), C(7, b), AWAY)
+        ts(U(5), C(1, 1), C(1, 0), SUB, M(2, 1), MUL)
+        for b in range(2):
+            af(C(2, b), U(5), C(1, b), sg[b])
+            ts(C(9, b), lane3[b], float(OWN + BLK * (2 + (b != near))), ADD, C(8, b), MIN)
+            ts(C(10, b), C(9, b), C(2, b), SUB, M(3, 1 + b), MUL)
+            af(C(3, b), C(10, b), C(2, b))
+        ts(U(0), C(3, 1 - e), C(3, e), SUB, U(4), MUL)
+        held, back = C(3, e), 0
     else:
-        lanes_out(3, first[3], pos, aw, T_LAST)
-        out, oth, k4 = 2 + near, (NR - 1) * near, first[4]
+        if not edge:
+            masks(3, [2 * near + 1])
+            m3 = M(3, 1 + near)
+        else:
+            lanes_out(3, first[3], pos, aw, T_LAST)
+            m3 = R("me3", 0, 1)
+        out, oth = 2 + near, (NR - 1) * near
         for c, k in ((1, k4), (2, nk - 1)):
-            ts(U(c), old(3, k, out, "rec2"), old(3, k, pos, "rec2"), SUB, R("me3", 0, 1), MUL)
+            ts(U(c), old(3, k, out, "rec2"), old(3, k, pos, "rec2"), SUB, m3, MUL)
         ts(U(3), U(2), col(2, pos), ADD, R("lf", 0, 1), MIN)
         ts(U(4), U(1), old(3, k4, pos, "rec2"), ADD, old(3, k4, oth, "rec2"), LT if near else GT)
         ts(U(0), U(3), col(2, oth), SUB, U(4), MUL)
         held, back = (col(2, oth), 0) if edge else (U(3), 1)
 
-    def out_of(t, h):
-        bank, c = 512 * ((2 * t + h) % 8), 256 * t + 128 * h
-        return T.yb[:, c:c + 128], T.ps[:, bank:bank + 128]
-
     if mid:
-        names = ["b1n", "b1o", "b3n", "b3o"]
+        names = ["b%d%d" % (t, b) for t in (1, 3) for b in (near, 1 - near)]
         src = [("p2", OWN + BLK * t, aw + [(s, n_off) for s in names[:t]]) for t in range(RD)]
     else:
         am = [("sh", 16), ("am", 2 * n_off)]
-        src = [("p1", OWN, aw)] + [("p2", 2 * OWN, am)] * 2 + [("p2", POOL, am + [("b1o", n_off)])] * 2
+        src = [("p1", OWN, aw)] + [("p2", 2 * OWN, am)] * 2 + [("p2", POOL, am + [("far", n_off)])] * 2
     tile = [t - 1 if edge and t % 2 else t for t in range(RD)]
-    evac = {}
+    stores, lists, outs = [], [], []
     for t in range(RD):
         if tile[t] == t:
             wc, tc = R("wc%d" % t, 0, 64), R("tc%d" % t, 0, 64)
             if t < 4:
-                af(wc, R("io64", 0, 64), col(t, r) if t < 3 else held)
+                af(wc, R("io64", 0, 64), held if t == 3 else C(t, e) if mid else col(t, r))
             else:
                 ts(wc, R("io64", 0, 64), U(0), SUB if back else ADD, held, ADD)
             tr(tc, wc)
-            ci(R("of%d" % t, 0, 16), tc, R("lkh", 0, 1))
-            if t < RD - 1:
+            lists.append(ci(R("of%d" % t, 0, 16), tc, R("lkh", 0, 1)))
+            if mid and t == 3 and SPLIT3:
+                for h in range(2):
+                    pick((t, h), "st3", src[t][0], src[t][1], R("of3", 8 * h, 8 * h + 8), src[t][2], 0.0, 128 * h, "av"[h])
+            elif t < RD - 1:
                 pick((t, 0), "st%d" % t, src[t][0], src[t][1], R("of%d" % t, 0, 16), src[t][2])
-                picks[t, 1] = picks[t, 0]
             else:
                 for h in range(2):
-                    pick((t, h), "st%d" % t, src[t][0], src[t][1], R("of%d" % t, 8 * h, 8 * h + 8), src[t][2], 2.5 * h, 128 * h)
+                    pick((t, h), "st%d" % t, src[t][0], src[t][1], R("of%d" % t, 8 * h, 8 * h + 8), src[t][2], 0.0, 128 * h)
         for h in range(2):
-            q = "v" if t >= 3 and h == 0 else "a"
-            args = out_of(t, h) if q == "v" else out_of(t, h) + (COPY,)
-            evac[t, h] = note(q, vec.tensor_copy if q == "v" else sca.activation, args,
-                              [R("st%d%s" % (tile[t], k), 128 * h, 128 * h + 1) for k in "cs"] + [R("xqc", 0, 128 * t + 128)],
-                              [R("yb", 256 * t + 128 * h, 256 * t + 128 * h + 128)], 128, [("mm", 2 * t + h + 1)], 2.0 if t == 4 else 1.0, T_PE)
+            bank, c = 512 * ((2 * t + h) % 8), 256 * t + 128 * h
+            ps, yb = R("ps", bank, bank + 128), R("yb", c, c + 128)
+            ins = [R("st%d%s" % (tile[t], k), 128 * h, 128 * h + 128) for k in "cs"] + [R("xq" + k, 128 * t, 128 * t + 128) for k in "cs"]
+            note("t", g.tensor.matmul_mx, (ap(ps), *[ap(x) for x in ins], True, True), ins, [ps], 190)
+            outs.append(note("va"[h], None, (ap(yb), ap(ps)), [ps], [yb], 128))
+        for a, b in [(0, 256)] if t < RD - 1 else [(0, 128), (128, 256)]:
+            yb = R("yb", 256 * t + a, 256 * t + b)
+            stores.append(note("s", g.sync.dma_start, (T.y[:, yb[1]:yb[2]], ap(yb)), [yb], [], T_STORE * (b - a), tail=T_OUT))
 
     n_ops = len(ops)
     queue = [o[0] for o in ops]
@@ -423,48 +459,67 @@ def rank_program(g, core, T, topo):
         for kind, regs in (("r", o[4]), ("w", o[5])):
             for name, a, b, step in regs:
                 hist.setdefault(name, []).append((i, kind, set(range(a, b, step))))
-    chain = [(t, 0) for t in sorted(set(tile))] + [(RD - 1, 1)]
+    for a, b in zip(stores, stores[1:]):
+        seq[b].add(a)
     if not mid:
-        chain = ["snd1", "snd3"] + chain
-    for a, b in zip(chain, chain[1:]):
         for n in range(2):
-            seq[picks[b][n]].add(picks[a][n])
-    T_WAKE, T_URGENT = T_ROLE["mid" if mid else "edge" if edge else "near"]
-    prio = [0.0] * n_ops
-    for i in range(n_ops - 1, -1, -1):
-        prio[i] += ops[i][7] + ops[i][8]
+            seq[picks[0, 0][n]].add(picks["snd3" if edge else "snd1"][n])
+    cost = [o[7] for o in ops]
+    prio = [o[8] for o in ops]
+    topo_order, seen = [], set()
+    while len(topo_order) < n_ops:
+        for i in range(n_ops):
+            if i not in seen and raw[i] <= seen and seq[i] <= seen:
+                seen.add(i)
+                topo_order.append(i)
+    for i in topo_order[::-1]:
+        prio[i] += cost[i]
         for j in raw[i]:
             prio[j] = max(prio[j], prio[i] + T_WAKE)
         for j in seq[i]:
             prio[j] = max(prio[j], prio[i])
+    ext = dict(T_EXT)
+    if mid:
+        ext.update(T_MID, **dict(zip([n + k for n in names for k in "cs"], T_BLOCKS)))
+    if edge:
+        ext.update(T_EDGE)
 
     def ext_time(s):
-        if mid and s[:3] in T_MID:
-            return T_MID[s[:3]]
-        if mid and s[:2] in T_MID:
-            return T_MID[s[:2]]
-        if s in T_EXT or s in ("sdm", "mm"):
-            return T_EXT.get(s, 0.0)
-        return T_EXT["far" if s[:2] == "b1" else s[:2]] + (T_SCALES if s[-1] == "s" else 0.0)
+        return ext[s] if s in ext else ext[s[:-1]] + (T_SCALES if s[-1] == "s" else 0.0)
 
-    done, tok, now, count, order = {}, {}, {"v": 0.0, "a": 0.6}, {"v": 0, "a": 0}, []
-    while len(order) < n_ops:
-        ready = []
-        for i in range(n_ops):
-            if i in tok or not all(j in tok for j in raw[i]) or not all(j in tok for j in seq[i]):
-                continue
-            at = max([now[queue[i]]] + [done[j] + T_WAKE + ops[i][9] for j in raw[i]] + [ext_time(s) for s, _ in ops[i][6]])
-            ready.append((at, -prio[i], i))
-        best = min(ready)
-        urgent = [c for c in ready if queue[c[2]] == queue[best[2]] and c[1] < best[1] - T_URGENT and c[0] < best[0] + ops[best[2]][7] - T_SLACK]
-        if urgent:
-            best = min(urgent, key=lambda c: c[1])
-        i = best[2]
-        q = queue[i]
-        now[q] = done[i] = best[0] + ops[i][7]
-        count[q] += 1
-        tok[i] = count[q]
-        order.append(i)
+    def arrange(queue):
+        done, tok, now, count, order = {}, {}, {q: 0.0 for q in "vats"}, {q: 0 for q in "vats"}, []
+        while len(order) < n_ops:
+            ready = []
+            for i in range(n_ops):
+                if i in tok or not all(j in tok for j in raw[i]) or not all(j in tok for j in seq[i]):
+                    continue
+                at = max([now[queue[i]]] + [done[j] + T_WAKE for j in raw[i]] + [ext_time(s) for s, _ in ops[i][6]])
+                ready.append((at, -prio[i], i))
+            best = min(ready)
+            at, _, i = best
+            q = queue[i]
+            rest = sum(cost[j] for j in range(n_ops) if j not in tok and queue[j] == q) * T_FULL + T_OUT
+            gain = [(max(at + prio[i], at + cost[i] + prio[j], at + rest) - max(a + prio[j], a + cost[j] + prio[i], a + rest), a, j)
+                    for a, _, j in ready if queue[j] == q and a < at + cost[i]]
+            if max(gain)[0] > T_SLACK:
+                _, a, j = max(gain)
+                fit = [c for c in ready if queue[c[2]] == q and c[0] + cost[c[2]] <= a + T_SLACK]
+                best = min(fit, key=lambda c: c[1]) if fit else (a, 0, j)
+            i = best[2]
+            now[q] = done[i] = best[0] + cost[i]
+            count[q] += 1
+            tok[i] = count[q]
+            order.append(i)
+        return now["s"], tok, count, order
+
+    plan = arrange(queue)
+    for i in outs[::-1]:
+        other = queue[:i] + ["a" if queue[i] == "v" else "v"] + queue[i + 1:]
+        trial = arrange(other)
+        if trial[0] < plan[0] - T_SLACK:
+            queue, plan = other, trial
+    _, tok, count, order = plan
 
     for b in range(4):
         for h, q in ((0, g.sync), (1, sca)):
@@ -472,29 +527,34 @@ def rank_program(g, core, T, topo):
             q.dma_start(T.lst[p0:p0 + 16, LC * r:LC * r + LC], T.dm[:, 6 * h:6 * h + LC]).then_inc(S.sdm, 16)
     g.sync.dma_start(T.wt[:], T.w[:]).then_inc(S.sw, 16)
     g.sync.dma_start(T.xt[:, 0:512 * XA], T.x[:, 0:512 * XA]).then_inc(S.sxa, 16)
-    g.sync.wait_ge(S.al, (NR - 1) * n_off)
-    g.sync.dma_start(T.xt[:, 512 * XA:], T.x[:, 512 * XA:]).then_inc(S.sxb, 16)
+    if XA < RD:
+        g.sync.wait_ge(S.al, (NR - 1) * n_off)
+        g.sync.dma_start(T.xt[:, 512 * XA:], T.x[:, 512 * XA:]).then_inc(S.sxb, 16)
 
     if not mid:
         for kind in "cs":
             g.sync.wait_ge(S["aw" + kind], n_off)
+            if kind == "s" and not edge:
+                g.sync.wait_ge(S.a, tok[picks["snd1"][1]])
             g.sync.dma_start(side(T, "p2", kind, his, HALF), side(T, "p1", kind, his, HALF)).then_inc(S["sh" + kind], 16)
 
     waited = {}
 
     def wait(q, sem, n):
         if waited.get((q, sem), 0) < n:
-            (vec if q == "v" else sca).wait_ge(S[sem], n)
+            {"v": vec, "a": sca, "t": g.tensor, "s": g.sync}[q].wait_ge(S[sem], n)
             waited[q, sem] = n
 
     wait("a", "gi", gi[0][1])
     for i in order:
-        q, call, args, kw, reads, writes, ex, cost, tail, lag = ops[i]
+        q, (call, args, kw), ex = queue[i], ops[i][1:4], ops[i][6]
+        if call is None:
+            call, args = (vec.tensor_copy, args) if q == "v" else (sca.activation, args + (COPY,))
         for sem, n in ex:
             wait(q, sem, n)
-        for s in ("v", "a"):
+        for s in "vat":
             wait(q, s, max([0] + [tok[j] for j in raw[i] if queue[j] == s]))
-        call(*args, **kw).then_inc(S[q], 1)
+        call(*args, **kw).then_inc(S[q], 16 if q == "s" else 1)
 
     big = {"allow_small_or_imprecise_dtypes": True}
     g.iota(T.pi[:, 0:1], [[0, 1]], 0, 1).then_inc(S.gi, 1)
@@ -508,7 +568,7 @@ def rank_program(g, core, T, topo):
         g.remote_dma_fused(trs, local_sem=S.loc)
         left[0] += n_off * len(trs)
 
-    others = sorted([q for q in range(NR) if q != r], key=lambda q: (q // 2 == 1, (q - r) % NR))
+    others = sorted([q for q in range(NR) if q != r], key=lambda q: (q // 2 == 1, q not in (0, NR - 1), (q - r) % NR))
     mycol = T.lst[:, LC * r:LC * r + LC]
     g.wait_ge(S.sdm, 128)
     send([transfer(T, topo, mycol, [(cores[q], mycol) for q in others], S.al, off_eng)])
@@ -516,43 +576,39 @@ def rank_program(g, core, T, topo):
     g.wait_ge(S.v, tok[i_w])
     for kind in "cs":
         src_v = side(T, src_w, kind, my[0], HALF)
-        to_h = [(h, side(T, buf, kind, 0, HALF)) for h, buf, n, sem, _, _ in rel if sem == "h0"]
+        to_h = [(h, side(T, buf, kind, 0, HALF)) for h, buf, n, sem, _, _ in (rel[1:] if mid else rel[:1])]
         trs = [transfer(T, topo, src_v, [(cores[mate], src_v)], S["aw" + kind], off_eng), transfer(T, topo, src_v, to_h, S["h0" + kind], on_eng)]
         send(trs if mid else trs[:1] if kind == "c" else trs[1:])
     if mid:
-        for q in sorted([on_plane(T, topo, r, s) for s in (0, 2)], key=lambda q: q in (0, NR - 1)):
-            for kind in "cs":
-                send([transfer(T, topo, side(T, "p2", kind, my[0], HALF), [(cores[q], side(T, "p2", kind, OWN + my[0], HALF))], S["am" + kind], off_eng)])
+        q = on_plane(T, topo, r, 2 - 2 * near)
+        for kind in "cs":
+            send([transfer(T, topo, side(T, "p2", kind, my[0], HALF), [(cores[q], side(T, "p2", kind, OWN + my[0], HALF))], S["am" + kind], off_eng)])
+        g.wait_ge(S["b1%dc" % near], n_off)
+        send([transfer(T, topo, side(T, "p2", "c", OWN, BLK), [(cores[NR - 2 - 3 * near], side(T, "p2", "c", 2 * OWN, BLK))], S.farc, off_eng)])
     else:
-        q = on_plane(T, topo, r, 1)
-        other = int(near != q % 2)
-        for t in (1, 3):
-            key = "snd%d" % t
-            for kind, sem, i in zip("cs", (S.v, S.a), picks[key]):
-                g.wait_ge(sem, tok[i])
-                src_v = side(T, key, kind, 0, BLK)
-                trs = [transfer(T, topo, src_v, [(cores[q], side(T, "p2", kind, OWN + BLK * (t - 1 + other), BLK))],
-                                S["b%d%s%s" % (t, "no"[other], kind)], off_eng)]
-                h, buf, n, sem, _, _ = rel[(t + 1) // 2]
-                trs.append(transfer(T, topo, src_v, [(h, side(T, buf, kind, 0, BLK))], S[sem + kind], on_eng))
-                send(trs if t == 1 else trs[:1] if kind == "c" else trs[1:])
+        t = 3 if edge else 1
+        key = "snd%d" % t
+        h, buf, n, hsem, _, _ = rel[1]
+        to_h = lambda kind: transfer(T, topo, side(T, key, kind, 0, BLK), [(h, side(T, buf, kind, 0, BLK))], S[hsem + kind], on_eng)
+        to_mid = lambda kind, ds: transfer(T, topo, side(T, key, kind, 0, BLK), [(cores[q], side(T, b, kind, c, BLK)) for q, b, c in ds],
+                                           S["b%d%d%s" % (t, near, kind)], off_eng)
+        ds = block_places(t, near)
+        if t == 1:
+            g.wait_ge(S.v, tok[picks[key][0]])
+            send([to_mid("c", ds[:1]), to_h("c")])
+            to_far = lambda kind, qs: transfer(T, topo, side(T, key, kind, 0, BLK), [(cores[q], side(T, "p2", kind, 2 * OWN, BLK)) for q in qs],
+                                               S["far" + kind], off_eng)
+            inner, outer = NR - 1 - r, NR - 1 - mate
+            g.wait_ge(S.a, tok[picks[key][1]])
+            send([to_mid("s", ds)])
+            send([to_far("s", [inner, outer])])
+        else:
+            g.wait_ge(S.a, tok[picks[key][1]])
+            send([to_mid("s", ds[:1]), to_h("s")])
+            g.wait_ge(S.v, tok[picks[key][0]])
+            send([to_mid("c", ds)])
 
-    for t in range(RD):
-        for h in range(2):
-            if h == 0 or t == RD - 1:
-                g.tensor.wait_ge(S.v, max(tok[picks[tile[t], h][0]], tok[i_x[t]]))
-                g.tensor.wait_ge(S.a, max(tok[picks[tile[t], h][1]], tok[evac[0, h]] if t == RD - 1 else 0))
-            st, c = slice(128 * h, 128 * h + 128), slice(128 * t, 128 * t + 128)
-            g.tensor.matmul_mx(out_of(t, h)[1], T["st%dc" % tile[t]][:, st], T["st%ds" % tile[t]][:, st], T.xqc[:, c], T.xqs[:, c],
-                               True, True).then_inc(S.mm, 1)
-
-    for t, hs in [(t, (0, 1)) for t in range(RD - 1)] + [(RD - 1, (0,)), (RD - 1, (1,))]:
-        for h in hs:
-            i = evac[t, h]
-            g.sync.wait_ge(S[queue[i]], tok[i])
-        c = slice(256 * t + 128 * hs[0], 256 * t + 128 * hs[-1] + 128)
-        g.sync.dma_start(T.y[:, c], T.yb[:, c]).then_inc(S.sy, 16)
     g.sync.wait_ge(S.v, count["v"])
     g.sync.wait_ge(S.a, count["a"])
-    g.sync.wait_ge(S.sy, 16 * (RD + 1))
+    g.sync.wait_ge(S.s, 16 * count["s"])
     g.wait_ge(S.loc, left[0])

@@ -10,21 +10,22 @@ HALF = 8 * PC
 OWN = 2 * HALF
 POOL = 2 * OWN + BLK
 AWAY = 4096.0
-LC = 9
 XA_END, XA_MID = 4, 4
 PAD = 8
-KC = 256
+SP = 24
+L0 = 16
 
 F32 = "float32"
 CODES = "float8_e4m3fn_x4"
 SCRATCH = {
     "wt": ("sbuf", [128, 1024], "bfloat16"),
     "xt": ("sbuf", [128, 512 * RD], "bfloat16"),
-    "lst": ("sbuf", [128, 56], "int32"),
+    "dmt": ("sbuf", [128, 2, RD, 3], "int32"),
+    "lst": ("sbuf", [128, NR, 48], "float16"),
     "yb": ("sbuf", [128, 256 * RD], F32),
     "ps": ("psum", [128, 4096], F32),
     "pi": ("sbuf", [128, 8], "int32"),
-    "klist": ("sbuf", [128, 6], "uint16"), "l8": ("sbuf", [128, 4], "uint16"), "l4": ("sbuf", [128, 4], "uint16"),
+    "pj": ("sbuf", [128, 4], "int32"), "l8": ("sbuf", [128, 4], "uint16"), "l3": ("sbuf", [128, 2], "uint16"),
     "lkh": ("sbuf", [128, 2], "uint16"),
     "off1": ("sbuf", [128, 10], "uint16"), "off3": ("sbuf", [128, 10], "uint16"),
 }
@@ -36,10 +37,10 @@ for _t in range(RD):
     SCRATCH["st%dc" % _t] = ("sbuf", [128, 256], CODES)
     SCRATCH["st%ds" % _t] = ("sbuf", [128, 256], "uint8")
 _WORK = {
-    "pf": 16, "kf": 8, "z64": 64, "one32": 32, "wv": 32, "c64": 128, "cut": 128, "n48": 48, "io64": 64,
-    "gd": 64, "xx": 96, "kq": KC + 80, "mk": 32, "lf": 2, "t4": 8, "v64": 64, "nb1": 2, "nb2": 4, "nb3": 2, "cc": 24, "e3": 4,
-    "rec": 72, "rec0": 72, "rec1": 72, "rec2": 72, "d0": 48, "d1": 48, "d2": 48, "s0": 32, "s1": 32, "s2": 32,
-    "me1": 128, "me3": 128, "fm1": 128, "fm3": 128, "ln1": 128, "ln3": 128,
+    "pf": 16, "kf": 4, "z64": 64, "one32": 32, "wv": 32, "c64": 128, "cut": 128, "n48": 48, "io64": 64,
+    "mk": 32, "lf": 2, "t4": 8, "v64": 64, "nb1": 2, "nb2": 4, "nb3": 2, "cc": 24, "e3": 4,
+    "rec": 64, "rec0": 64, "rec1": 64, "rec2": 64, "d0": 48, "d1": 48, "d2": 48, "s0": 32, "s1": 32, "s2": 32,
+    "me1": 160, "me3": 160, "fm1": 160, "fm3": 160, "ln1": 128, "ln3": 128,
 }
 for _t in (1, 3):
     _WORK.update({"wn%d" % _t: 32, "dv%d" % _t: 8, "dr%d" % _t: 48, "in%d" % _t: 16, "ge%d" % _t: 48, "sl%d" % _t: 48})
@@ -57,12 +58,12 @@ AND, SHR = AluOpType.bitwise_and, AluOpType.logical_shift_right
 COPY, IDENT = ActivationFunctionType.Copy, ActivationFunctionType.Identity
 
 T_CYC, T_WAKE, T_SLACK, T_FULL = 0.00104, 0.15, 0.02, 1.0
-T_BLOCK, T_LAST, T_SCALES, T_OUT, T_STORE = 6.0, 5.0, 0.4, 1.3, 1.6
-T_EXT = {"gi": 1.0, "sdm": 1.5, "sw": 2.3, "sxa": 4.0, "al": 5.0, "awc": 6.5, "aws": 8.5, "sxb": 7.0, "am": 10.3, "sh": 9.5, "farc": 11.5, "fars": 11.3}
-EV_FROM, SPLIT3 = {"mid": 2, "edge": 0, "near": 2}, False
-T_EDGE = {"al": 4.7, "am": 11.3, "farc": 12.8, "fars": 12.3}
-T_MID = {"al": 5.2, "aws": 7.0, "sxb": 9.7}
-T_BLOCKS = (10.3, 10.8, 11.8, 11.1, 12.3, 11.7, 13.0, 12.6)
+T_BLOCK, T_LAST, T_SCALES, T_OUT, T_STORE = 6.5, 5.0, 0.4, 1.3, 1.6
+T_EXT = {"gi": 1.0, "sdm": 1.5, "sw": 2.3, "sxa": 4.0, "al": 4.75, "awc": 6.25, "aws": 7.65, "sxb": 6.75, "am": 9.05, "sh": 9.55, "farc": 10.95, "fars": 10.45}
+EV_FROM, SPLIT3 = {"mid": 2, "edge": 0, "near": 2}, True
+T_EDGE = {"al": 4.45, "am": 10.45, "sh": 8.95, "farc": 11.65, "fars": 10.75}
+T_MID = {"al": 4.95, "aws": 6.65, "sxb": 8.25, "loc": 10.35}
+T_BLOCKS = (9.3, 9.6, 10.9, 9.9, 10.85, 10.1, 11.55, 11.4)
 
 
 def R(name, a, b, step=1):
@@ -215,38 +216,50 @@ def rank_program(g, core, T, topo):
     nk = len(keys) + (not mid)
 
     def col(t, pos, n=1):
-        c = PAD + 8 * (nk - 1) + pos
+        c = PAD + NR * (nk - 1) + pos
         return R("rec%d" % t, c, c + n)
 
-    for n in ["z64", "gd", "xx", "mk", "rec0", "rec1", "rec2", "d0", "d1", "d2"] + ([] if mid else ["in1", "in3"]):
+    def at_list(q, t):
+        return L0 + NR * (0 if t == 4 and q in (0, NR - 1) else t - 1)
+
+    for b in range(4):
+        note("v", vec.memset, (T.dmt[32 * b:32 * b + SP], 0), [], [R("dmt", b, b + 1)], 30, tail=30.0)
+    note("v", vec.memset, (T.lst[:, r, L0 - 2:L0 - 1], 0.0), [], [R("lst", 0, 1)], 1, tail=30.0)
+    own = [(T.lst[:, r, L0 - 1:L0], vec.tensor_tensor, (T.dmt[:, 1, 0, pair:pair + 1], T.dmt[:, 0, 0, pair:pair + 1], SUB))]
+    for h in range(2):
+        rounds, n = (slice(4, 1, -2), 2) if edge else (slice(1, RD), 4)
+        own.append((T.lst[:, r, L0 + h:L0 + NR * n:2], vec.tensor_copy, (T.dmt[:, h, rounds, :],)))
+    i_own = [note("v", call, (o,) + args, [R("dmt", 0, 4)], [R("lst", 1 + n, 2 + n)], 12, [("sdm", 128)], 30.0) for n, (o, call, args) in enumerate(own)]
+
+    for n in ["z64", "mk", "rec0", "rec1", "rec2", "d0", "d1", "d2"] + ([] if mid else ["in1", "in3"]):
         fill(n, 0.0)
-    fill("kq", 0.0, KC)
+    if not mid:
+        fill("fm3" if edge else "fm1", 0.0, 64, 72)
     gi = [("gi", 3 if mid else 4)]
     P = lambda c: R("pi", c, c + 1)
     F = lambda c: R("pf", c, c + 1)
-    for c, (sh, m) in enumerate([(0, 15), (0, 7), (0, 3), (0, 31), (3, 1), (0, 1), (1, 7)]):
+    for c, (sh, m) in enumerate([(0, 15), (0, 7), (0, 31), (0, 1), (1, 7)]):
         ts(P(c + 1), P(0), sh, SHR, m, AND, ext=gi)
-    cp(R("pf", 0, 3), R("pi", 1, 4))
+    cp(R("pf", 0, 2), R("pi", 1, 3))
     ts(F(3), F(0), 16.0, ADD)
-    ts(F(4), P(4), 8.0, LT)
+    ts(F(4), P(3), float(SP), GE)
     ts(F(5), F(4), float(PC), MUL)
     ts(R("v64", 0, 64), R("z64", 0, 64), F(5), ADD)
     tt(F(6), F(5), F(1), MUL)
-    cp(F(7), P(7))
-    ts(F(8), P(5), -4.0, MUL, F(7), ADD)
-    ts(F(9), P(6), 64.0, MUL, F(8), ADD)
+    ts(F(7), P(5), float(SP), ADD)
     ts(R("l8", 0, 4), R("z64", 0, 4), F(1), ADD)
-    ts(R("l4", 0, 4), R("z64", 0, 4), F(2), ADD)
-    ts(R("lkh", 0, 1), P(6), 32.0, MUL, F(7), ADD)
-    at_key = [128 * (t // 3) + LC * a + 3 * t - 6 * (t // 3) for a, t in keys] + [KC, KC]
-    nl = (nk + 1) // 2
-    for c in range(nl):
-        ts(R("kf", c, c + 1), P(5), float(at_key[2 * c + 1] - at_key[2 * c]), MUL, float(at_key[2 * c]), ADD)
-    ts(R("klist", 0, nl), R("kf", 0, nl), F(9), ADD)
+    ts(R("lkh", 0, 1), P(4), 32.0, MUL, F(7), ADD)
+    for c in range(2):
+        ts(R("kf", c, c + 1), F(0), float(c), ADD)
+    ts(R("pj", 0, 2), R("kf", 0, 2), 11.0, MUL)
+    ts(R("pj", 2, 4), R("pj", 0, 2), 5, SHR)
+    ts(R("kf", 2, 4), R("pj", 2, 4), -3.0, MUL)
+    tt(R("kf", 2, 4), R("kf", 2, 4), R("kf", 0, 2), ADD)
+    cp(R("l3", 0, 2), R("kf", 2, 4))
     for q in range(0 if mid else NR):
         home = HALF * (q % 2) + (0 if q // 2 == pair else OWN if q // 2 == 1 else AWAY)
-        c = KC + 64 * (q % 2) + q // 2
-        ts(R("kq", c, c + 1), F(4), float(home), MUL, F(6), ADD)
+        c = PAD + NR * (nk - 1) + q
+        ts(R("rec", c, c + 1), F(4), float(home), MUL, F(6), ADD)
     for c in range(4 if mid else 0):
         ts(F(10 + c), F(6), HALF * (c % 2) + AWAY * (c // 2), ADD)
     nc = 128 if mid else 64
@@ -263,16 +276,19 @@ def rank_program(g, core, T, topo):
         quant(R("p2c", *my), R("p2s", *my), R("wt", 0, 1024), [("sw", 16)])
     XA = XA_MID if mid else XA_END
     for t in range(RD):
-        quant(R("xqc", 128 * t, 128 * t + 128), R("xqs", 128 * t, 128 * t + 128), R("xt", 512 * t, 512 * t + 512), [("sxa" if t < XA else "sxb", 16)])
+        i_x = quant(R("xqc", 128 * t, 128 * t + 128), R("xqs", 128 * t, 128 * t + 128), R("xt", 512 * t, 512 * t + 512), [("sxa" if t < XA else "sxb", 16)])
 
-    tt(R("gd", 0, 5 * LC), R("lst", 0, 5 * LC), R("lst", LC, 6 * LC), SUB, [("sdm", 128), ("al", (NR - 1) * n_off)])
-    tr(R("xx", 0, 64), R("gd", 0, 64))
-    for q in range(4):
-        tr(R("kq", 64 * q, 64 * q + 64), R("xx", 8 * q, 8 * q + 64))
-    ci(R("rec", PAD, PAD + 16 * nl), R("kq", 0, KC + 80), R("klist", 0, nl))
+    def from_lists(out, a, b, op):
+        note("v", vec.tensor_tensor, (ap(out), a, b, op), [R("lst", 0, 8)], [out], 2 * width(out), [("al", (NR - 1) * n_off)])
+
+    from_lists(R("mk", 0, 3), T.lst[:, 0:NR:2, L0 - 1], T.lst[:, 1:NR:2, L0 - 1], GT)
+    for t in range(1, RD):
+        k, n, a = first[t], first[t + 1] - first[t], keys[first[t]][0]
+        lo, up = [T.lst[:, q:q + 2 * n - 1:2, at_list(q, t):at_list(q, t) + NR] for q in (a, a + 1)]
+        from_lists(R("rec", PAD + NR * k, PAD + NR * (k + n)), lo, up, SUB)
 
     def sides(name, t, k):
-        a, b = PAD + 8 * k - t % 2, PAD + 8 * nk - t % 2
+        a, b = PAD + NR * k - t % 2, PAD + NR * nk + t % 2
         return R(name, a, b, 2), R(name, a + 1, b, 2)
 
     def before(t):
@@ -281,29 +297,29 @@ def rank_program(g, core, T, topo):
     def diff(t):
         k = first.get(t, 0)
         lo, up = sides(before(t), t, k)
-        tt(R("d%d" % t, 0, 4 * (nk - k)), up, lo, SUB)
+        tt(R("d%d" % t, 0, 3 * (nk - k) + t % 2), up, lo, SUB)
 
     def change(t):
         k = first[t + 1]
-        a, n = 4 * (k - first.get(t, 0)), 4 * (nk - k)
+        a, n = 3 * (k - first.get(t, 0)), 3 * (nk - k) + t % 2
         w = (n + 15) // 16
         s = "s%d" % t
-        ti(R(s, 0, 16 * w), R("mk", 8 * t, 8 * t + 8), R("l4", 0, w), R("d%d" % t, a, a + 16 * w), MUL)
+        ti(R(s, 0, 16 * w), R("mk", 8 * t, 8 * t + 8), R("l3", 0, w), R("d%d" % t, a, a + 16 * w), MUL)
         for new, old, op in zip(sides("rec%d" % t, t, k), sides(before(t), t, k), (ADD, SUB)):
             tt(new, old, R(s, 0, n), op)
 
     def old(t, k, pos, name=None):
-        c = PAD + 8 * k + pos
+        c = PAD + NR * k + pos
         return R(name or before(t - 1), c, c + 1)
 
     def step(t, k, pos):
-        c = 4 * (k - first[t]) + (pos + (t - 1) % 2) // 2
+        c = 3 * (k - first[t]) + (pos + (t - 1) % 2) // 2
         return R("s%d" % (t - 1), c, c + 1)
 
     def masks(t, lows):
         k, n, nb = first[t], len(lows), "nb%d" % t
-        a = PAD + 8 * k + lows[0]
-        tt(R(nb, 0, n), R(before(t - 1), a, a + 10 * n - 9, 10), R(before(t - 1), a + 1, a + 10 * n - 8, 10), SUB)
+        a = PAD + NR * k + lows[0]
+        tt(R(nb, 0, n), R(before(t - 1), a, a + 8 * n - 7, 8), R(before(t - 1), a + 1, a + 8 * n - 6, 8), SUB)
         for i, lo in enumerate(lows):
             c = 8 * t + (lo + t % 2) // 2
             ts(R("mk", c, c + 1), step(t, k + i, lo), step(t, k + i, lo + 1), ADD, R(nb, i, i + 1), GT)
@@ -314,11 +330,7 @@ def rank_program(g, core, T, topo):
 
     def lanes_out(t, k, pos, ext, tail):
         n, lo = str(t), 2 * near + 1
-
-        def was(kk, x):
-            c = at_key[kk] + 64 * (x % 2) + x // 2
-            return R("kq", c, c + 1) if t == 1 else old(t, kk, x)
-
+        was = lambda kk, x: old(t, kk, x)
         ts(R("wn" + n, 0, 32), R("z64", 0, 32), was(k, lo), ADD, was(k, lo + 1), SUB)
         steps = [R("e3", i, i + 1) for i in range(3)]
         for s, (kk, x) in zip(steps, [(k, lo), (k, lo + 1), (nk - 1, pos)]):
@@ -328,10 +340,10 @@ def rank_program(g, core, T, topo):
         note("a", sca.activation, (ap(o), ap(R("one32", 0, 32)), IDENT), [R("one32", 0, 32), c], [o], 32, kw={"scale": ap(c)})
         af(R("me" + n, 32, 64), o, steps[2], 1.0 if near else -1.0)
         tr(R("fm" + n, 0, 64), R("me" + n, 0, 64))
-        tt(R("dv" + n, 0, 8), R("fm" + n, 33 - near, 41 - near), R("fm" + n, 32 + near, 40 + near), SUB)
+        tt(R("dv" + n, 0, 8), R("fm" + n, SP + 33 - near, SP + 41 - near), R("fm" + n, SP + 32 + near, SP + 40 + near), SUB)
         o, w, l = R("dr" + n, 0, 48), R("dv" + n, 0, 8), R("l8", 0, 3)
         note("a", sca.activation, (ap(o), ap(w).indirect(ap(l)), COPY), [w, l], [o], 65 + 1.5 * 48)
-        scan(R("in" + n, 1, 9), R("one32", 0, 8), R("fm" + n, 0, 8))
+        scan(R("in" + n, 1, 9), R("one32", 0, 8), R("fm" + n, SP, SP + 8))
         ti(R("ge" + n, 0, 48), R("in" + n, 0, 16), R("l8", 0, 3), R("n48", 0, 48), GE)
         scan(R("sl" + n, 0, 40), R("ge" + n, 0, 40), R("dr" + n, 0, 40))
         for h in range(2):
@@ -344,12 +356,11 @@ def rank_program(g, core, T, topo):
             widen("me" + n, at + 64 * i, 64, key)
         w = 64 * len(ks)
         tr(R("fm" + n, at, at + w), R("me" + n, at, at + w))
-        scan(R("ln" + n, 0, w - 24), R("cut", 0, w - 24), R("fm" + n, at, at + w - 24))
+        scan(R("ln" + n, 0, w - 24), R("cut", 0, w - 24), R("fm" + n, at + SP, at + w))
         return [R("ln" + n, 64 * i + 39, 64 * i + 40) for i in range(len(ks))]
 
     aw = [("aw", n_off)]
     M = lambda t, c: R("mk", 8 * t + c, 8 * t + c + 1)
-    tt(R("mk", 0, 3), R("kq", 64, 103, 19), R("kq", 0, 39, 19), GT)
     diff(0)
     change(0)
     diff(1)
@@ -360,12 +371,12 @@ def rank_program(g, core, T, topo):
         pos = 1 + 3 * near
         if not edge:
             lanes_out(1, near, pos, aw, T_BLOCK)
-        af(R("lf", 0, 1), lanes_in(1, 64, [M(1, 2 - near)])[0], float(2 * OWN))
+        af(R("lf", 0, 1), lanes_in(1, 96, [M(1, 2 - near)])[0], float(2 * OWN))
     diff(2)
     if mid or edge:
         masks(2, [2 * c for c in c2])
     else:
-        ts(R("mk", 16 + near, 18 + near), R("d2", near, near + 6, 5), 0.0, GT)
+        ts(R("mk", 16 + near, 18 + near), R("d2", near, near + 5, 4), 0.0, GT)
     change(2)
     U = lambda c: R("t4", c, c + 1)
     k4 = first[4]
@@ -426,10 +437,7 @@ def rank_program(g, core, T, topo):
                 ts(wc, R("io64", 0, 64), U(0), SUB if back else ADD, held, ADD)
             tr(tc, wc)
             lists.append(ci(R("of%d" % t, 0, 16), tc, R("lkh", 0, 1)))
-            if mid and t == 3 and SPLIT3:
-                for h in range(2):
-                    pick((t, h), "st3", src[t][0], src[t][1], R("of3", 8 * h, 8 * h + 8), src[t][2], 0.0, 128 * h, "av"[h])
-            elif t < RD - 1:
+            if t < RD - 1 and not (edge and t == 2 and SPLIT3):
                 pick((t, 0), "st%d" % t, src[t][0], src[t][1], R("of%d" % t, 0, 16), src[t][2])
             else:
                 for h in range(2):
@@ -442,7 +450,8 @@ def rank_program(g, core, T, topo):
             outs.append(note("va"[h], None, (ap(yb), ap(ps)), [ps], [yb], 128))
         for a, b in [(0, 256)] if t < RD - 1 else [(0, 128), (128, 256)]:
             yb = R("yb", 256 * t + a, 256 * t + b)
-            stores.append(note("s", g.sync.dma_start, (T.y[:, yb[1]:yb[2]], ap(yb)), [yb], [], T_STORE * (b - a), tail=T_OUT))
+            stores.append(note("s", g.sync.dma_start, (T.y[:, yb[1]:yb[2]], ap(yb)), [yb], [], T_STORE * (b - a),
+                               [("loc", 9 * n_off)] if mid else [], T_OUT))
 
     n_ops = len(ops)
     queue = [o[0] for o in ops]
@@ -464,6 +473,11 @@ def rank_program(g, core, T, topo):
     if not mid:
         for n in range(2):
             seq[picks[0, 0][n]].add(picks["snd3" if edge else "snd1"][n])
+    if mid:
+        seq[picks[1, 0][0]].update([i_x, outs[0]])
+        seq[picks[1, 0][1]].add(outs[1])
+        seq[picks[2, 0][0]].update(lists)
+        queue[outs[2]] = "a"
     cost = [o[7] for o in ops]
     prio = [o[8] for o in ops]
     topo_order, seen = [], set()
@@ -514,7 +528,7 @@ def rank_program(g, core, T, topo):
         return now["s"], tok, count, order
 
     plan = arrange(queue)
-    for i in outs[::-1]:
+    for i in [] if mid else outs[::-1]:
         other = queue[:i] + ["a" if queue[i] == "v" else "v"] + queue[i + 1:]
         trial = arrange(other)
         if trial[0] < plan[0] - T_SLACK:
@@ -523,8 +537,7 @@ def rank_program(g, core, T, topo):
 
     for b in range(4):
         for h, q in ((0, g.sync), (1, sca)):
-            p0 = 32 * b + 16 * h
-            q.dma_start(T.lst[p0:p0 + 16, LC * r:LC * r + LC], T.dm[:, 6 * h:6 * h + LC]).then_inc(S.sdm, 16)
+            q.dma_start(T.dmt[32 * b + SP:32 * b + 32, h], T.dm[8 * h:8 * h + 8, :]).then_inc(S.sdm, 16)
     g.sync.dma_start(T.wt[:], T.w[:]).then_inc(S.sw, 16)
     g.sync.dma_start(T.xt[:, 0:512 * XA], T.x[:, 0:512 * XA]).then_inc(S.sxa, 16)
     if XA < RD:
@@ -569,12 +582,17 @@ def rank_program(g, core, T, topo):
         left[0] += n_off * len(trs)
 
     others = sorted([q for q in range(NR) if q != r], key=lambda q: (q // 2 == 1, q not in (0, NR - 1), (q - r) % NR))
-    mycol = T.lst[:, LC * r:LC * r + LC]
-    g.wait_ge(S.sdm, 128)
-    send([transfer(T, topo, mycol, [(cores[q], mycol) for q in others], S.al, off_eng)])
+    g.wait_ge(S.v, max(tok[i] for i in i_own))
+    if edge:
+        calls = [(others, 3)]
+    else:
+        calls = [([mate], 5), ([q for q in others if q != mate], 4)][::-1 if mid else 1]
+    for qs, t1 in calls:
+        mine = T.lst[:, r, L0 - 2:L0 + NR * (t1 - 1)]
+        send([transfer(T, topo, mine, [(cores[q], mine) for q in qs], S.al, off_eng)])
     rel = relays(T, topo, r)
     g.wait_ge(S.v, tok[i_w])
-    for kind in "cs":
+    for kind in "cs" if mid else "sc":
         src_v = side(T, src_w, kind, my[0], HALF)
         to_h = [(h, side(T, buf, kind, 0, HALF)) for h, buf, n, sem, _, _ in (rel[1:] if mid else rel[:1])]
         trs = [transfer(T, topo, src_v, [(cores[mate], src_v)], S["aw" + kind], off_eng), transfer(T, topo, src_v, to_h, S["h0" + kind], on_eng)]

from concourse.bass import DstId, RemoteDMATransfer
from concourse.mybir import dt, AluOpType, ActivationFunctionType

NR = 6
RD = 5
PC = 32
LANES = 5
BLK = LANES * PC
HALF = 8 * PC
OWN = 2 * HALF
POOL = 2 * OWN + BLK
AWAY = 4096.0
XA_END, XA_MID = 4, 4
PAD = 8
SP = 24
L0 = 16

F32 = "float32"
CODES = "float8_e4m3fn_x4"
SCRATCH = {
    "wt": ("sbuf", [128, 1024], "bfloat16"),
    "xt": ("sbuf", [128, 512 * RD], "bfloat16"),
    "dmt": ("sbuf", [128, 2, RD, 3], "int32"),
    "lst": ("sbuf", [128, NR, 48], "float16"),
    "yb": ("sbuf", [128, 256 * RD], F32),
    "ps": ("psum", [128, 4096], F32),
    "pi": ("sbuf", [128, 8], "int32"),
    "pj": ("sbuf", [128, 4], "int32"), "l8": ("sbuf", [128, 4], "uint16"), "l3": ("sbuf", [128, 2], "uint16"),
    "lkh": ("sbuf", [128, 2], "uint16"),
    "off1": ("sbuf", [128, 10], "uint16"), "off3": ("sbuf", [128, 10], "uint16"),
}
for _n, _w in (("p1", OWN), ("p2", POOL), ("snd1", BLK), ("snd3", BLK), ("xq", 128 * RD), ("ha", HALF), ("hb", HALF), ("hc", BLK), ("hd", BLK)):
    SCRATCH[_n + "c"] = ("sbuf", [128, _w], CODES)
    SCRATCH[_n + "s"] = ("sbuf", [128, _w], "uint8")
for _t in range(RD):
    SCRATCH["of%d" % _t] = ("sbuf", [128, 16], "uint16")
    SCRATCH["st%dc" % _t] = ("sbuf", [128, 256], CODES)
    SCRATCH["st%ds" % _t] = ("sbuf", [128, 256], "uint8")
_WORK = {
    "pf": 16, "kf": 4, "z64": 64, "one32": 32, "wv": 32, "c64": 128, "cut": 128, "n48": 48, "io64": 64,
    "mk": 32, "lf": 2, "t4": 8, "v64": 64, "nb1": 2, "nb2": 4, "nb3": 2, "cc": 24, "e3": 4,
    "rec": 64, "rec0": 64, "rec1": 64, "rec2": 64, "d0": 48, "d1": 48, "d2": 48, "s0": 32, "s1": 32, "s2": 32,
    "me1": 160, "me3": 160, "fm1": 160, "fm3": 160, "ln1": 128, "ln3": 128,
}
for _t in (1, 3):
    _WORK.update({"wn%d" % _t: 32, "dv%d" % _t: 8, "dr%d" % _t: 48, "in%d" % _t: 16, "ge%d" % _t: 48, "sl%d" % _t: 48})
for _t in range(RD):
    _WORK.update({"wc%d" % _t: 64, "tc%d" % _t: 64})
for _n in _WORK:
    SCRATCH[_n] = ("sbuf", [128, _WORK[_n]], F32)

_ARR = ["aw", "am", "b10", "b11", "b30", "b31", "far", "h0", "h1"]
SEMAPHORES = ["v", "a", "t", "s", "gi", "sdm", "sw", "sxa", "sxb", "al", "loc", "shc", "shs"] + [n + k for n in _ARR for k in "cs"]

ADD, SUB, MUL, MIN = AluOpType.add, AluOpType.subtract, AluOpType.mult, AluOpType.min
LT, GT, GE, NE = AluOpType.is_lt, AluOpType.is_gt, AluOpType.is_ge, AluOpType.not_equal
AND, SHR = AluOpType.bitwise_and, AluOpType.logical_shift_right
COPY, IDENT = ActivationFunctionType.Copy, ActivationFunctionType.Identity

T_CYC, T_WAKE, T_SLACK, T_FULL = 0.00104, 0.15, 0.02, 1.0
T_BLOCK, T_LAST, T_SCALES, T_OUT, T_STORE = 6.5, 5.0, 0.4, 1.3, 1.6
T_EXT = {"gi": 1.0, "sdm": 1.5, "sw": 2.3, "sxa": 4.0, "al": 4.75, "awc": 6.25, "aws": 7.65, "sxb": 6.75, "am": 9.05, "sh": 9.55, "farc": 10.95, "fars": 10.45}
EV_FROM, SPLIT3 = {"mid": 2, "edge": 0, "near": 2}, True
T_EDGE = {"al": 4.45, "am": 10.45, "sh": 8.95, "farc": 11.65, "fars": 10.75}
T_MID = {"al": 4.95, "aws": 6.65, "sxb": 8.25, "loc": 10.35}
T_BLOCKS = (9.3, 9.6, 10.9, 9.9, 10.85, 10.1, 11.55, 11.4)


def R(name, a, b, step=1):
    return (name, a, b, step)


def on_plane(T, topo, r, s):
    return [q for q in (2 * s, 2 * s + 1) if topo.same_plane(topo.chip(T.cores[r]), topo.chip(T.cores[q]))][0]


def helpers(T, topo, r):
    c = T.cores[r]
    hs = [h for h in topo.cores_of(c) if T.rank_of(h) is None and topo.may_write(h, T.cores[r ^ 1])]
    return sorted(hs, key=lambda h: topo.die(h) != topo.die(c))


def relays(T, topo, r):
    hs = helpers(T, topo, r)
    if r // 2 == 1:
        to = lambda qs: [(q, "p2", OWN + HALF * (r % 2)) for q in qs]
        ends = [1, NR - 2, 0, NR - 1]
        across = [q for q in ends if on_plane(T, topo, r, q // 2) != q]
        outer = [q for q in ends[2:] if q not in across]
        return [(h, "hb", HALF, "h0", to([q]), "am") for h, q in zip([hs[0], hs[0], hs[-1]], across[:1] + outer + across[1:])]
    first = (hs[-1], "ha", HALF, "h0", [(r ^ 1, "p1", HALF * (r % 2))], "aw")
    if r not in (0, NR - 1):
        return [first, (hs[-1], "hc", BLK, "h1", block_places(1, r // 4)[1:], "b1%d" % (r // 4)),
                (hs[-1], "hc", BLK, "h1", [(NR - 1 - (r ^ 1), "p2", 2 * OWN)], "far")]
    return [first, (hs[-1], "hd", BLK, "h1", block_places(3, r // 4)[1:], "b3%d" % (r // 4))]


def block_places(t, b):
    return [(2 + b, "p2", OWN + BLK * (t - 1)), (3 - b, "p2", OWN + BLK * t)]


def side(T, name, kind, a, n):
    v = T[name + kind][:, a:a + n]
    return v.bitcast(dt.uint8) if kind == "c" else v


def transfer(T, topo, src, dsts, sem, engines):
    return RemoteDMATransfer(dst_ids=[DstId(rid=topo.addr(c)[0], pnc=topo.addr(c)[1]) for c, _ in dsts], srcs=[src],
                             dsts=[v for _, v in dsts], dma_engine_mask=sum(1 << x for x in engines), remote_sem=sem)


def chip_engines(T, topo, r):
    off = topo.engines(T.cores[r], T.cores[r ^ 1])
    return [x for x in topo.engines(T.cores[r], helpers(T, topo, r)[0]) if x not in off]


def hand_on(g, core, T, topo):
    left = 0
    for r in range(NR):
        for h, buf, n, sem, dsts, there in relays(T, topo, r):
            if h != core:
                continue
            eng = topo.engines(core, T.cores[dsts[0][0]])
            for kind in {"ha": "s", "hb": "cs", "hc": "c", "hd": "s"}[buf]:
                g.wait_ge(T.sem[sem + kind], len(chip_engines(T, topo, r)))
                g.remote_dma_fused([transfer(T, topo, side(T, buf, kind, 0, n), [(T.cores[q], side(T, b, kind, c, n)) for q, b, c in dsts],
                                             T.sem[there + kind], eng)], local_sem=T.sem.loc)
                left += len(eng)
    if left:
        g.wait_ge(T.sem.loc, left)


def rank_program(g, core, T, topo):
    r = T.rank_of(core)
    if r is None:
        hand_on(g, core, T, topo)
        return
    cores = T.cores
    pair = r // 2
    base, e = 2 * pair, r % 2
    mate = r ^ 1
    mid = pair == 1
    edge = r in (0, NR - 1)
    near = e if mid else pair // 2
    vec, sca = g.vector, g.scalar
    S = T.sem
    off_eng = topo.engines(core, cores[mate])
    on_eng = chip_engines(T, topo, r)
    n_off = len(off_eng)

    def ap(o):
        name, a, b, step = o
        return T[name][:, a:b] if step == 1 else T[name][:, a:b:step]

    ops = []

    def note(q, call, args, reads, writes, cost, ext=(), tail=0.0, lag=0.0, kw=None):
        ops.append((q, call, args, kw or {}, reads, writes, tuple(ext), max(64, cost) * T_CYC, tail, lag))
        return len(ops) - 1

    def val(x):
        return ap(x) if isinstance(x, tuple) else x

    def width(o):
        return len(range(o[1], o[2], o[3]))

    def ts(out, in0, s1, op0, s2=None, op1=None, ext=()):
        args = (ap(out), ap(in0), val(s1), None, op0) if op1 is None else (ap(out), ap(in0), val(s1), val(s2), op0, op1)
        return note("v", vec.tensor_scalar, args, [x for x in (in0, s1, s2) if isinstance(x, tuple)], [out], width(out), ext)

    def af(out, in0, bias, scale=1.0):
        return note("a", sca.activation, (ap(out), ap(in0), IDENT), [x for x in (in0, bias) if isinstance(x, tuple)], [out],
                    width(out), kw={"bias": val(bias), "scale": scale})

    def tt(out, a, b, op, ext=()):
        return note("v", vec.tensor_tensor, (ap(out), ap(a), ap(b), op), [a, b], [out], 2 * width(out), ext)

    def ti(out, win, off, b, op):
        return note("v", vec.tensor_tensor, (ap(out), ap(win).indirect(ap(off)), ap(b), op), [win, off, b], [out], 50 + 1.5 * width(out))

    def ci(out, win, off):
        return note("v", vec.tensor_copy, (ap(out), ap(win).indirect(ap(off))), [win, off], [out], 50 + 1.5 * width(out))

    def tr(out, a):
        return note("v", vec.transpose, (ap(out), ap(a)), [a], [out], width(out))

    def scan(out, d0, d1):
        return note("v", vec.tensor_tensor_scan, (ap(out), ap(d0), ap(d1), 0.0, MUL, ADD), [d0, d1], [out], width(out))

    def cp(out, a):
        return note("v", vec.tensor_copy, (ap(out), ap(a)), [a], [out], width(out))

    def fill(name, v, a=0, b=None, step=1):
        o = R(name, a, _WORK[name] if b is None else b, step)
        return note("v", vec.memset, (ap(o), v), [], [o], width(o))

    def quant(c, s, src, ext, tail=0.0):
        return note("v", vec.quantize_mx, (ap(c), ap(s), ap(src)), [], [c, s], 12 + 0.22 * width(src), ext, tail)

    picks = {}

    def pick(key, dst, src, wid, o, ext, tail=0.0, at=0, by="a"):
        n = width(o)
        c, d, w = 50 + 1.5 * 16 * n, R(dst + "c", at, at + 16 * n), R(src + "c", 0, wid)
        i = note("v", vec.tensor_copy, (ap(d).bitcast(dt.uint32), ap(w).bitcast(dt.uint32).indirect(ap(o))), [w, o], [d], c,
                 [(s + "c", k) for s, k in ext], tail)
        d, w = R(dst + "s", at, at + 16 * n), R(src + "s", 0, wid)
        call, args = (sca.activation, (COPY,)) if by == "a" else (vec.tensor_copy, ())
        j = note(by, call, (ap(d), ap(w).indirect(ap(o))) + args, [w, o], [d], c, [(s + "s", k) for s, k in ext], tail)
        picks[key] = (i, j)

    c2 = [0, 1, 2] if mid else [near, near + 1]
    b3 = [0, 1] if mid else [near]
    keys = [(1, 1), (3, 1)] + [(2 * c, 2) for c in c2] + [(2 * b + 1, 3) for b in b3] + [(base, 4)]
    first = {1: 0, 2: 2, 3: 2 + len(c2), 4: len(keys) - 1, 5: len(keys)}
    nk = len(keys) + (not mid)

    def col(t, pos, n=1):
        c = PAD + NR * (nk - 1) + pos
        return R("rec%d" % t, c, c + n)

    def at_list(q, t):
        return L0 + NR * (0 if t == 4 and q in (0, NR - 1) else t - 1)

    for b in range(4):
        note("v", vec.memset, (T.dmt[32 * b:32 * b + SP], 0), [], [R("dmt", b, b + 1)], 30, tail=30.0)
    note("v", vec.memset, (T.lst[:, r, L0 - 2:L0 - 1], 0.0), [], [R("lst", 0, 1)], 1, tail=30.0)
    own = [(T.lst[:, r, L0 - 1:L0], vec.tensor_tensor, (T.dmt[:, 1, 0, pair:pair + 1], T.dmt[:, 0, 0, pair:pair + 1], SUB))]
    for h in range(2):
        rounds, n = (slice(4, 1, -2), 2) if edge else (slice(1, RD), 4)
        own.append((T.lst[:, r, L0 + h:L0 + NR * n:2], vec.tensor_copy, (T.dmt[:, h, rounds, :],)))
    i_own = [note("v", call, (o,) + args, [R("dmt", 0, 4)], [R("lst", 1 + n, 2 + n)], 12, [("sdm", 128)], 30.0) for n, (o, call, args) in enumerate(own)]

    for n in ["z64", "mk", "rec0", "rec1", "rec2", "d0", "d1", "d2"] + ([] if mid else ["in1", "in3"]):
        fill(n, 0.0)
    if not mid:
        fill("fm3" if edge else "fm1", 0.0, 64, 72)
    gi = [("gi", 3 if mid else 4)]
    P = lambda c: R("pi", c, c + 1)
    F = lambda c: R("pf", c, c + 1)
    for c, (sh, m) in enumerate([(0, 15), (0, 7), (0, 31), (0, 1), (1, 7)]):
        ts(P(c + 1), P(0), sh, SHR, m, AND, ext=gi)
    cp(R("pf", 0, 2), R("pi", 1, 3))
    ts(F(3), F(0), 16.0, ADD)
    ts(F(4), P(3), float(SP), GE)
    ts(F(5), F(4), float(PC), MUL)
    ts(R("v64", 0, 64), R("z64", 0, 64), F(5), ADD)
    tt(F(6), F(5), F(1), MUL)
    ts(F(7), P(5), float(SP), ADD)
    ts(R("l8", 0, 4), R("z64", 0, 4), F(1), ADD)
    ts(R("lkh", 0, 1), P(4), 32.0, MUL, F(7), ADD)
    for c in range(2):
        ts(R("kf", c, c + 1), F(0), float(c), ADD)
    ts(R("pj", 0, 2), R("kf", 0, 2), 11.0, MUL)
    ts(R("pj", 2, 4), R("pj", 0, 2), 5, SHR)
    ts(R("kf", 2, 4), R("pj", 2, 4), -3.0, MUL)
    tt(R("kf", 2, 4), R("kf", 2, 4), R("kf", 0, 2), ADD)
    cp(R("l3", 0, 2), R("kf", 2, 4))
    for q in range(0 if mid else NR):
        home = HALF * (q % 2) + (0 if q // 2 == pair else OWN if q // 2 == 1 else AWAY)
        c = PAD + NR * (nk - 1) + q
        ts(R("rec", c, c + 1), F(4), float(home), MUL, F(6), ADD)
    for c in range(4 if mid else 0):
        ts(F(10 + c), F(6), HALF * (c % 2) + AWAY * (c // 2), ADD)
    nc = 128 if mid else 64
    ts(R("cut", 0, nc), R("c64", 0, nc), F(1), NE, ext=gi)
    fill("cut", -1.0, 32, nc, 64)
    his = HALF * (1 - e)
    if not mid:
        fill("one32", 1.0)

    my = (HALF * e, HALF * (e + 1))
    src_w = "p2" if mid else "p1"
    i_w = quant(R(src_w + "c", *my), R(src_w + "s", *my), R("wt", 0, 1024), [("sw", 16)], 20.0)
    if not mid:
        quant(R("p2c", *my), R("p2s", *my), R("wt", 0, 1024), [("sw", 16)])
    XA = XA_MID if mid else XA_END
    for t in range(RD):
        i_x = quant(R("xqc", 128 * t, 128 * t + 128), R("xqs", 128 * t, 128 * t + 128), R("xt", 512 * t, 512 * t + 512), [("sxa" if t < XA else "sxb", 16)])

    def from_lists(out, a, b, op):
        note("v", vec.tensor_tensor, (ap(out), a, b, op), [R("lst", 0, 8)], [out], 2 * width(out), [("al", (NR - 1) * n_off)])

    from_lists(R("mk", 0, 3), T.lst[:, 0:NR:2, L0 - 1], T.lst[:, 1:NR:2, L0 - 1], GT)
    for t in range(1, RD):
        k, n, a = first[t], first[t + 1] - first[t], keys[first[t]][0]
        lo, up = [T.lst[:, q:q + 2 * n - 1:2, at_list(q, t):at_list(q, t) + NR] for q in (a, a + 1)]
        from_lists(R("rec", PAD + NR * k, PAD + NR * (k + n)), lo, up, SUB)

    def sides(name, t, k):
        a, b = PAD + NR * k - t % 2, PAD + NR * nk + t % 2
        return R(name, a, b, 2), R(name, a + 1, b, 2)

    def before(t):
        return "rec%d" % (t - 1) if t else "rec"

    def diff(t):
        k = first.get(t, 0)
        lo, up = sides(before(t), t, k)
        tt(R("d%d" % t, 0, 3 * (nk - k) + t % 2), up, lo, SUB)

    def change(t):
        k = first[t + 1]
        a, n = 3 * (k - first.get(t, 0)), 3 * (nk - k) + t % 2
        w = (n + 15) // 16
        s = "s%d" % t
        ti(R(s, 0, 16 * w), R("mk", 8 * t, 8 * t + 8), R("l3", 0, w), R("d%d" % t, a, a + 16 * w), MUL)
        for new, old, op in zip(sides("rec%d" % t, t, k), sides(before(t), t, k), (ADD, SUB)):
            tt(new, old, R(s, 0, n), op)

    def old(t, k, pos, name=None):
        c = PAD + NR * k + pos
        return R(name or before(t - 1), c, c + 1)

    def step(t, k, pos):
        c = 3 * (k - first[t]) + (pos + (t - 1) % 2) // 2
        return R("s%d" % (t - 1), c, c + 1)

    def masks(t, lows):
        k, n, nb = first[t], len(lows), "nb%d" % t
        a = PAD + NR * k + lows[0]
        tt(R(nb, 0, n), R(before(t - 1), a, a + 8 * n - 7, 8), R(before(t - 1), a + 1, a + 8 * n - 6, 8), SUB)
        for i, lo in enumerate(lows):
            c = 8 * t + (lo + t % 2) // 2
            ts(R("mk", c, c + 1), step(t, k + i, lo), step(t, k + i, lo + 1), ADD, R(nb, i, i + 1), GT)

    def widen(me, at, n, m):
        o, i = R(me, at, at + n), R("v64", 0, n)
        note("a", sca.activation, (ap(o), ap(i), IDENT), [i, m], [o], n, kw={"scale": ap(m)})

    def lanes_out(t, k, pos, ext, tail):
        n, lo = str(t), 2 * near + 1
        was = lambda kk, x: old(t, kk, x)
        ts(R("wn" + n, 0, 32), R("z64", 0, 32), was(k, lo), ADD, was(k, lo + 1), SUB)
        steps = [R("e3", i, i + 1) for i in range(3)]
        for s, (kk, x) in zip(steps, [(k, lo), (k, lo + 1), (nk - 1, pos)]):
            ts(s, was(kk, x | 1), was(kk, x & ~1), SUB, M(t - 1, x // 2), MUL)
        ts(R("me" + n, 0, 32), R("wn" + n, 0, 32), steps[0], SUB, steps[1], LT)
        o, c = R("wv", 0, 32), was(nk - 1, pos)
        note("a", sca.activation, (ap(o), ap(R("one32", 0, 32)), IDENT), [R("one32", 0, 32), c], [o], 32, kw={"scale": ap(c)})
        af(R("me" + n, 32, 64), o, steps[2], 1.0 if near else -1.0)
        tr(R("fm" + n, 0, 64), R("me" + n, 0, 64))
        tt(R("dv" + n, 0, 8), R("fm" + n, SP + 33 - near, SP + 41 - near), R("fm" + n, SP + 32 + near, SP + 40 + near), SUB)
        o, w, l = R("dr" + n, 0, 48), R("dv" + n, 0, 8), R("l8", 0, 3)
        note("a", sca.activation, (ap(o), ap(w).indirect(ap(l)), COPY), [w, l], [o], 65 + 1.5 * 48)
        scan(R("in" + n, 1, 9), R("one32", 0, 8), R("fm" + n, SP, SP + 8))
        ti(R("ge" + n, 0, 48), R("in" + n, 0, 16), R("l8", 0, 3), R("n48", 0, 48), GE)
        scan(R("sl" + n, 0, 40), R("ge" + n, 0, 40), R("dr" + n, 0, 40))
        for h in range(2):
            ts(R("off" + n, h, 10, 2), R("sl" + n, 7, 40, 8), F(3 * h), ADD, float(OWN - 1), MIN)
        pick("snd" + n, "snd" + n, "p1", OWN, R("off" + n, 0, 10), ext, tail)

    def lanes_in(t, at, ks):
        n = str(t)
        for i, key in enumerate(ks):
            widen("me" + n, at + 64 * i, 64, key)
        w = 64 * len(ks)
        tr(R("fm" + n, at, at + w), R("me" + n, at, at + w))
        scan(R("ln" + n, 0, w - 24), R("cut", 0, w - 24), R("fm" + n, at + SP, at + w))
        return [R("ln" + n, 64 * i + 39, 64 * i + 40) for i in range(len(ks))]

    aw = [("aw", n_off)]
    M = lambda t, c: R("mk", 8 * t + c, 8 * t + c + 1)
    diff(0)
    change(0)
    diff(1)
    masks(1, [1, 3])
    change(1)

    if not mid:
        pos = 1 + 3 * near
        if not edge:
            lanes_out(1, near, pos, aw, T_BLOCK)
        af(R("lf", 0, 1), lanes_in(1, 96, [M(1, 2 - near)])[0], float(2 * OWN))
    diff(2)
    if mid or edge:
        masks(2, [2 * c for c in c2])
    else:
        ts(R("mk", 16 + near, 18 + near), R("d2", near, near + 5, 4), 0.0, GT)
    change(2)
    U = lambda c: R("t4", c, c + 1)
    k4 = first[4]
    if mid:
        masks(3, [1, 3])
        for b in range(2):
            ts(U(1 + b), old(3, k4, 1 + 3 * b, "rec2"), old(3, k4, 2 + b, "rec2"), SUB, M(3, 1 + b), MUL)
        tt(U(3), old(3, k4, 2, "rec2"), old(3, k4, 3, "rec2"), SUB)
        ts(U(4), U(2), U(1), SUB, U(3), GT)
        C = lambda n, b: R("cc", 2 * n + b, 2 * n + b + 1)
        sg = (1.0, -1.0)
        lane1, lane3 = lanes_in(1, 0, [M(1, 1), M(1, 2)]), lanes_in(3, 0, [M(3, 1), M(3, 2)])
        for b in range(2):
            af(C(0, b), M(0, 1), F(10 + b), sg[b] * HALF)
            af(C(4, b), C(0, b), float(OWN + BLK * (b != near)), -1.0)
            ts(C(5, b), lane1[b], C(4, b), ADD, M(1, 1 + b), MUL)
            af(C(1, b), C(5, b), C(0, b))
            af(C(6, b), M(0, 1), F(12 + b), sg[b] * HALF)
            af(C(7, b), M(1, 1 + b), C(6, b), -AWAY)
            af(C(8, b), M(2, 2 * b), C(7, b), AWAY)
        ts(U(5), C(1, 1), C(1, 0), SUB, M(2, 1), MUL)
        for b in range(2):
            af(C(2, b), U(5), C(1, b), sg[b])
            ts(C(9, b), lane3[b], float(OWN + BLK * (2 + (b != near))), ADD, C(8, b), MIN)
            ts(C(10, b), C(9, b), C(2, b), SUB, M(3, 1 + b), MUL)
            af(C(3, b), C(10, b), C(2, b))
        ts(U(0), C(3, 1 - e), C(3, e), SUB, U(4), MUL)
        held, back = C(3, e), 0
    else:
        if not edge:
            masks(3, [2 * near + 1])
            m3 = M(3, 1 + near)
        else:
            lanes_out(3, first[3], pos, aw, T_LAST)
            m3 = R("me3", 0, 1)
        out, oth = 2 + near, (NR - 1) * near
        for c, k in ((1, k4), (2, nk - 1)):
            ts(U(c), old(3, k, out, "rec2"), old(3, k, pos, "rec2"), SUB, m3, MUL)
        ts(U(3), U(2), col(2, pos), ADD, R("lf", 0, 1), MIN)
        ts(U(4), U(1), old(3, k4, pos, "rec2"), ADD, old(3, k4, oth, "rec2"), LT if near else GT)
        ts(U(0), U(3), col(2, oth), SUB, U(4), MUL)
        held, back = (col(2, oth), 0) if edge else (U(3), 1)

    if mid:
        names = ["b%d%d" % (t, b) for t in (1, 3) for b in (near, 1 - near)]
        src = [("p2", OWN + BLK * t, aw + [(s, n_off) for s in names[:t]]) for t in range(RD)]
    else:
        am = [("sh", 16), ("am", 2 * n_off)]
        src = [("p1", OWN, aw)] + [("p2", 2 * OWN, am)] * 2 + [("p2", POOL, am + [("far", n_off)])] * 2
    tile = [t - 1 if edge and t % 2 else t for t in range(RD)]
    stores, lists, outs = [], [], []
    for t in range(RD):
        if tile[t] == t:
            wc, tc = R("wc%d" % t, 0, 64), R("tc%d" % t, 0, 64)
            if t < 4:
                af(wc, R("io64", 0, 64), held if t == 3 else C(t, e) if mid else col(t, r))
            else:
                ts(wc, R("io64", 0, 64), U(0), SUB if back else ADD, held, ADD)
            tr(tc, wc)
            lists.append(ci(R("of%d" % t, 0, 16), tc, R("lkh", 0, 1)))
            if t < RD - 1 and not (edge and t == 2 and SPLIT3):
                pick((t, 0), "st%d" % t, src[t][0], src[t][1], R("of%d" % t, 0, 16), src[t][2])
            else:
                for h in range(2):
                    pick((t, h), "st%d" % t, src[t][0], src[t][1], R("of%d" % t, 8 * h, 8 * h + 8), src[t][2], 0.0, 128 * h)
        for h in range(2):
            bank, c = 512 * ((2 * t + h) % 8), 256 * t + 128 * h
            ps, yb = R("ps", bank, bank + 128), R("yb", c, c + 128)
            ins = [R("st%d%s" % (tile[t], k), 128 * h, 128 * h + 128) for k in "cs"] + [R("xq" + k, 128 * t, 128 * t + 128) for k in "cs"]
            note("t", g.tensor.matmul_mx, (ap(ps), *[ap(x) for x in ins], True, True), ins, [ps], 190)
            outs.append(note("va"[h], None, (ap(yb), ap(ps)), [ps], [yb], 128))
        for a, b in [(0, 256)] if t < RD - 1 else [(0, 128), (128, 256)]:
            yb = R("yb", 256 * t + a, 256 * t + b)
            stores.append(note("s", g.sync.dma_start, (T.y[:, yb[1]:yb[2]], ap(yb)), [yb], [], T_STORE * (b - a),
                               [("loc", 9 * n_off)] if mid else [], T_OUT))

    n_ops = len(ops)
    queue = [o[0] for o in ops]
    raw = [set() for _ in ops]
    seq = [set() for _ in ops]
    hist = {}
    for i, o in enumerate(ops):
        for kind, regs in (("r", o[4]), ("w", o[5])):
            for name, a, b, step in regs:
                cols = set(range(a, b, step))
                for j, k2, cs in hist.get(name, []):
                    if j != i and (kind == "w" or k2 == "w") and not cols.isdisjoint(cs):
                        (raw if k2 == "w" or queue[j] != queue[i] else seq)[i].add(j)
        for kind, regs in (("r", o[4]), ("w", o[5])):
            for name, a, b, step in regs:
                hist.setdefault(name, []).append((i, kind, set(range(a, b, step))))
    for a, b in zip(stores, stores[1:]):
        seq[b].add(a)
    if not mid:
        for n in range(2):
            seq[picks[0, 0][n]].add(picks["snd3" if edge else "snd1"][n])
    if mid:
        seq[picks[1, 0][0]].update([i_x, outs[0]])
        seq[picks[1, 0][1]].add(outs[1])
        seq[picks[2, 0][0]].update(lists)
        queue[outs[2]] = "a"
    cost = [o[7] for o in ops]
    prio = [o[8] for o in ops]
    topo_order, seen = [], set()
    while len(topo_order) < n_ops:
        for i in range(n_ops):
            if i not in seen and raw[i] <= seen and seq[i] <= seen:
                seen.add(i)
                topo_order.append(i)
    for i in topo_order[::-1]:
        prio[i] += cost[i]
        for j in raw[i]:
            prio[j] = max(prio[j], prio[i] + T_WAKE)
        for j in seq[i]:
            prio[j] = max(prio[j], prio[i])
    ext = dict(T_EXT)
    if mid:
        ext.update(T_MID, **dict(zip([n + k for n in names for k in "cs"], T_BLOCKS)))
    if edge:
        ext.update(T_EDGE)

    def ext_time(s):
        return ext[s] if s in ext else ext[s[:-1]] + (T_SCALES if s[-1] == "s" else 0.0)

    def arrange(queue):
        done, tok, now, count, order = {}, {}, {q: 0.0 for q in "vats"}, {q: 0 for q in "vats"}, []
        while len(order) < n_ops:
            ready = []
            for i in range(n_ops):
                if i in tok or not all(j in tok for j in raw[i]) or not all(j in tok for j in seq[i]):
                    continue
                at = max([now[queue[i]]] + [done[j] + T_WAKE for j in raw[i]] + [ext_time(s) for s, _ in ops[i][6]])
                ready.append((at, -prio[i], i))
            best = min(ready)
            at, _, i = best
            q = queue[i]
            rest = sum(cost[j] for j in range(n_ops) if j not in tok and queue[j] == q) * T_FULL + T_OUT
            gain = [(max(at + prio[i], at + cost[i] + prio[j], at + rest) - max(a + prio[j], a + cost[j] + prio[i], a + rest), a, j)
                    for a, _, j in ready if queue[j] == q and a < at + cost[i]]
            if max(gain)[0] > T_SLACK:
                _, a, j = max(gain)
                fit = [c for c in ready if queue[c[2]] == q and c[0] + cost[c[2]] <= a + T_SLACK]
                best = min(fit, key=lambda c: c[1]) if fit else (a, 0, j)
            i = best[2]
            now[q] = done[i] = best[0] + cost[i]
            count[q] += 1
            tok[i] = count[q]
            order.append(i)
        return now["s"], tok, count, order

    plan = arrange(queue)
    for i in [] if mid else outs[::-1]:
        other = queue[:i] + ["a" if queue[i] == "v" else "v"] + queue[i + 1:]
        trial = arrange(other)
        if trial[0] < plan[0] - T_SLACK:
            queue, plan = other, trial
    _, tok, count, order = plan

    for b in range(4):
        for h, q in ((0, g.sync), (1, sca)):
            q.dma_start(T.dmt[32 * b + SP:32 * b + 32, h], T.dm[8 * h:8 * h + 8, :]).then_inc(S.sdm, 16)
    g.sync.dma_start(T.wt[:], T.w[:]).then_inc(S.sw, 16)
    g.sync.dma_start(T.xt[:, 0:512 * XA], T.x[:, 0:512 * XA]).then_inc(S.sxa, 16)
    if XA < RD:
        g.sync.wait_ge(S.al, (NR - 1) * n_off)
        g.sync.dma_start(T.xt[:, 512 * XA:], T.x[:, 512 * XA:]).then_inc(S.sxb, 16)

    if not mid:
        for kind in "cs":
            g.sync.wait_ge(S["aw" + kind], n_off)
            if kind == "s" and not edge:
                g.sync.wait_ge(S.a, tok[picks["snd1"][1]])
            g.sync.dma_start(side(T, "p2", kind, his, HALF), side(T, "p1", kind, his, HALF)).then_inc(S["sh" + kind], 16)

    waited = {}

    def wait(q, sem, n):
        if waited.get((q, sem), 0) < n:
            {"v": vec, "a": sca, "t": g.tensor, "s": g.sync}[q].wait_ge(S[sem], n)
            waited[q, sem] = n

    wait("a", "gi", gi[0][1])
    for i in order:
        q, (call, args, kw), ex = queue[i], ops[i][1:4], ops[i][6]
        if call is None:
            call, args = (vec.tensor_copy, args) if q == "v" else (sca.activation, args + (COPY,))
        for sem, n in ex:
            wait(q, sem, n)
        for s in "vat":
            wait(q, s, max([0] + [tok[j] for j in raw[i] if queue[j] == s]))
        call(*args, **kw).then_inc(S[q], 16 if q == "s" else 1)

    big = {"allow_small_or_imprecise_dtypes": True}
    g.iota(T.pi[:, 0:1], [[0, 1]], 0, 1).then_inc(S.gi, 1)
    g.iota(T.c64[:, 0:nc], [[0, nc // 64], [1, 64]], 0, 0, **big).then_inc(S.gi, 1)
    g.iota(T.io64[:], [[16, 2], [0, 2], [1, 16]], 0, 0, **big).then_inc(S.gi, 1)
    if not mid:
        g.iota(T.n48[:], [[1, 6], [0, 8]], 1, 0, **big).then_inc(S.gi, 1)
    left = [0]

    def send(trs):
        g.remote_dma_fused(trs, local_sem=S.loc)
        left[0] += n_off * len(trs)

    others = sorted([q for q in range(NR) if q != r], key=lambda q: (q // 2 == 1, q not in (0, NR - 1), (q - r) % NR))
    g.wait_ge(S.v, max(tok[i] for i in i_own))
    if edge:
        calls = [(others, 3)]
    else:
        calls = [([mate], 5), ([q for q in others if q != mate], 4)][::-1 if mid else 1]
    for qs, t1 in calls:
        mine = T.lst[:, r, L0 - 2:L0 + NR * (t1 - 1)]
        send([transfer(T, topo, mine, [(cores[q], mine) for q in qs], S.al, off_eng)])
    rel = relays(T, topo, r)
    g.wait_ge(S.v, tok[i_w])
    for kind in "cs" if mid else "sc":
        src_v = side(T, src_w, kind, my[0], HALF)
        to_h = [(h, side(T, buf, kind, 0, HALF)) for h, buf, n, sem, _, _ in (rel[1:] if mid else rel[:1])]
        trs = [transfer(T, topo, src_v, [(cores[mate], src_v)], S["aw" + kind], off_eng), transfer(T, topo, src_v, to_h, S["h0" + kind], on_eng)]
        send(trs if mid else trs[:1] if kind == "c" else trs[1:])
    if mid:
        q = on_plane(T, topo, r, 2 - 2 * near)
        for kind in "cs":
            send([transfer(T, topo, side(T, "p2", kind, my[0], HALF), [(cores[q], side(T, "p2", kind, OWN + my[0], HALF))], S["am" + kind], off_eng)])
        g.wait_ge(S["b1%dc" % near], n_off)
        send([transfer(T, topo, side(T, "p2", "c", OWN, BLK), [(cores[NR - 2 - 3 * near], side(T, "p2", "c", 2 * OWN, BLK))], S.farc, off_eng)])
    else:
        t = 3 if edge else 1
        key = "snd%d" % t
        h, buf, n, hsem, _, _ = rel[1]
        to_h = lambda kind: transfer(T, topo, side(T, key, kind, 0, BLK), [(h, side(T, buf, kind, 0, BLK))], S[hsem + kind], on_eng)
        to_mid = lambda kind, ds: transfer(T, topo, side(T, key, kind, 0, BLK), [(cores[q], side(T, b, kind, c, BLK)) for q, b, c in ds],
                                           S["b%d%d%s" % (t, near, kind)], off_eng)
        ds = block_places(t, near)
        if t == 1:
            g.wait_ge(S.v, tok[picks[key][0]])
            send([to_mid("c", ds[:1]), to_h("c")])
            to_far = lambda kind, qs: transfer(T, topo, side(T, key, kind, 0, BLK), [(cores[q], side(T, "p2", kind, 2 * OWN, BLK)) for q in qs],
                                               S["far" + kind], off_eng)
            inner, outer = NR - 1 - r, NR - 1 - mate
            g.wait_ge(S.a, tok[picks[key][1]])
            send([to_mid("s", ds)])
            send([to_far("s", [inner, outer])])
        else:
            g.wait_ge(S.a, tok[picks[key][1]])
            send([to_mid("s", ds[:1]), to_h("s")])
            g.wait_ge(S.v, tok[picks[key][0]])
            send([to_mid("c", ds)])

    g.sync.wait_ge(S.v, count["v"])
    g.sync.wait_ge(S.a, count["a"])
    g.sync.wait_ge(S.s, 16 * count["s"])
    g.wait_ge(S.loc, left[0])
